import numpy as np
import ml_dtypes


def mxq(x, axis, fmt="e4m3"):
    dtype, down = {"e4m3": (ml_dtypes.float8_e4m3fn, 7), "e5m2": (ml_dtypes.float8_e5m2, 14)}[fmt]
    v = np.moveaxis(np.asarray(x, np.float32).astype(ml_dtypes.bfloat16).astype(np.float64), axis, -1)
    blocks = v.reshape(v.shape[:-1] + (-1, 32))
    amax = np.abs(blocks).max(-1, keepdims=True)
    byte = np.maximum(np.where(amax > 0, np.frexp(amax)[1] - 1 + 127, 0) - down, 1)
    scale = np.exp2(byte - 127.0)
    codes = (blocks / scale).astype(np.float32).astype(dtype).astype(np.float64)
    return np.moveaxis((codes * scale).reshape(v.shape), -1, axis)


WIDE = False


def mx_kscale(k):
    if not WIDE:
        return np.ones(k)
    levels = np.array([10, -10, 5, -5, 0])
    if k % 512:
        return np.exp2(np.random.permutation(np.resize(levels, k // 32))).repeat(32)
    a = np.empty((k // 512, 16))
    for p in range(k // 512):
        a[p, :8] = np.random.permutation(np.resize(levels, 8))
        for g in range(8):
            far = levels[np.abs(levels - a[p, g]) >= 10]
            a[p, g + 8] = far[np.random.randint(len(far))]
    return np.exp2(a.ravel()).repeat(32)


def f64(x):
    return np.asarray(x).astype(np.float64)


def striped(idx):
    return np.tile(idx.reshape(-1, 16).T, (8, 1)).astype(np.uint16)


def unstriped(offs):
    return offs[:16].T.reshape(-1).astype(np.int64)


E2M1 = np.array([0.0, 0.5, 1.0, 1.5, 2.0, 3.0, 4.0, 6.0, -0.0, -0.5, -1.0, -1.5, -2.0, -3.0, -4.0, -6.0])


def pack_weight(w, fmt):
    k, n = w.shape
    w = f64(np.asarray(w, np.float32).astype(ml_dtypes.bfloat16)).reshape(k // 32, 32, n)
    amax = np.abs(w).max(1)
    if fmt == "e4m3":
        byte = np.frexp(amax)[1] - 1 + 127 - 7
    else:
        mant, ex = np.frexp(amax / 6.0)
        byte = np.where(mant > 0.5, ex, ex - 1) + 127
    byte = np.clip(np.where(amax > 0, byte, 1), 1, 254)
    scaled = (w * np.exp2(127.0 - byte)[:, None, :]).reshape(k, n).astype(np.float32)
    by_word = np.ascontiguousarray(scaled.reshape(k // 512, 128, 4, n).transpose(0, 1, 3, 2))
    if fmt == "e4m3":
        words = by_word.astype(ml_dtypes.float8_e4m3fn).view(np.uint8)
    else:
        c = by_word.astype(ml_dtypes.float4_e2m1fn).view(np.uint8) & 0xF
        words = (c[..., 0::2] | (c[..., 1::2] << 4)).reshape(k // 512, 128, 2 * n)
    return np.ascontiguousarray(words), np.ascontiguousarray(byte.astype(np.uint8).reshape(k // 512, 16, n))


def unpack_weight(words, scales, fmt):
    g, _, n = scales.shape
    words = np.ascontiguousarray(words).reshape(g, 128, n, -1)
    if fmt == "e4m3":
        vals = words.view(ml_dtypes.float8_e4m3fn).astype(np.float64)
    else:
        nib = np.empty((g, 128, n, 4), np.uint8)
        nib[..., 0::2] = words & 0xF
        nib[..., 1::2] = words >> 4
        vals = E2M1[nib]
    vals = vals * np.repeat(np.exp2(scales.astype(np.float64) - 127.0), 8, axis=1)[..., None]
    return vals.transpose(0, 1, 3, 2).reshape(g * 512, n)


def silu(v):
    return v / (1.0 + np.exp(-np.maximum(v, -700.0)))


K, T, E, C, H, N = 1024, 768, 2, 256, 1024, 256


def by_expert(wq, xq):
    return np.concatenate([wq[e].T @ xq[:, e * C:(e + 1) * C] for e in range(E)], axis=1)


def setup_inputs():
    n = np.random.standard_normal
    s = mx_kscale(K)[:, None]
    u = mx_kscale(H)
    w1 = [pack_weight(m, "e2m1") for m in n((E, K, H)) / np.sqrt(K) / s[None]]
    w3 = [pack_weight(m, "e2m1") for m in n((E, K, H)) / np.sqrt(K) / s[None] * u[None, None, :]]
    w2 = [pack_weight(m, "e2m1") for m in n((E, H, N)) / np.sqrt(H) / u[None, :, None]]
    return {
        "xT": (n((K, T)) * s).astype(np.float32),
        "xr": n((N, T)).astype(np.float32),
        "w1_words": np.stack([m[0] for m in w1]),
        "w1_scales": np.stack([m[1] for m in w1]),
        "w3_words": np.stack([m[0] for m in w3]),
        "w3_scales": np.stack([m[1] for m in w3]),
        "w2_words": np.stack([m[0] for m in w2]),
        "w2_scales": np.stack([m[1] for m in w2]),
        "gate": np.tile(np.random.uniform(0.2, 1.0, E * C), (N, 1)).astype(np.float32),
        "offs": striped(np.random.permutation(T)[:E * C]),
    }


def reference(xT, xr, w1_words, w1_scales, w3_words, w3_scales, w2_words, w2_scales, gate, offs):
    idx = unstriped(offs)
    w1 = np.stack([unpack_weight(w1_words[e], w1_scales[e], "e2m1") for e in range(E)])
    w3 = np.stack([unpack_weight(w3_words[e], w3_scales[e], "e2m1") for e in range(E)])
    w2 = np.stack([unpack_weight(w2_words[e], w2_scales[e], "e2m1") for e in range(E)])
    xq = mxq(f64(xT)[:, idx], 0, "e4m3")
    h = silu(by_expert(w1, xq))
    h = h * by_expert(w3, xq)
    y = by_expert(w2, mxq(h, 0, "e4m3"))
    out = f64(xr).copy()
    out[:, idx] += f64(gate) * y
    return out

@@ -1,0 +1,234 @@
+from contextlib import ExitStack
+
+import concourse.mybir as mybir
+from concourse.masks import make_identity
+
+K, T, E, C, H, N = 1024, 768, 2, 256, 1024, 256
+SLOTS = E * C
+FLOPS = 2 * SLOTS * (2 * K * H + H * N)
+
+F32 = mybir.dt.float32
+BF16 = mybir.dt.bfloat16
+U32 = mybir.dt.uint32
+I32 = mybir.dt.int32
+U16 = mybir.dt.uint16
+U8 = mybir.dt.uint8
+FP8X4 = mybir.dt.float8_e4m3fn_x4
+FP4X4 = mybir.dt.float4_e2m1fn_x4
+MULT, ADD = mybir.AluOpType.mult, mybir.AluOpType.add
+SILU = mybir.ActivationFunctionType.Silu
+
+P = 128
+KP = 512
+PASSES = K // KP
+G = H // KP
+UNITS = SLOTS // P
+NT = N // P
+VEC_COLS = {(0, 0): 512, (0, 1): 256, (1, 0): 256, (1, 1): 384}
+
+
+def tile_moe_res_glu_silu_kernel(
+    tc, xT, xr, w1_words, w1_scales, w3_words, w3_scales, w2_words, w2_scales, gate, offs, out
+):
+    nc = tc.nc
+    with ExitStack() as ctx:
+        keep = ctx.enter_context(tc.tile_pool(name="keep", bufs=1))
+        ring = ctx.enter_context(tc.tile_pool(name="ring", bufs=2))
+        psum = ctx.enter_context(tc.psum_pool(name="psum", bufs=1))
+
+        offsets = keep.tile([P, SLOTS // 16], U16, name="offsets")
+
+        warm = keep.tile([P, 1], F32, name="warm")
+        nc.vector.memset(warm[:], 0.0)
+        nc.scalar.activation(warm[:], warm[:], SILU)
+        ident = keep.tile([P, P], F32, name="ident")
+        make_identity(nc, ident[:])
+        words = (w1_words, w3_words)
+        w2sc = keep.tile([P, E, PASSES, N], U8, name="w2sc", align_bytes=64)
+        nc.vector.memset(w2sc[:].rearrange("p e s n -> p (e s n)").bitcast(I32), 0)
+        wsc = {}
+        for m in range(2):
+            wsc[m] = keep.tile([P, E, PASSES, H], U8, name=f"wsc{m}", align_bytes=64)
+            nc.vector.memset(wsc[m][:].rearrange("p e s i -> p (e s i)").bitcast(I32), 0)
+        back = {}
+        for n in range(NT):
+            back[n] = keep.tile([P, T], F32, name=f"back{n}")
+            nc.vector.memset(back[n][:], 0.0)
+
+        def load_scales(plane, scales):
+            for q in range(4):
+                nc.sync.dma_start(
+                    plane[32 * q : 32 * q + 4].rearrange("p e s i -> p (e s) i").bitcast(I32),
+                    scales[:, :, 4 * q : 4 * q + 4, :].rearrange("e s q i -> q (e s) i").bitcast(I32),
+                )
+
+        xview = xT.rearrange("(s p u e) w -> s u p e w", s=PASSES, p=P, u=2, e=2)
+        raw = {}
+
+        def load_x(s, u):
+            raw[s, u] = keep.tile([P, 2, T], F32, name=f"raw{s}{u}")
+            nc.sync.dma_start(raw[s, u][:], xview[s, u])
+
+        wt = {}
+
+        def load_words(e, m):
+            wt[e, m] = keep.tile([P, PASSES, 2 * H], U8, name=f"wt{e}{m}", align_bytes=64)
+            nc.sync.dma_start(wt[e, m][:].bitcast(I32), words[m][e].rearrange("s p b -> p s b").bitcast(I32))
+
+        load_x(0, 0)
+        nc.sync.dma_start(offsets[:], offs)
+        load_scales(w2sc, w2_scales)
+        load_x(0, 1)
+        load_x(1, 0)
+        load_x(1, 1)
+        load_scales(wsc[0], w1_scales)
+        load_words(0, 0)
+        load_words(0, 1)
+        load_scales(wsc[1], w3_scales)
+        w2t = keep.tile([P, E, PASSES, 2 * N], U8, name="w2t", align_bytes=64)
+        nc.sync.dma_start(w2t[:].bitcast(I32), w2_words.rearrange("e s p b -> p e s b").bitcast(I32))
+        load_words(1, 0)
+        load_words(1, 1)
+        gates = keep.tile([P, SLOTS], F32, name="gates")
+        nc.sync.dma_start(gates[:], gate[0:P, :])
+        res_in = {}
+        for n in range(NT):
+            res_in[n] = keep.tile([P, T], F32, name=f"res_in{n}")
+            nc.sync.dma_start(res_in[n][:], xr[n * P : (n + 1) * P, :])
+
+        xq, xs, grouped, pairs = {}, {}, {}, {}
+        for s in range(PASSES):
+            for e in range(E):
+                grouped[s, e] = keep.tile([P, C, 4], BF16, name=f"grouped{s}{e}", align_bytes=64)
+                xq[s, e] = keep.tile([P, C], U32, name=f"xq{s}{e}", align_bytes=64)
+                xs[s, e] = keep.tile([P, C], U8, name=f"xs{s}{e}", align_bytes=64)
+
+        def gather(s, u, e):
+            pair_out = grouped[s, e][:].rearrange("p r t -> p (r t)").bitcast(U32).rearrange("p (r u) -> p r u", u=2)
+            table = pairs[s, u][:].rearrange("p w e -> p (w e)").bitcast(U32)
+            nc.vector.tensor_copy(pair_out[:, :, u], table.indirect(offsets[:, e * C // 16 : (e + 1) * C // 16]))
+
+        def quantise(s, e):
+            nc.vector.quantize_mx(
+                out=xq[s, e][:].bitcast(FP8X4), scales=xs[s, e][:], in_=grouped[s, e][:].rearrange("p r t -> p (r t)")
+            )
+
+        def round_pairs(s, u):
+            pairs[s, u] = keep.tile([P, T, 2], BF16, name=f"pairs{s}{u}", align_bytes=64)
+            src = raw[s, u][:].rearrange("p e w -> p w e")
+            v = VEC_COLS[s, u]
+            nc.vector.tensor_copy(pairs[s, u][:, 0:v, :], src[:, 0:v, :])
+            nc.scalar.copy(pairs[s, u][:, v:T, :], src[:, v:T, :])
+
+        round_pairs(0, 0)
+        gather(0, 0, 0)
+        gather(0, 0, 1)
+        round_pairs(0, 1)
+        gather(0, 1, 0)
+        round_pairs(1, 0)
+        quantise(0, 0)
+        gather(0, 1, 1)
+        round_pairs(1, 1)
+        gather(1, 0, 0)
+        gather(1, 1, 0)
+        quantise(1, 0)
+        quantise(0, 1)
+        gather(1, 0, 1)
+        gather(1, 1, 1)
+        quantise(1, 1)
+
+        def stage1(j):
+            e, c0 = j * P // C, j * P % C
+            cols = slice(c0, c0 + P)
+            acc = {}
+            for g in range(G):
+                for m in range(2):
+                    acc[g, m] = psum.tile([P, KP], F32, name=f"acc{g}{m}", tag="acc", bufs=5)
+            if j == 0:
+                order = [(g, m, s) for s in range(PASSES) for g in range(G) for m in range(2)]
+            else:
+                order = [(g, m, s) for g in range(G) for m in range(2) for s in range(PASSES)]
+            for g, m, s in order:
+                nc.tensor.matmul_mx(
+                    out=acc[g, m][:],
+                    lhsT=xq[s, e][:, cols].bitcast(FP8X4),
+                    lhsT_scale=xs[s, e][:, cols],
+                    rhs=wt[e, m][:, s, 2 * KP * g : 2 * KP * (g + 1)].bitcast(FP4X4),
+                    rhs_scale=wsc[m][:, e, s, g * KP : (g + 1) * KP],
+                    start=(s == 0),
+                    stop=(s == PASSES - 1),
+                )
+            h = ring.tile([P, G, 2, P, 2], BF16, name="h", align_bytes=64)
+            for g in range(G):
+                act = ring.tile([P, KP], F32, name="act", bufs=3)
+                nc.scalar.activation(act[:], acc[g, 0][:], SILU)
+                nc.vector.tensor_tensor(
+                    h[:, g, :, :, :],
+                    act[:].rearrange("r (p u e) -> r u p e", u=2, e=2),
+                    acc[g, 1][:].rearrange("r (p u e) -> r u p e", u=2, e=2),
+                    MULT,
+                )
+            return h
+
+        def turn(h):
+            turned = psum.tile([P, G, 2, P], F32, name="turned", tag="turned", bufs=2)
+            hq_in = ring.tile([P, G, P, 4], BF16, name="hq_in", align_bytes=64)
+            hq = ring.tile([P, G, P], U32, name="hq", align_bytes=64)
+            hs = ring.tile([P, G, P], U8, name="hs", align_bytes=64)
+            hw = h[:].rearrange("r g u p e -> r (g u p e)").bitcast(F32)
+            for g in range(G):
+                for u in range(2):
+                    w0 = (2 * g + u) * P
+                    nc.tensor.transpose(turned[:, g, u, :], hw[:, w0 : w0 + P], ident[:])
+            nc.scalar.copy(
+                hq_in[:].rearrange("p g r t -> p (g r t)").bitcast(F32).rearrange("p (g r u) -> p g r u", g=G, u=2),
+                turned[:].rearrange("p g u r -> p g r u"),
+            )
+            nc.vector.quantize_mx(
+                out=hq[:].rearrange("p g r -> p (g r)").bitcast(FP8X4),
+                scales=hs[:].rearrange("p g r -> p (g r)"),
+                in_=hq_in[:].rearrange("p g r t -> p (g r t)"),
+            )
+            return hq, hs
+
+        def stage2(j, hq, hs, y_sb):
+            e = j * P // C
+            y = psum.tile([P, NT, P], F32, name="y", tag="y", bufs=1)
+            for n in range(NT):
+                for g in range(G):
+                    nc.tensor.matmul_mx(
+                        out=y[:, n, :],
+                        lhsT=w2t[:, e, g, 2 * P * n : 2 * P * (n + 1)].bitcast(FP4X4),
+                        lhsT_scale=w2sc[:, e, g, P * n : P * (n + 1)],
+                        rhs=hq[:, g, :].bitcast(FP8X4),
+                        rhs_scale=hs[:, g, :],
+                        start=(g == 0),
+                        stop=(g == G - 1),
+                    )
+            nc.scalar.copy(y_sb[:], y[:])
+
+        def scatter(y_sb, j):
+            cols = slice(j * P, (j + 1) * P)
+            for n in range(NT):
+                nc.vector.tensor_tensor(
+                    back[n][:].indirect(offsets[:, j * P // 16 : (j + 1) * P // 16]), y_sb[:, n, :], gates[:, cols], MULT
+                )
+
+        ys = {j: keep.tile([P, NT, P], F32, name=f"ys{j}") for j in range(UNITS)}
+        h = {}
+        h[0] = stage1(0)
+        turned_h = {}
+        for t in range(1, UNITS + 2):
+            if t < UNITS:
+                h[t] = stage1(t)
+            if t - 1 < UNITS:
+                turned_h[t - 1] = turn(h[t - 1])
+            if t >= 2:
+                stage2(t - 2, *turned_h[t - 2], ys[t - 2])
+                scatter(ys[t - 2], t - 2)
+
+        for n in range(NT):
+            done = keep.tile([P, T], F32, name=f"done{n}")
+            for cols in (slice(0, 512), slice(512, T)):
+                nc.vector.tensor_tensor(done[:, cols], back[n][:, cols], res_in[n][:, cols], ADD)
+                nc.sync.dma_start(out[n * P : (n + 1) * P, cols], done[:, cols])

@@ -24,7 +24,9 @@ PASSES = K // KP
 G = H // KP
 UNITS = SLOTS // P
 NT = N // P
-VEC_COLS = {(0, 0): 512, (0, 1): 256, (1, 0): 256, (1, 1): 384}
+CHUNK = 256
+CHUNKS = T // CHUNK
+VEC_TOKENS = 160
 
 
 def tile_moe_res_glu_silu_kernel(
@@ -34,144 +36,169 @@ def tile_moe_res_glu_silu_kernel(
     with ExitStack() as ctx:
         keep = ctx.enter_context(tc.tile_pool(name="keep", bufs=1))
         ring = ctx.enter_context(tc.tile_pool(name="ring", bufs=2))
-        psum = ctx.enter_context(tc.psum_pool(name="psum", bufs=1))
+        psum = ctx.enter_context(tc.psum_pool(name="psum", bufs=8))
 
         offsets = keep.tile([P, SLOTS // 16], U16, name="offsets")
+
+        words = (w1_words, w3_words)
+        scales = (w1_scales, w3_scales)
+        wsc = {}
+        for e in range(E):
+            for m in range(2):
+                wsc[e, m] = keep.tile([P, PASSES, H], U8, name=f"wsc{e}{m}", align_bytes=64)
+                engine = nc.gpsimd if m == 0 else nc.vector
+                engine.memset(wsc[e, m][:].rearrange("p s i -> p (s i)").bitcast(I32), 0)
+
+        def load_scales(e, m, first):
+            rows = scales[m][e].rearrange("s (q r) i -> r q s i", r=4)
+            for r in (first, first + 1):
+                nc.sync.dma_start(wsc[e, m][r:P:32].bitcast(I32), rows[r].bitcast(I32))
+
+        def load_w2_scales(first):
+            rows = w2_scales.rearrange("e s (q r) n -> r q (e s) n", r=4)
+            for r in (first, first + 1):
+                nc.sync.dma_start(w2sc[r:P:32].rearrange("p e s n -> p (e s) n").bitcast(I32), rows[r].bitcast(I32))
 
         warm = keep.tile([P, 1], F32, name="warm")
         nc.vector.memset(warm[:], 0.0)
         nc.scalar.activation(warm[:], warm[:], SILU)
-        ident = keep.tile([P, P], F32, name="ident")
-        make_identity(nc, ident[:])
-        words = (w1_words, w3_words)
+        codes, bytes_all, xq, xs = {}, {}, {}, {}
+        for s in range(PASSES):
+            codes[s] = keep.tile([P, T], U32, name=f"codes{s}", align_bytes=64)
+            bytes_all[s] = keep.tile([P, T], U8, name=f"bytes{s}", align_bytes=64)
+            nc.vector.memset(bytes_all[s][:].bitcast(I32), 0)
+            xq[s] = keep.tile([P, SLOTS], U32, name=f"xq{s}", align_bytes=64)
+            xs[s] = keep.tile([P, SLOTS], U8, name=f"xs{s}", align_bytes=64)
         w2sc = keep.tile([P, E, PASSES, N], U8, name="w2sc", align_bytes=64)
         nc.vector.memset(w2sc[:].rearrange("p e s n -> p (e s n)").bitcast(I32), 0)
-        wsc = {}
-        for m in range(2):
-            wsc[m] = keep.tile([P, E, PASSES, H], U8, name=f"wsc{m}", align_bytes=64)
-            nc.vector.memset(wsc[m][:].rearrange("p e s i -> p (e s i)").bitcast(I32), 0)
         back = {}
         for n in range(NT):
             back[n] = keep.tile([P, T], F32, name=f"back{n}")
             nc.vector.memset(back[n][:], 0.0)
+        ident = keep.tile([P, P], F32, name="ident")
+        make_identity(nc, ident[:])
 
-        def load_scales(plane, scales):
-            for q in range(4):
-                nc.sync.dma_start(
-                    plane[32 * q : 32 * q + 4].rearrange("p e s i -> p (e s) i").bitcast(I32),
-                    scales[:, :, 4 * q : 4 * q + 4, :].rearrange("e s q i -> q (e s) i").bitcast(I32),
-                )
-
-        xview = xT.rearrange("(s p u e) w -> s u p e w", s=PASSES, p=P, u=2, e=2)
+        xview = xT.rearrange("(s p j) w -> s p j w", s=PASSES, p=P)
         raw = {}
 
-        def load_x(s, u):
-            raw[s, u] = keep.tile([P, 2, T], F32, name=f"raw{s}{u}")
-            nc.sync.dma_start(raw[s, u][:], xview[s, u])
+        def load_x(s, c):
+            raw[s, c] = keep.tile([P, 4, CHUNK], F32, name=f"raw{s}{c}")
+            nc.sync.dma_start(raw[s, c][:], xview[s][:, :, c * CHUNK : (c + 1) * CHUNK])
 
         wt = {}
 
-        def load_words(e, m):
-            wt[e, m] = keep.tile([P, PASSES, 2 * H], U8, name=f"wt{e}{m}", align_bytes=64)
-            nc.sync.dma_start(wt[e, m][:].bitcast(I32), words[m][e].rearrange("s p b -> p s b").bitcast(I32))
+        def load_words(e, m, s):
+            wt[e, m, s] = keep.tile([P, 2 * H], U8, name=f"wt{e}{m}{s}", align_bytes=64)
+            nc.sync.dma_start(wt[e, m, s][:].bitcast(I32), words[m][e, s].bitcast(I32))
+
+        def load_words_both(e, m):
+            both = keep.tile([P, PASSES, 2 * H], U8, name=f"wt{e}{m}", align_bytes=64)
+            nc.sync.dma_start(both[:].bitcast(I32), words[m][e].rearrange("s p b -> p s b").bitcast(I32))
+            for s in range(PASSES):
+                wt[e, m, s] = both[:, s, :]
 
         load_x(0, 0)
         nc.sync.dma_start(offsets[:], offs)
-        load_scales(w2sc, w2_scales)
         load_x(0, 1)
+        load_x(0, 2)
+        load_scales(0, 0, 0)
+        load_scales(0, 0, 2)
+        load_words(0, 0, 0)
         load_x(1, 0)
         load_x(1, 1)
-        load_scales(wsc[0], w1_scales)
-        load_words(0, 0)
-        load_words(0, 1)
-        load_scales(wsc[1], w3_scales)
+        load_x(1, 2)
+        load_scales(0, 1, 0)
+        load_scales(0, 1, 2)
+        load_words(0, 1, 0)
+        load_words(0, 0, 1)
+        load_words(0, 1, 1)
+        load_scales(1, 0, 0)
+        load_words_both(1, 0)
+        load_scales(1, 0, 2)
+        load_scales(1, 1, 0)
+        load_words_both(1, 1)
+        load_scales(1, 1, 2)
         w2t = keep.tile([P, E, PASSES, 2 * N], U8, name="w2t", align_bytes=64)
         nc.sync.dma_start(w2t[:].bitcast(I32), w2_words.rearrange("e s p b -> p e s b").bitcast(I32))
-        load_words(1, 0)
-        load_words(1, 1)
+        load_w2_scales(0)
         gates = keep.tile([P, SLOTS], F32, name="gates")
         nc.sync.dma_start(gates[:], gate[0:P, :])
+        load_w2_scales(2)
         res_in = {}
         for n in range(NT):
             res_in[n] = keep.tile([P, T], F32, name=f"res_in{n}")
             nc.sync.dma_start(res_in[n][:], xr[n * P : (n + 1) * P, :])
 
-        xq, xs, grouped, pairs = {}, {}, {}, {}
-        for s in range(PASSES):
-            for e in range(E):
-                grouped[s, e] = keep.tile([P, C, 4], BF16, name=f"grouped{s}{e}", align_bytes=64)
-                xq[s, e] = keep.tile([P, C], U32, name=f"xq{s}{e}", align_bytes=64)
-                xs[s, e] = keep.tile([P, C], U8, name=f"xs{s}{e}", align_bytes=64)
-
-        def gather(s, u, e):
-            pair_out = grouped[s, e][:].rearrange("p r t -> p (r t)").bitcast(U32).rearrange("p (r u) -> p r u", u=2)
-            table = pairs[s, u][:].rearrange("p w e -> p (w e)").bitcast(U32)
-            nc.vector.tensor_copy(pair_out[:, :, u], table.indirect(offsets[:, e * C // 16 : (e + 1) * C // 16]))
-
-        def quantise(s, e):
+        def quantise_chunk(s, c):
+            grouped = keep.tile([P, CHUNK, 4], BF16, name=f"grouped{s}{c}", align_bytes=64)
+            src = raw[s, c][:].rearrange("p j w -> p w j")
+            v = VEC_TOKENS if s == 0 or c == CHUNKS - 1 else 0
+            if v:
+                nc.vector.tensor_copy(grouped[:, 0:v, :], src[:, 0:v, :])
+            nc.scalar.copy(grouped[:, v:CHUNK, :], src[:, v:CHUNK, :])
+            cols = slice(c * CHUNK, (c + 1) * CHUNK)
             nc.vector.quantize_mx(
-                out=xq[s, e][:].bitcast(FP8X4), scales=xs[s, e][:], in_=grouped[s, e][:].rearrange("p r t -> p (r t)")
+                out=codes[s][:, cols].bitcast(FP8X4),
+                scales=bytes_all[s][:, cols],
+                in_=grouped[:].rearrange("p w j -> p (w j)"),
             )
 
-        def round_pairs(s, u):
-            pairs[s, u] = keep.tile([P, T, 2], BF16, name=f"pairs{s}{u}", align_bytes=64)
-            src = raw[s, u][:].rearrange("p e w -> p w e")
-            v = VEC_COLS[s, u]
-            nc.vector.tensor_copy(pairs[s, u][:, 0:v, :], src[:, 0:v, :])
-            nc.scalar.copy(pairs[s, u][:, v:T, :], src[:, v:T, :])
+        def gather(s, first, last):
+            part = offsets[:, first // 16 : last // 16]
+            nc.vector.tensor_copy(xq[s][:, first:last], codes[s][:].indirect(part))
+            nc.vector.tensor_copy(xs[s][:, first:last], bytes_all[s][:].indirect(part))
 
-        round_pairs(0, 0)
-        gather(0, 0, 0)
-        gather(0, 0, 1)
-        round_pairs(0, 1)
-        gather(0, 1, 0)
-        round_pairs(1, 0)
-        quantise(0, 0)
-        gather(0, 1, 1)
-        round_pairs(1, 1)
-        gather(1, 0, 0)
-        gather(1, 1, 0)
-        quantise(1, 0)
-        quantise(0, 1)
-        gather(1, 0, 1)
-        gather(1, 1, 1)
-        quantise(1, 1)
+        acc = {}
 
-        def stage1(j):
-            e, c0 = j * P // C, j * P % C
-            cols = slice(c0, c0 + P)
-            acc = {}
+        def first_layer(j, s):
+            e = j * P // C
+            cols = slice(j * P, (j + 1) * P)
             for g in range(G):
                 for m in range(2):
-                    acc[g, m] = psum.tile([P, KP], F32, name=f"acc{g}{m}", tag="acc", bufs=5)
-            if j == 0:
-                order = [(g, m, s) for s in range(PASSES) for g in range(G) for m in range(2)]
-            else:
-                order = [(g, m, s) for g in range(G) for m in range(2) for s in range(PASSES)]
-            for g, m, s in order:
-                nc.tensor.matmul_mx(
-                    out=acc[g, m][:],
-                    lhsT=xq[s, e][:, cols].bitcast(FP8X4),
-                    lhsT_scale=xs[s, e][:, cols],
-                    rhs=wt[e, m][:, s, 2 * KP * g : 2 * KP * (g + 1)].bitcast(FP4X4),
-                    rhs_scale=wsc[m][:, e, s, g * KP : (g + 1) * KP],
-                    start=(s == 0),
-                    stop=(s == PASSES - 1),
-                )
+                    if s == 0:
+                        acc[j, g, m] = psum.tile([P, KP], F32, name="acc", tag="bank")
+                    nc.tensor.matmul_mx(
+                        out=acc[j, g, m][:],
+                        lhsT=xq[s][:, cols].bitcast(FP8X4),
+                        lhsT_scale=xs[s][:, cols],
+                        rhs=wt[e, m, s][:, 2 * KP * g : 2 * KP * (g + 1)].bitcast(FP4X4),
+                        rhs_scale=wsc[e, m][:, s, g * KP : (g + 1) * KP],
+                        start=(s == 0),
+                        stop=(s == PASSES - 1),
+                    )
+
+        def first_layer_whole(j):
+            e = j * P // C
+            cols = slice(j * P, (j + 1) * P)
+            for g in range(G):
+                for m in range(2):
+                    acc[j, g, m] = psum.tile([P, KP], F32, name="acc", tag="bank")
+                    for s in range(PASSES):
+                        nc.tensor.matmul_mx(
+                            out=acc[j, g, m][:],
+                            lhsT=xq[s][:, cols].bitcast(FP8X4),
+                            lhsT_scale=xs[s][:, cols],
+                            rhs=wt[e, m, s][:, 2 * KP * g : 2 * KP * (g + 1)].bitcast(FP4X4),
+                            rhs_scale=wsc[e, m][:, s, g * KP : (g + 1) * KP],
+                            start=(s == 0),
+                            stop=(s == PASSES - 1),
+                        )
+
+        def hidden(j):
             h = ring.tile([P, G, 2, P, 2], BF16, name="h", align_bytes=64)
             for g in range(G):
                 act = ring.tile([P, KP], F32, name="act", bufs=3)
-                nc.scalar.activation(act[:], acc[g, 0][:], SILU)
+                nc.scalar.activation(act[:], acc[j, g, 0][:], SILU)
                 nc.vector.tensor_tensor(
                     h[:, g, :, :, :],
                     act[:].rearrange("r (p u e) -> r u p e", u=2, e=2),
-                    acc[g, 1][:].rearrange("r (p u e) -> r u p e", u=2, e=2),
+                    acc[j, g, 1][:].rearrange("r (p u e) -> r u p e", u=2, e=2),
                     MULT,
                 )
             return h
 
         def turn(h):
-            turned = psum.tile([P, G, 2, P], F32, name="turned", tag="turned", bufs=2)
+            turned = psum.tile([P, G, 2, P], F32, name="turned", tag="bank")
             hq_in = ring.tile([P, G, P, 4], BF16, name="hq_in", align_bytes=64)
             hq = ring.tile([P, G, P], U32, name="hq", align_bytes=64)
             hs = ring.tile([P, G, P], U8, name="hs", align_bytes=64)
@@ -191,9 +218,9 @@ def tile_moe_res_glu_silu_kernel(
             )
             return hq, hs
 
-        def stage2(j, hq, hs, y_sb):
+        def second_layer(j, hq, hs):
             e = j * P // C
-            y = psum.tile([P, NT, P], F32, name="y", tag="y", bufs=1)
+            y = psum.tile([P, NT, P], F32, name="y", tag="bank")
             for n in range(NT):
                 for g in range(G):
                     nc.tensor.matmul_mx(
@@ -205,27 +232,38 @@ def tile_moe_res_glu_silu_kernel(
                         start=(g == 0),
                         stop=(g == G - 1),
                     )
+            y_sb = keep.tile([P, NT, P], F32, name=f"ys{j}")
             nc.scalar.copy(y_sb[:], y[:])
-
-        def scatter(y_sb, j):
             cols = slice(j * P, (j + 1) * P)
             for n in range(NT):
                 nc.vector.tensor_tensor(
                     back[n][:].indirect(offsets[:, j * P // 16 : (j + 1) * P // 16]), y_sb[:, n, :], gates[:, cols], MULT
                 )
 
-        ys = {j: keep.tile([P, NT, P], F32, name=f"ys{j}") for j in range(UNITS)}
-        h = {}
-        h[0] = stage1(0)
-        turned_h = {}
+        for c in range(CHUNKS):
+            quantise_chunk(0, c)
+        gather(0, 0, C)
+        first_layer(0, 0)
+        first_layer(1, 0)
+        for c in range(CHUNKS):
+            quantise_chunk(1, c)
+        gather(0, C, SLOTS)
+        gather(1, 0, P)
+        first_layer(0, 1)
+        gather(1, P, C)
+        first_layer(1, 1)
+        h, turned_h = {}, {}
+        h[0] = hidden(0)
+        gather(1, C, SLOTS)
         for t in range(1, UNITS + 2):
-            if t < UNITS:
-                h[t] = stage1(t)
             if t - 1 < UNITS:
                 turned_h[t - 1] = turn(h[t - 1])
             if t >= 2:
-                stage2(t - 2, *turned_h[t - 2], ys[t - 2])
-                scatter(ys[t - 2], t - 2)
+                second_layer(t - 2, *turned_h[t - 2])
+            if t < UNITS:
+                h[t] = hidden(t)
+            if 2 <= t + 1 < UNITS:
+                first_layer_whole(t + 1)
 
         for n in range(NT):
             done = keep.tile([P, T], F32, name=f"done{n}")

@@ -131,11 +131,12 @@ def tile_moe_res_glu_silu_kernel(
 
         def quantise_chunk(s, c):
             grouped = keep.tile([P, CHUNK, 4], BF16, name=f"grouped{s}{c}", align_bytes=64)
-            src = raw[s, c][:].rearrange("p j w -> p w j")
+            src = raw[s, c][:].rearrange("p j (b i) -> p b j i", i=4)
+            dst = grouped[:].rearrange("p (b i) j -> p b j i", i=4)
             v = VEC_TOKENS if s == 0 or c == CHUNKS - 1 else 0
             if v:
-                nc.vector.tensor_copy(grouped[:, 0:v, :], src[:, 0:v, :])
-            nc.scalar.copy(grouped[:, v:CHUNK, :], src[:, v:CHUNK, :])
+                nc.vector.tensor_copy(dst[:, 0 : v // 4], src[:, 0 : v // 4])
+            nc.scalar.copy(dst[:, v // 4 :], src[:, v // 4 :])
             cols = slice(c * CHUNK, (c + 1) * CHUNK)
             nc.vector.quantize_mx(
                 out=codes[s][:, cols].bitcast(FP8X4),

@@ -24,8 +24,9 @@ PASSES = K // KP
 G = H // KP
 UNITS = SLOTS // P
 NT = N // P
-CHUNK = 256
-CHUNKS = T // CHUNK
+CHUNK_STARTS = (0, 512, T)
+CHUNKS = 2
+QUANT = 256
 VEC_TOKENS = 160
 
 
@@ -82,8 +83,9 @@ def tile_moe_res_glu_silu_kernel(
         raw = {}
 
         def load_x(s, c):
-            raw[s, c] = keep.tile([P, 4, CHUNK], F32, name=f"raw{s}{c}")
-            nc.sync.dma_start(raw[s, c][:], xview[s][:, :, c * CHUNK : (c + 1) * CHUNK])
+            first, last = CHUNK_STARTS[c], CHUNK_STARTS[c + 1]
+            raw[s, c] = keep.tile([P, 4, last - first], F32, name=f"raw{s}{c}")
+            nc.sync.dma_start(raw[s, c][:], xview[s][:, :, first:last])
 
         wt = {}
 
@@ -100,13 +102,11 @@ def tile_moe_res_glu_silu_kernel(
         load_x(0, 0)
         nc.sync.dma_start(offsets[:], offs)
         load_x(0, 1)
-        load_x(0, 2)
         load_scales(0, 0, 0)
         load_scales(0, 0, 2)
         load_words(0, 0, 0)
         load_x(1, 0)
         load_x(1, 1)
-        load_x(1, 2)
         load_scales(0, 1, 0)
         load_scales(0, 1, 2)
         load_words(0, 1, 0)
@@ -129,15 +129,17 @@ def tile_moe_res_glu_silu_kernel(
             res_in[n] = keep.tile([P, T], F32, name=f"res_in{n}")
             nc.sync.dma_start(res_in[n][:], xr[n * P : (n + 1) * P, :])
 
-        def quantise_chunk(s, c):
-            grouped = keep.tile([P, CHUNK, 4], BF16, name=f"grouped{s}{c}", align_bytes=64)
-            src = raw[s, c][:].rearrange("p j (b i) -> p b j i", i=4)
+        def quantise_chunk(s, b):
+            c = b * QUANT // CHUNK_STARTS[1]
+            first = b * QUANT - CHUNK_STARTS[c]
+            grouped = keep.tile([P, QUANT, 4], BF16, name=f"grouped{s}{b}", align_bytes=64)
+            src = raw[s, c][:, :, first : first + QUANT].rearrange("p j (b i) -> p b j i", i=4)
             dst = grouped[:].rearrange("p (b i) j -> p b j i", i=4)
-            v = VEC_TOKENS if s == 0 or c == CHUNKS - 1 else 0
+            v = VEC_TOKENS if s == 0 or b == T // QUANT - 1 else 0
             if v:
                 nc.vector.tensor_copy(dst[:, 0 : v // 4], src[:, 0 : v // 4])
             nc.scalar.copy(dst[:, v // 4 :], src[:, v // 4 :])
-            cols = slice(c * CHUNK, (c + 1) * CHUNK)
+            cols = slice(b * QUANT, (b + 1) * QUANT)
             nc.vector.quantize_mx(
                 out=codes[s][:, cols].bitcast(FP8X4),
                 scales=bytes_all[s][:, cols],
@@ -241,12 +243,12 @@ def tile_moe_res_glu_silu_kernel(
                     back[n][:].indirect(offsets[:, j * P // 16 : (j + 1) * P // 16]), y_sb[:, n, :], gates[:, cols], MULT
                 )
 
-        for c in range(CHUNKS):
+        for c in range(T // QUANT):
             quantise_chunk(0, c)
         gather(0, 0, C)
         first_layer(0, 0)
         first_layer(1, 0)
-        for c in range(CHUNKS):
+        for c in range(T // QUANT):
             quantise_chunk(1, c)
         gather(0, C, SLOTS)
         gather(1, 0, P)

@@ -24,10 +24,8 @@ PASSES = K // KP
 G = H // KP
 UNITS = SLOTS // P
 NT = N // P
-CHUNK_STARTS = (0, 512, T)
-CHUNKS = 2
 QUANT = 256
-VEC_TOKENS = 160
+VEC_TOKENS = ((160, 160, 160), (0, 0, 160))
 
 
 def tile_moe_res_glu_silu_kernel(
@@ -81,42 +79,43 @@ def tile_moe_res_glu_silu_kernel(
 
         xview = xT.rearrange("(s p j) w -> s p j w", s=PASSES, p=P)
         raw = {}
+        for s in range(PASSES):
+            raw[s] = keep.tile([P, 4, T], F32, name=f"raw{s}")
 
-        def load_x(s, c):
-            first, last = CHUNK_STARTS[c], CHUNK_STARTS[c + 1]
-            raw[s, c] = keep.tile([P, 4, last - first], F32, name=f"raw{s}{c}")
-            nc.sync.dma_start(raw[s, c][:], xview[s][:, :, first:last])
+        def load_x(s, j0, j1, c0, c1):
+            nc.sync.dma_start(raw[s][:, j0:j1, c0:c1], xview[s][:, j0:j1, c0:c1])
 
         wt = {}
 
-        def load_words(e, m, s):
-            wt[e, m, s] = keep.tile([P, 2 * H], U8, name=f"wt{e}{m}{s}", align_bytes=64)
-            nc.sync.dma_start(wt[e, m, s][:].bitcast(I32), words[m][e, s].bitcast(I32))
+        def load_words(e, m, passes, halves):
+            piece = keep.tile(
+                [P, len(passes), len(halves) * 2 * KP], U8, name=f"wt{e}{m}{passes[0]}{halves[0]}", align_bytes=64
+            )
+            source = words[m][e].rearrange("s p b -> p s b")
+            cols = slice(halves[0] * 2 * KP, (halves[-1] + 1) * 2 * KP)
+            nc.sync.dma_start(piece[:].bitcast(I32), source[:, passes[0] : passes[-1] + 1, cols].bitcast(I32))
+            for s in passes:
+                for g in halves:
+                    wt[e, m, s, g] = piece[:, s - passes[0], (g - halves[0]) * 2 * KP : (g - halves[0] + 1) * 2 * KP]
 
-        def load_words_both(e, m):
-            both = keep.tile([P, PASSES, 2 * H], U8, name=f"wt{e}{m}", align_bytes=64)
-            nc.sync.dma_start(both[:].bitcast(I32), words[m][e].rearrange("s p b -> p s b").bitcast(I32))
-            for s in range(PASSES):
-                wt[e, m, s] = both[:, s, :]
-
-        load_x(0, 0)
+        load_x(0, 0, 4, 0, 512)
         nc.sync.dma_start(offsets[:], offs)
-        load_x(0, 1)
+        load_x(0, 0, 4, 512, 768)
+        load_x(1, 0, 4, 0, 512)
         load_scales(0, 0, 0)
         load_scales(0, 0, 2)
-        load_words(0, 0, 0)
-        load_x(1, 0)
-        load_x(1, 1)
+        load_words(0, 0, (0,), (0, 1))
+        load_x(1, 0, 4, 512, 768)
         load_scales(0, 1, 0)
         load_scales(0, 1, 2)
-        load_words(0, 1, 0)
-        load_words(0, 0, 1)
-        load_words(0, 1, 1)
+        load_words(0, 1, (0,), (0, 1))
+        load_words(0, 0, (1,), (0, 1))
+        load_words(0, 1, (1,), (0, 1))
         load_scales(1, 0, 0)
-        load_words_both(1, 0)
+        load_words(1, 0, (0, 1), (0, 1))
         load_scales(1, 0, 2)
         load_scales(1, 1, 0)
-        load_words_both(1, 1)
+        load_words(1, 1, (0, 1), (0, 1))
         load_scales(1, 1, 2)
         w2t = keep.tile([P, E, PASSES, 2 * N], U8, name="w2t", align_bytes=64)
         nc.sync.dma_start(w2t[:].bitcast(I32), w2_words.rearrange("e s p b -> p e s b").bitcast(I32))
@@ -130,12 +129,11 @@ def tile_moe_res_glu_silu_kernel(
             nc.sync.dma_start(res_in[n][:], xr[n * P : (n + 1) * P, :])
 
         def quantise_chunk(s, b):
-            c = b * QUANT // CHUNK_STARTS[1]
-            first = b * QUANT - CHUNK_STARTS[c]
+            first = b * QUANT
             grouped = keep.tile([P, QUANT, 4], BF16, name=f"grouped{s}{b}", align_bytes=64)
-            src = raw[s, c][:, :, first : first + QUANT].rearrange("p j (b i) -> p b j i", i=4)
+            src = raw[s][:, :, first : first + QUANT].rearrange("p j (b i) -> p b j i", i=4)
             dst = grouped[:].rearrange("p (b i) j -> p b j i", i=4)
-            v = VEC_TOKENS if s == 0 or b == T // QUANT - 1 else 0
+            v = VEC_TOKENS[s][b]
             if v:
                 nc.vector.tensor_copy(dst[:, 0 : v // 4], src[:, 0 : v // 4])
             nc.scalar.copy(dst[:, v // 4 :], src[:, v // 4 :])
@@ -164,7 +162,7 @@ def tile_moe_res_glu_silu_kernel(
                         out=acc[j, g, m][:],
                         lhsT=xq[s][:, cols].bitcast(FP8X4),
                         lhsT_scale=xs[s][:, cols],
-                        rhs=wt[e, m, s][:, 2 * KP * g : 2 * KP * (g + 1)].bitcast(FP4X4),
+                        rhs=wt[e, m, s, g].bitcast(FP4X4),
                         rhs_scale=wsc[e, m][:, s, g * KP : (g + 1) * KP],
                         start=(s == 0),
                         stop=(s == PASSES - 1),
@@ -181,7 +179,7 @@ def tile_moe_res_glu_silu_kernel(
                             out=acc[j, g, m][:],
                             lhsT=xq[s][:, cols].bitcast(FP8X4),
                             lhsT_scale=xs[s][:, cols],
-                            rhs=wt[e, m, s][:, 2 * KP * g : 2 * KP * (g + 1)].bitcast(FP4X4),
+                            rhs=wt[e, m, s, g].bitcast(FP4X4),
                             rhs_scale=wsc[e, m][:, s, g * KP : (g + 1) * KP],
                             start=(s == 0),
                             stop=(s == PASSES - 1),

@@ -112,17 +112,19 @@ def tile_moe_res_glu_silu_kernel(
         load_words(0, 0, (1,), (0, 1))
         load_words(0, 1, (1,), (0, 1))
         load_scales(1, 0, 0)
-        load_words(1, 0, (0, 1), (0, 1))
         load_scales(1, 0, 2)
+        load_words(1, 0, (0, 1), (0,))
         load_scales(1, 1, 0)
-        load_words(1, 1, (0, 1), (0, 1))
         load_scales(1, 1, 2)
+        load_words(1, 1, (0, 1), (0,))
+        load_words(1, 0, (0, 1), (1,))
+        load_words(1, 1, (0, 1), (1,))
         w2t = keep.tile([P, E, PASSES, 2 * N], U8, name="w2t", align_bytes=64)
         nc.sync.dma_start(w2t[:].bitcast(I32), w2_words.rearrange("e s p b -> p e s b").bitcast(I32))
         load_w2_scales(0)
+        load_w2_scales(2)
         gates = keep.tile([P, SLOTS], F32, name="gates")
         nc.sync.dma_start(gates[:], gate[0:P, :])
-        load_w2_scales(2)
         res_in = {}
         for n in range(NT):
             res_in[n] = keep.tile([P, T], F32, name=f"res_in{n}")
@@ -149,61 +151,46 @@ def tile_moe_res_glu_silu_kernel(
             nc.vector.tensor_copy(xq[s][:, first:last], codes[s][:].indirect(part))
             nc.vector.tensor_copy(xs[s][:, first:last], bytes_all[s][:].indirect(part))
 
-        acc = {}
+        acc, h, turned, hq, hs = {}, {}, {}, {}, {}
 
-        def first_layer(j, s):
+        def product(j, g, m, s):
             e = j * P // C
             cols = slice(j * P, (j + 1) * P)
-            for g in range(G):
-                for m in range(2):
-                    if s == 0:
-                        acc[j, g, m] = psum.tile([P, KP], F32, name="acc", tag="bank")
-                    nc.tensor.matmul_mx(
-                        out=acc[j, g, m][:],
-                        lhsT=xq[s][:, cols].bitcast(FP8X4),
-                        lhsT_scale=xs[s][:, cols],
-                        rhs=wt[e, m, s, g].bitcast(FP4X4),
-                        rhs_scale=wsc[e, m][:, s, g * KP : (g + 1) * KP],
-                        start=(s == 0),
-                        stop=(s == PASSES - 1),
-                    )
+            if s == 0:
+                acc[j, g, m] = psum.tile([P, KP], F32, name="acc", tag="bank")
+            nc.tensor.matmul_mx(
+                out=acc[j, g, m][:],
+                lhsT=xq[s][:, cols].bitcast(FP8X4),
+                lhsT_scale=xs[s][:, cols],
+                rhs=wt[e, m, s, g].bitcast(FP4X4),
+                rhs_scale=wsc[e, m][:, s, g * KP : (g + 1) * KP],
+                start=(s == 0),
+                stop=(s == PASSES - 1),
+            )
 
-        def first_layer_whole(j):
-            e = j * P // C
-            cols = slice(j * P, (j + 1) * P)
-            for g in range(G):
-                for m in range(2):
-                    acc[j, g, m] = psum.tile([P, KP], F32, name="acc", tag="bank")
-                    for s in range(PASSES):
-                        nc.tensor.matmul_mx(
-                            out=acc[j, g, m][:],
-                            lhsT=xq[s][:, cols].bitcast(FP8X4),
-                            lhsT_scale=xs[s][:, cols],
-                            rhs=wt[e, m, s, g].bitcast(FP4X4),
-                            rhs_scale=wsc[e, m][:, s, g * KP : (g + 1) * KP],
-                            start=(s == 0),
-                            stop=(s == PASSES - 1),
-                        )
+        def first_layer(j, g):
+            for m in range(2):
+                for s in range(PASSES):
+                    product(j, g, m, s)
 
-        def hidden(j):
-            h = ring.tile([P, G, 2, P, 2], BF16, name="h", align_bytes=64)
-            for g in range(G):
-                act = ring.tile([P, KP], F32, name="act", bufs=3)
-                nc.scalar.activation(act[:], acc[j, g, 0][:], SILU)
-                nc.vector.tensor_tensor(
-                    h[:, g, :, :, :],
-                    act[:].rearrange("r (p u e) -> r u p e", u=2, e=2),
-                    acc[j, g, 1][:].rearrange("r (p u e) -> r u p e", u=2, e=2),
-                    MULT,
-                )
-            return h
+        def hidden(j, g):
+            if g == 0:
+                h[j] = ring.tile([P, G, 2, P, 2], BF16, name="h", align_bytes=64)
+            act = ring.tile([P, KP], F32, name="act", bufs=3)
+            nc.scalar.activation(act[:], acc[j, g, 0][:], SILU)
+            nc.vector.tensor_tensor(
+                h[j][:, g, :, :, :],
+                act[:].rearrange("r (p u e) -> r u p e", u=2, e=2),
+                acc[j, g, 1][:].rearrange("r (p u e) -> r u p e", u=2, e=2),
+                MULT,
+            )
 
-        def turn(h):
+        def turn(j):
             turned = psum.tile([P, G, 2, P], F32, name="turned", tag="bank")
             hq_in = ring.tile([P, G, P, 4], BF16, name="hq_in", align_bytes=64)
-            hq = ring.tile([P, G, P], U32, name="hq", align_bytes=64)
-            hs = ring.tile([P, G, P], U8, name="hs", align_bytes=64)
-            hw = h[:].rearrange("r g u p e -> r (g u p e)").bitcast(F32)
+            hq[j] = ring.tile([P, G, P], U32, name="hq", align_bytes=64)
+            hs[j] = ring.tile([P, G, P], U8, name="hs", align_bytes=64)
+            hw = h[j][:].rearrange("r g u p e -> r (g u p e)").bitcast(F32)
             for g in range(G):
                 for u in range(2):
                     w0 = (2 * g + u) * P
@@ -213,13 +200,12 @@ def tile_moe_res_glu_silu_kernel(
                 turned[:].rearrange("p g u r -> p g r u"),
             )
             nc.vector.quantize_mx(
-                out=hq[:].rearrange("p g r -> p (g r)").bitcast(FP8X4),
-                scales=hs[:].rearrange("p g r -> p (g r)"),
+                out=hq[j][:].rearrange("p g r -> p (g r)").bitcast(FP8X4),
+                scales=hs[j][:].rearrange("p g r -> p (g r)"),
                 in_=hq_in[:].rearrange("p g r t -> p (g r t)"),
             )
-            return hq, hs
 
-        def second_layer(j, hq, hs):
+        def second_layer(j):
             e = j * P // C
             y = psum.tile([P, NT, P], F32, name="y", tag="bank")
             for n in range(NT):
@@ -228,8 +214,8 @@ def tile_moe_res_glu_silu_kernel(
                         out=y[:, n, :],
                         lhsT=w2t[:, e, g, 2 * P * n : 2 * P * (n + 1)].bitcast(FP4X4),
                         lhsT_scale=w2sc[:, e, g, P * n : P * (n + 1)],
-                        rhs=hq[:, g, :].bitcast(FP8X4),
-                        rhs_scale=hs[:, g, :],
+                        rhs=hq[j][:, g, :].bitcast(FP8X4),
+                        rhs_scale=hs[j][:, g, :],
                         start=(g == 0),
                         stop=(g == G - 1),
                     )
@@ -244,27 +230,39 @@ def tile_moe_res_glu_silu_kernel(
         for c in range(T // QUANT):
             quantise_chunk(0, c)
         gather(0, 0, C)
-        first_layer(0, 0)
-        first_layer(1, 0)
         for c in range(T // QUANT):
             quantise_chunk(1, c)
+        for m in range(2):
+            for j in range(2):
+                for g in range(G):
+                    product(j, g, m, 0)
         gather(0, C, SLOTS)
-        gather(1, 0, P)
-        first_layer(0, 1)
-        gather(1, P, C)
-        first_layer(1, 1)
-        h, turned_h = {}, {}
-        h[0] = hidden(0)
+        for j in range(2):
+            gather(1, j * P, (j + 1) * P)
+            for g in range(G):
+                for m in range(2):
+                    product(j, g, m, 1)
+        hidden(0, 0)
+        hidden(0, 1)
         gather(1, C, SLOTS)
-        for t in range(1, UNITS + 2):
-            if t - 1 < UNITS:
-                turned_h[t - 1] = turn(h[t - 1])
-            if t >= 2:
-                second_layer(t - 2, *turned_h[t - 2])
-            if t < UNITS:
-                h[t] = hidden(t)
-            if 2 <= t + 1 < UNITS:
-                first_layer_whole(t + 1)
+        first_layer(2, 0)
+        turn(0)
+        hidden(1, 0)
+        hidden(1, 1)
+        first_layer(2, 1)
+        turn(1)
+        second_layer(0)
+        hidden(2, 0)
+        hidden(2, 1)
+        first_layer(3, 0)
+        first_layer(3, 1)
+        turn(2)
+        second_layer(1)
+        hidden(3, 0)
+        hidden(3, 1)
+        turn(3)
+        second_layer(2)
+        second_layer(3)
 
         for n in range(NT):
             done = keep.tile([P, T], F32, name=f"done{n}")

@@ -25,7 +25,7 @@ G = H // KP
 UNITS = SLOTS // P
 NT = N // P
 QUANT = 256
-VEC_TOKENS = ((160, 160, 160), (0, 0, 160))
+VEC_TOKENS = (512, 256, 0, 384)
 
 
 def tile_moe_res_glu_silu_kernel(
@@ -61,11 +61,8 @@ def tile_moe_res_glu_silu_kernel(
         warm = keep.tile([P, 1], F32, name="warm")
         nc.vector.memset(warm[:], 0.0)
         nc.scalar.activation(warm[:], warm[:], SILU)
-        codes, bytes_all, xq, xs = {}, {}, {}, {}
+        xq, xs = {}, {}
         for s in range(PASSES):
-            codes[s] = keep.tile([P, T], U32, name=f"codes{s}", align_bytes=64)
-            bytes_all[s] = keep.tile([P, T], U8, name=f"bytes{s}", align_bytes=64)
-            nc.vector.memset(bytes_all[s][:].bitcast(I32), 0)
             xq[s] = keep.tile([P, SLOTS], U32, name=f"xq{s}", align_bytes=64)
             xs[s] = keep.tile([P, SLOTS], U8, name=f"xs{s}", align_bytes=64)
         w2sc = keep.tile([P, E, PASSES, N], U8, name="w2sc", align_bytes=64)
@@ -77,13 +74,12 @@ def tile_moe_res_glu_silu_kernel(
         ident = keep.tile([P, P], F32, name="ident")
         make_identity(nc, ident[:])
 
-        xview = xT.rearrange("(s p j) w -> s p j w", s=PASSES, p=P)
+        xview = xT.rearrange("(s p u d) w -> s u p d w", s=PASSES, p=P, u=2)
         raw = {}
-        for s in range(PASSES):
-            raw[s] = keep.tile([P, 4, T], F32, name=f"raw{s}")
 
-        def load_x(s, j0, j1, c0, c1):
-            nc.sync.dma_start(raw[s][:, j0:j1, c0:c1], xview[s][:, j0:j1, c0:c1])
+        def load_x(s, u):
+            raw[s, u] = keep.tile([P, 2, T], F32, name=f"raw{s}{u}")
+            nc.sync.dma_start(raw[s, u][:], xview[s, u])
 
         wt = {}
 
@@ -98,14 +94,14 @@ def tile_moe_res_glu_silu_kernel(
                 for g in halves:
                     wt[e, m, s, g] = piece[:, s - passes[0], (g - halves[0]) * 2 * KP : (g - halves[0] + 1) * 2 * KP]
 
-        load_x(0, 0, 4, 0, 512)
+        load_x(0, 0)
         nc.sync.dma_start(offsets[:], offs)
-        load_x(0, 0, 4, 512, 768)
-        load_x(1, 0, 4, 0, 512)
+        load_x(0, 1)
+        load_x(1, 0)
         load_scales(0, 0, 0)
         load_scales(0, 0, 2)
         load_words(0, 0, (0,), (0, 1))
-        load_x(1, 0, 4, 512, 768)
+        load_x(1, 1)
         load_scales(0, 1, 0)
         load_scales(0, 1, 2)
         load_words(0, 1, (0,), (0, 1))
@@ -130,26 +126,49 @@ def tile_moe_res_glu_silu_kernel(
             res_in[n] = keep.tile([P, T], F32, name=f"res_in{n}")
             nc.sync.dma_start(res_in[n][:], xr[n * P : (n + 1) * P, :])
 
-        def quantise_chunk(s, b):
-            first = b * QUANT
-            grouped = keep.tile([P, QUANT, 4], BF16, name=f"grouped{s}{b}", align_bytes=64)
-            src = raw[s][:, :, first : first + QUANT].rearrange("p j (b i) -> p b j i", i=4)
-            dst = grouped[:].rearrange("p (b i) j -> p b j i", i=4)
-            v = VEC_TOKENS[s][b]
+        pairs = {}
+
+        def round_pairs(s, u):
+            pairs[s, u] = keep.tile([P, T, 2], BF16, name=f"pairs{s}{u}", align_bytes=64)
+            src = raw[s, u][:].rearrange("p d w -> p w d")
+            v = VEC_TOKENS[2 * s + u]
             if v:
-                nc.vector.tensor_copy(dst[:, 0 : v // 4], src[:, 0 : v // 4])
-            nc.scalar.copy(dst[:, v // 4 :], src[:, v // 4 :])
-            cols = slice(b * QUANT, (b + 1) * QUANT)
-            nc.vector.quantize_mx(
-                out=codes[s][:, cols].bitcast(FP8X4),
-                scales=bytes_all[s][:, cols],
-                in_=grouped[:].rearrange("p w j -> p (w j)"),
+                nc.vector.tensor_copy(pairs[s, u][:, 0:v, :], src[:, 0:v, :])
+            nc.scalar.copy(pairs[s, u][:, v:T, :], src[:, v:T, :])
+
+        grouped, plain = {}, {}
+        for s in range(PASSES):
+            plain[s] = keep.tile([P, 2 * C], U32, name=f"plain{s}", align_bytes=64)
+
+        def table(s, u):
+            return pairs[s, u][:].rearrange("p w d -> p (w d)").bitcast(U32)
+
+        def gather(s, u, first, last):
+            if (s, first) == (1, 0):
+                grouped[s, first] = plain[1][:, C : 2 * C]
+            elif u == 0:
+                own = keep.tile([P, 2 * (last - first)], U32, name=f"grouped{s}{first}", align_bytes=64)
+                grouped[s, first] = own[:]
+            nc.vector.tensor_copy(
+                grouped[s, first].rearrange("p (r u) -> p r u", u=2)[:, :, u],
+                table(s, u).indirect(offsets[:, first // 16 : last // 16]),
             )
 
-        def gather(s, first, last):
-            part = offsets[:, first // 16 : last // 16]
-            nc.vector.tensor_copy(xq[s][:, first:last], codes[s][:].indirect(part))
-            nc.vector.tensor_copy(xs[s][:, first:last], bytes_all[s][:].indirect(part))
+        def gather_plain(s, u):
+            nc.vector.tensor_copy(plain[s][:, u * C : (u + 1) * C], table(s, u).indirect(offsets[:, C // 16 : SLOTS // 16]))
+
+        def weave(s):
+            woven = keep.tile([P, 2 * C], U32, name=f"woven{s}", align_bytes=64)
+            grouped[s, C] = woven[:]
+            nc.scalar.copy(
+                woven[:].bitcast(F32).rearrange("p (r u) -> p r u", u=2),
+                plain[s][:].bitcast(F32).rearrange("p (u r) -> p r u", u=2),
+            )
+
+        def quantise(s, first, last):
+            nc.vector.quantize_mx(
+                out=xq[s][:, first:last].bitcast(FP8X4), scales=xs[s][:, first:last], in_=grouped[s, first].bitcast(BF16)
+            )
 
         acc, h, turned, hq, hs = {}, {}, {}, {}, {}
 
@@ -227,24 +246,36 @@ def tile_moe_res_glu_silu_kernel(
                     back[n][:].indirect(offsets[:, j * P // 16 : (j + 1) * P // 16]), y_sb[:, n, :], gates[:, cols], MULT
                 )
 
-        for c in range(T // QUANT):
-            quantise_chunk(0, c)
-        gather(0, 0, C)
-        for c in range(T // QUANT):
-            quantise_chunk(1, c)
+        round_pairs(0, 0)
+        gather(0, 0, 0, C)
+        round_pairs(0, 1)
+        gather(0, 1, 0, C)
+        quantise(0, 0, C)
+        round_pairs(1, 0)
+        gather(1, 0, 0, P)
+        gather(1, 0, P, C)
+        round_pairs(1, 1)
         for m in range(2):
             for j in range(2):
                 for g in range(G):
                     product(j, g, m, 0)
-        gather(0, C, SLOTS)
-        for j in range(2):
-            gather(1, j * P, (j + 1) * P)
-            for g in range(G):
-                for m in range(2):
-                    product(j, g, m, 1)
+        gather(1, 1, 0, P)
+        quantise(1, 0, P)
+        for g in range(G):
+            for m in range(2):
+                product(0, g, m, 1)
+        gather(1, 1, P, C)
+        quantise(1, P, C)
+        for g in range(G):
+            for m in range(2):
+                product(1, g, m, 1)
         hidden(0, 0)
         hidden(0, 1)
-        gather(1, C, SLOTS)
+        for s in range(PASSES):
+            for u in range(2):
+                gather_plain(s, u)
+            weave(s)
+            quantise(s, C, SLOTS)
         first_layer(2, 0)
         turn(0)
         hidden(1, 0)

@@ -25,7 +25,7 @@ G = H // KP
 UNITS = SLOTS // P
 NT = N // P
 QUANT = 256
-VEC_TOKENS = (512, 256, 0, 384)
+VEC_TOKENS = (512, 384, 256, 448)
 
 
 def tile_moe_res_glu_silu_kernel(
@@ -78,7 +78,7 @@ def tile_moe_res_glu_silu_kernel(
         raw = {}
 
         def load_x(s, u):
-            raw[s, u] = keep.tile([P, 2, T], F32, name=f"raw{s}{u}")
+            raw[s, u] = keep.tile([P, 2, T], F32, name=f"raw{s}{u}", align_bytes=64)
             nc.sync.dma_start(raw[s, u][:], xview[s, u])
 
         wt = {}
@@ -158,9 +158,10 @@ def tile_moe_res_glu_silu_kernel(
             nc.vector.tensor_copy(plain[s][:, u * C : (u + 1) * C], table(s, u).indirect(offsets[:, C // 16 : SLOTS // 16]))
 
         def weave(s):
-            woven = keep.tile([P, 2 * C], U32, name=f"woven{s}", align_bytes=64)
+            woven = keep.tile([P, 2 * C], U32, name=f"woven{s}", tag="raw11" if s == 0 else "woven", align_bytes=64)
             grouped[s, C] = woven[:]
-            nc.scalar.copy(
+            copy = nc.scalar.copy if s == 0 else nc.vector.tensor_copy
+            copy(
                 woven[:].bitcast(F32).rearrange("p (r u) -> p r u", u=2),
                 plain[s][:].bitcast(F32).rearrange("p (u r) -> p r u", u=2),
             )

@@ -197,10 +197,14 @@ def tile_moe_res_glu_silu_kernel(
             if g == 0:
                 h[j] = ring.tile([P, G, 2, P, 2], BF16, name="h", align_bytes=64)
             act = ring.tile([P, KP], F32, name="act", bufs=3)
-            nc.scalar.activation(act[:], acc[j, g, 0][:], SILU)
+            nc.scalar.activation(
+                act[:].rearrange("r (u p e) -> r u p e", u=2, e=2),
+                acc[j, g, 0][:].rearrange("r (p u e) -> r u p e", u=2, e=2),
+                SILU,
+            )
             nc.vector.tensor_tensor(
                 h[j][:, g, :, :, :],
-                act[:].rearrange("r (p u e) -> r u p e", u=2, e=2),
+                act[:].rearrange("r (u p e) -> r u p e", u=2, e=2),
                 acc[j, g, 1][:].rearrange("r (p u e) -> r u p e", u=2, e=2),
                 MULT,
             )

@@ -48,15 +48,23 @@ def tile_moe_res_glu_silu_kernel(
                 engine = nc.gpsimd if m == 0 else nc.vector
                 engine.memset(wsc[e, m][:].rearrange("p s i -> p (s i)").bitcast(I32), 0)
 
-        def load_scales(e, m, first):
+        def load_scales(e, m, first, last, passes=(0, 1), halves=(0, 1)):
             rows = scales[m][e].rearrange("s (q r) i -> r q s i", r=4)
-            for r in (first, first + 1):
-                nc.sync.dma_start(wsc[e, m][r:P:32].bitcast(I32), rows[r].bitcast(I32))
+            s0, s1, i0, i1 = passes[0], passes[-1] + 1, halves[0] * KP, (halves[-1] + 1) * KP
+            for r in range(first, last):
+                nc.sync.dma_start(wsc[e, m][r:P:32, s0:s1, i0:i1].bitcast(I32), rows[r][:, s0:s1, i0:i1].bitcast(I32))
 
-        def load_w2_scales(first):
-            rows = w2_scales.rearrange("e s (q r) n -> r q (e s) n", r=4)
-            for r in (first, first + 1):
-                nc.sync.dma_start(w2sc[r:P:32].rearrange("p e s n -> p (e s) n").bitcast(I32), rows[r].bitcast(I32))
+        def load_w2_scales(e0, e1):
+            rows = w2_scales[e0:e1].rearrange("e s (q r) n -> r q (e s) n", r=4)
+            for r in range(4):
+                plane = w2sc[r:P:32, e0:e1].rearrange("p e s n -> p (e s) n")
+                nc.sync.dma_start(plane.bitcast(I32), rows[r].bitcast(I32))
+
+        w2t = {}
+
+        def load_w2(e):
+            w2t[e] = keep.tile([P, PASSES, 2 * N], U8, name=f"w2t{e}", align_bytes=64)
+            nc.sync.dma_start(w2t[e][:].bitcast(I32), w2_words[e].rearrange("s p b -> p s b").bitcast(I32))
 
         warm = keep.tile([P, 1], F32, name="warm")
         nc.vector.memset(warm[:], 0.0)
@@ -96,31 +104,38 @@ def tile_moe_res_glu_silu_kernel(
 
         load_x(0, 0)
         nc.sync.dma_start(offsets[:], offs)
+        load_scales(0, 0, 0, 1)
         load_x(0, 1)
+        load_scales(0, 0, 1, 2)
+        load_scales(0, 0, 2, 3)
         load_x(1, 0)
-        load_scales(0, 0, 0)
-        load_scales(0, 0, 2)
+        load_scales(0, 0, 3, 4)
+        load_scales(0, 1, 0, 1)
         load_words(0, 0, (0,), (0, 1))
+        load_scales(0, 1, 1, 2)
         load_x(1, 1)
-        load_scales(0, 1, 0)
-        load_scales(0, 1, 2)
+        load_scales(0, 1, 2, 3)
+        load_scales(0, 1, 3, 4)
         load_words(0, 1, (0,), (0, 1))
+        load_scales(1, 0, 0, 1)
         load_words(0, 0, (1,), (0, 1))
+        load_scales(1, 0, 1, 2)
         load_words(0, 1, (1,), (0, 1))
-        load_scales(1, 0, 0)
-        load_scales(1, 0, 2)
+        load_scales(1, 0, 2, 3)
+        load_scales(1, 0, 3, 4)
+        load_scales(1, 1, 0, 1)
         load_words(1, 0, (0, 1), (0,))
-        load_scales(1, 1, 0)
-        load_scales(1, 1, 2)
+        load_scales(1, 1, 1, 2)
+        load_scales(1, 1, 2, 3)
+        load_scales(1, 1, 3, 4)
         load_words(1, 1, (0, 1), (0,))
         load_words(1, 0, (0, 1), (1,))
         load_words(1, 1, (0, 1), (1,))
-        w2t = keep.tile([P, E, PASSES, 2 * N], U8, name="w2t", align_bytes=64)
-        nc.sync.dma_start(w2t[:].bitcast(I32), w2_words.rearrange("e s p b -> p e s b").bitcast(I32))
-        load_w2_scales(0)
-        load_w2_scales(2)
+        load_w2(0)
+        load_w2_scales(0, 2)
         gates = keep.tile([P, SLOTS], F32, name="gates")
         nc.sync.dma_start(gates[:], gate[0:P, :])
+        load_w2(1)
         res_in = {}
         for n in range(NT):
             res_in[n] = keep.tile([P, T], F32, name=f"res_in{n}")
@@ -236,7 +251,7 @@ def tile_moe_res_glu_silu_kernel(
                 for g in range(G):
                     nc.tensor.matmul_mx(
                         out=y[:, n, :],
-                        lhsT=w2t[:, e, g, 2 * P * n : 2 * P * (n + 1)].bitcast(FP4X4),
+                        lhsT=w2t[e][:, g, 2 * P * n : 2 * P * (n + 1)].bitcast(FP4X4),
                         lhsT_scale=w2sc[:, e, g, P * n : P * (n + 1)],
                         rhs=hq[j][:, g, :].bitcast(FP8X4),
                         rhs_scale=hs[j][:, g, :],

@@ -104,30 +104,18 @@ def tile_moe_res_glu_silu_kernel(
 
         load_x(0, 0)
         nc.sync.dma_start(offsets[:], offs)
-        load_scales(0, 0, 0, 1)
         load_x(0, 1)
-        load_scales(0, 0, 1, 2)
-        load_scales(0, 0, 2, 3)
         load_x(1, 0)
-        load_scales(0, 0, 3, 4)
-        load_scales(0, 1, 0, 1)
+        load_scales(0, 0, 0, 4)
         load_words(0, 0, (0,), (0, 1))
-        load_scales(0, 1, 1, 2)
         load_x(1, 1)
-        load_scales(0, 1, 2, 3)
-        load_scales(0, 1, 3, 4)
+        load_scales(0, 1, 0, 4)
         load_words(0, 1, (0,), (0, 1))
-        load_scales(1, 0, 0, 1)
         load_words(0, 0, (1,), (0, 1))
-        load_scales(1, 0, 1, 2)
         load_words(0, 1, (1,), (0, 1))
-        load_scales(1, 0, 2, 3)
-        load_scales(1, 0, 3, 4)
-        load_scales(1, 1, 0, 1)
+        load_scales(1, 0, 0, 4)
         load_words(1, 0, (0, 1), (0,))
-        load_scales(1, 1, 1, 2)
-        load_scales(1, 1, 2, 3)
-        load_scales(1, 1, 3, 4)
+        load_scales(1, 1, 0, 4)
         load_words(1, 1, (0, 1), (0,))
         load_words(1, 0, (0, 1), (1,))
         load_words(1, 1, (0, 1), (1,))
@@ -151,17 +139,14 @@ def tile_moe_res_glu_silu_kernel(
                 nc.vector.tensor_copy(pairs[s, u][:, 0:v, :], src[:, 0:v, :])
             nc.scalar.copy(pairs[s, u][:, v:T, :], src[:, v:T, :])
 
-        grouped, plain = {}, {}
-        for s in range(PASSES):
-            plain[s] = keep.tile([P, 2 * C], U32, name=f"plain{s}", align_bytes=64)
+        grouped, acts = {}, {}
+        plain = keep.tile([P, 2 * C], U32, name="plain", align_bytes=64)
 
         def table(s, u):
             return pairs[s, u][:].rearrange("p w d -> p (w d)").bitcast(U32)
 
         def gather(s, u, first, last):
-            if (s, first) == (1, 0):
-                grouped[s, first] = plain[1][:, C : 2 * C]
-            elif u == 0:
+            if u == 0:
                 own = keep.tile([P, 2 * (last - first)], U32, name=f"grouped{s}{first}", align_bytes=64)
                 grouped[s, first] = own[:]
             nc.vector.tensor_copy(
@@ -169,16 +154,17 @@ def tile_moe_res_glu_silu_kernel(
                 table(s, u).indirect(offsets[:, first // 16 : last // 16]),
             )
 
-        def gather_plain(s, u):
-            nc.vector.tensor_copy(plain[s][:, u * C : (u + 1) * C], table(s, u).indirect(offsets[:, C // 16 : SLOTS // 16]))
+        def gather_plain(tile, s, u, first):
+            width = SLOTS - first
+            nc.vector.tensor_copy(tile[:, u * width : (u + 1) * width], table(s, u).indirect(offsets[:, first // 16 :]))
 
-        def weave(s):
-            woven = keep.tile([P, 2 * C], U32, name=f"woven{s}", tag="raw11" if s == 0 else "woven", align_bytes=64)
-            grouped[s, C] = woven[:]
-            copy = nc.scalar.copy if s == 0 else nc.vector.tensor_copy
+        def weave(copy, tile, s, first, tag):
+            width = SLOTS - first
+            woven = keep.tile([P, 2 * width], U32, name="woven", tag=tag, align_bytes=64)
+            grouped[s, first] = woven[:]
             copy(
                 woven[:].bitcast(F32).rearrange("p (r u) -> p r u", u=2),
-                plain[s][:].bitcast(F32).rearrange("p (u r) -> p r u", u=2),
+                tile[:, 0 : 2 * width].bitcast(F32).rearrange("p (u r) -> p r u", u=2),
             )
 
         def quantise(s, first, last):
@@ -203,14 +189,14 @@ def tile_moe_res_glu_silu_kernel(
                 stop=(s == PASSES - 1),
             )
 
-        def first_layer(j, g):
-            for m in range(2):
+        def first_layer(j, g, matrices=(0, 1)):
+            for m in matrices:
                 for s in range(PASSES):
                     product(j, g, m, s)
 
         def hidden(j, g):
             if g == 0:
-                h[j] = ring.tile([P, G, 2, P, 2], BF16, name="h", align_bytes=64)
+                h[j] = ring.tile([P, G, 2, P, 2], BF16, name="h", align_bytes=64, bufs=3)
             act = ring.tile([P, KP], F32, name="act", bufs=3)
             nc.scalar.activation(
                 act[:].rearrange("r (u p e) -> r u p e", u=2, e=2),
@@ -224,33 +210,35 @@ def tile_moe_res_glu_silu_kernel(
                 MULT,
             )
 
-        def turn(j):
-            turned = psum.tile([P, G, 2, P], F32, name="turned", tag="bank")
-            hq_in = ring.tile([P, G, P, 4], BF16, name="hq_in", align_bytes=64)
-            hq[j] = ring.tile([P, G, P], U32, name="hq", align_bytes=64)
-            hs[j] = ring.tile([P, G, P], U8, name="hs", align_bytes=64)
+        def turn(j, halves):
+            count, g0 = len(halves), halves[0]
+            turned = psum.tile([P, count, 2, P], F32, name="turned", tag="bank")
+            hq_in = ring.tile([P, count, P, 4], BF16, name="hq_in", align_bytes=64, bufs=3)
+            if g0 == 0:
+                hq[j] = ring.tile([P, G, P], U32, name="hq", align_bytes=64, bufs=3)
+                hs[j] = ring.tile([P, G, P], U8, name="hs", align_bytes=64, bufs=3)
             hw = h[j][:].rearrange("r g u p e -> r (g u p e)").bitcast(F32)
-            for g in range(G):
+            for g in halves:
                 for u in range(2):
                     w0 = (2 * g + u) * P
-                    nc.tensor.transpose(turned[:, g, u, :], hw[:, w0 : w0 + P], ident[:])
+                    nc.tensor.transpose(turned[:, g - g0, u, :], hw[:, w0 : w0 + P], ident[:])
             nc.scalar.copy(
-                hq_in[:].rearrange("p g r t -> p (g r t)").bitcast(F32).rearrange("p (g r u) -> p g r u", g=G, u=2),
+                hq_in[:].rearrange("p g r t -> p (g r t)").bitcast(F32).rearrange("p (g r u) -> p g r u", g=count, u=2),
                 turned[:].rearrange("p g u r -> p g r u"),
             )
             nc.vector.quantize_mx(
-                out=hq[j][:].rearrange("p g r -> p (g r)").bitcast(FP8X4),
-                scales=hs[j][:].rearrange("p g r -> p (g r)"),
+                out=hq[j][:, g0 : g0 + count, :].rearrange("p g r -> p (g r)").bitcast(FP8X4),
+                scales=hs[j][:, g0 : g0 + count, :].rearrange("p g r -> p (g r)"),
                 in_=hq_in[:].rearrange("p g r t -> p (g r t)"),
             )
 
-        def second_layer(j):
+        def second_layer(j, tiles):
             e = j * P // C
-            y = psum.tile([P, NT, P], F32, name="y", tag="bank")
-            for n in range(NT):
+            y = psum.tile([P, len(tiles), P], F32, name="y", tag="bank")
+            for i, n in enumerate(tiles):
                 for g in range(G):
                     nc.tensor.matmul_mx(
-                        out=y[:, n, :],
+                        out=y[:, i, :],
                         lhsT=w2t[e][:, g, 2 * P * n : 2 * P * (n + 1)].bitcast(FP4X4),
                         lhsT_scale=w2sc[:, e, g, P * n : P * (n + 1)],
                         rhs=hq[j][:, g, :].bitcast(FP8X4),
@@ -258,12 +246,12 @@ def tile_moe_res_glu_silu_kernel(
                         start=(g == 0),
                         stop=(g == G - 1),
                     )
-            y_sb = keep.tile([P, NT, P], F32, name=f"ys{j}")
+            y_sb = keep.tile([P, len(tiles), P], F32, name=f"ys{j}{tiles[0]}")
             nc.scalar.copy(y_sb[:], y[:])
             cols = slice(j * P, (j + 1) * P)
-            for n in range(NT):
+            for i, n in enumerate(tiles):
                 nc.vector.tensor_tensor(
-                    back[n][:].indirect(offsets[:, j * P // 16 : (j + 1) * P // 16]), y_sb[:, n, :], gates[:, cols], MULT
+                    back[n][:].indirect(offsets[:, j * P // 16 : (j + 1) * P // 16]), y_sb[:, i, :], gates[:, cols], MULT
                 )
 
         round_pairs(0, 0)
@@ -274,6 +262,7 @@ def tile_moe_res_glu_silu_kernel(
         round_pairs(1, 0)
         gather(1, 0, 0, P)
         gather(1, 0, P, C)
+        gather(1, 0, C, SLOTS)
         round_pairs(1, 1)
         for m in range(2):
             for j in range(2):
@@ -289,31 +278,36 @@ def tile_moe_res_glu_silu_kernel(
         for g in range(G):
             for m in range(2):
                 product(1, g, m, 1)
+        gather_plain(plain, 0, 0, C)
+        gather_plain(plain, 0, 1, C)
+        weave(nc.scalar.copy, plain, 0, C, "raw11")
+        quantise(0, C, SLOTS)
+        gather(1, 1, C, SLOTS)
+        quantise(1, C, SLOTS)
         hidden(0, 0)
         hidden(0, 1)
-        for s in range(PASSES):
-            for u in range(2):
-                gather_plain(s, u)
-            weave(s)
-            quantise(s, C, SLOTS)
-        first_layer(2, 0)
-        turn(0)
+        first_layer(2, 0, (0,))
+        turn(0, (0, 1))
         hidden(1, 0)
         hidden(1, 1)
+        first_layer(2, 0, (1,))
         first_layer(2, 1)
-        turn(1)
-        second_layer(0)
+        turn(1, (0, 1))
+        second_layer(0, (0, 1))
         hidden(2, 0)
         hidden(2, 1)
         first_layer(3, 0)
-        first_layer(3, 1)
-        turn(2)
-        second_layer(1)
+        first_layer(3, 1, (0,))
+        turn(2, (0, 1))
+        first_layer(3, 1, (1,))
+        second_layer(1, (0, 1))
         hidden(3, 0)
+        turn(3, (0,))
         hidden(3, 1)
-        turn(3)
-        second_layer(2)
-        second_layer(3)
+        turn(3, (1,))
+        second_layer(2, (0, 1))
+        second_layer(3, (0,))
+        second_layer(3, (1,))
 
         for n in range(NT):
             done = keep.tile([P, T], F32, name=f"done{n}")

@@ -71,8 +71,8 @@ def tile_moe_res_glu_silu_kernel(
         nc.scalar.activation(warm[:], warm[:], SILU)
         xq, xs = {}, {}
         for s in range(PASSES):
-            xq[s] = keep.tile([P, SLOTS], U32, name=f"xq{s}", align_bytes=64)
-            xs[s] = keep.tile([P, SLOTS], U8, name=f"xs{s}", align_bytes=64)
+            for e in range(E):
+                xs[s, e] = keep.tile([P, C], U8, name=f"xs{s}{e}", align_bytes=64)
         w2sc = keep.tile([P, E, PASSES, N], U8, name="w2sc", align_bytes=64)
         nc.vector.memset(w2sc[:].rearrange("p e s n -> p (e s n)").bitcast(I32), 0)
         back = {}
@@ -168,21 +168,25 @@ def tile_moe_res_glu_silu_kernel(
             )
 
         def quantise(s, first, last):
+            e, cols = first // C, slice(first % C, (last - 1) % C + 1)
+            if first % C == 0:
+                tag = "raw11" if (s, e) == (0, 1) else f"xq{s}{e}"
+                xq[s, e] = keep.tile([P, C], U32, name="xq", tag=tag, align_bytes=64)
             nc.vector.quantize_mx(
-                out=xq[s][:, first:last].bitcast(FP8X4), scales=xs[s][:, first:last], in_=grouped[s, first].bitcast(BF16)
+                out=xq[s, e][:, cols].bitcast(FP8X4), scales=xs[s, e][:, cols], in_=grouped[s, first].bitcast(BF16)
             )
 
         acc, h, turned, hq, hs = {}, {}, {}, {}, {}
 
         def product(j, g, m, s):
             e = j * P // C
-            cols = slice(j * P, (j + 1) * P)
+            cols = slice(j * P % C, j * P % C + P)
             if s == 0:
                 acc[j, g, m] = psum.tile([P, KP], F32, name="acc", tag="bank")
             nc.tensor.matmul_mx(
                 out=acc[j, g, m][:],
-                lhsT=xq[s][:, cols].bitcast(FP8X4),
-                lhsT_scale=xs[s][:, cols],
+                lhsT=xq[s, e][:, cols].bitcast(FP8X4),
+                lhsT_scale=xs[s, e][:, cols],
                 rhs=wt[e, m, s, g].bitcast(FP4X4),
                 rhs_scale=wsc[e, m][:, s, g * KP : (g + 1) * KP],
                 start=(s == 0),
@@ -262,14 +266,18 @@ def tile_moe_res_glu_silu_kernel(
         round_pairs(1, 0)
         gather(1, 0, 0, P)
         gather(1, 0, P, C)
-        gather(1, 0, C, SLOTS)
         round_pairs(1, 1)
+        gather_plain(plain, 0, 0, C)
+        gather_plain(plain, 0, 1, C)
+        weave(nc.scalar.copy, plain, 0, C, "raw10")
+        gather(1, 0, C, SLOTS)
         for m in range(2):
             for j in range(2):
                 for g in range(G):
                     product(j, g, m, 0)
         gather(1, 1, 0, P)
         quantise(1, 0, P)
+        quantise(0, C, SLOTS)
         for g in range(G):
             for m in range(2):
                 product(0, g, m, 1)
@@ -278,10 +286,6 @@ def tile_moe_res_glu_silu_kernel(
         for g in range(G):
             for m in range(2):
                 product(1, g, m, 1)
-        gather_plain(plain, 0, 0, C)
-        gather_plain(plain, 0, 1, C)
-        weave(nc.scalar.copy, plain, 0, C, "raw11")
-        quantise(0, C, SLOTS)
         gather(1, 1, C, SLOTS)
         quantise(1, C, SLOTS)
         hidden(0, 0)
@@ -291,8 +295,8 @@ def tile_moe_res_glu_silu_kernel(
         hidden(1, 0)
         hidden(1, 1)
         first_layer(2, 0, (1,))
-        first_layer(2, 1)
         turn(1, (0, 1))
+        first_layer(2, 1)
         second_layer(0, (0, 1))
         hidden(2, 0)
         hidden(2, 1)

@@ -24,6 +24,7 @@ PASSES = K // KP
 G = H // KP
 UNITS = SLOTS // P
 NT = N // P
+STORES = (((0, 128), (128, 384), (384, T)), ((0, 512), (512, T)))
 QUANT = 256
 VEC_TOKENS = (512, 384, 256, 448)
 
@@ -315,6 +316,7 @@ def tile_moe_res_glu_silu_kernel(
 
         for n in range(NT):
             done = keep.tile([P, T], F32, name=f"done{n}")
-            for cols in (slice(0, 512), slice(512, T)):
+            for first, last in STORES[n]:
+                cols = slice(first, last)
                 nc.vector.tensor_tensor(done[:, cols], back[n][:, cols], res_in[n][:, cols], ADD)
                 nc.sync.dma_start(out[n * P : (n + 1) * P, cols], done[:, cols])

@@ -26,7 +26,8 @@ UNITS = SLOTS // P
 NT = N // P
 STORES = (((0, 128), (128, 384), (384, T)), ((0, 512), (512, T)))
 QUANT = 256
-VEC_TOKENS = (512, 384, 256, 448)
+CUTS = (T, T, T, 384)
+VEC_TOKENS = (512, 384, 256, 256)
 
 
 def tile_moe_res_glu_silu_kernel(
@@ -86,9 +87,10 @@ def tile_moe_res_glu_silu_kernel(
         xview = xT.rearrange("(s p u d) w -> s u p d w", s=PASSES, p=P, u=2)
         raw = {}
 
-        def load_x(s, u):
-            raw[s, u] = keep.tile([P, 2, T], F32, name=f"raw{s}{u}", align_bytes=64)
-            nc.sync.dma_start(raw[s, u][:], xview[s, u])
+        def load_x(s, u, first=0, last=T):
+            if first == 0:
+                raw[s, u] = keep.tile([P, 2, T], F32, name=f"raw{s}{u}", align_bytes=64)
+            nc.sync.dma_start(raw[s, u][:, :, first:last], xview[s, u][:, :, first:last])
 
         wt = {}
 
@@ -109,7 +111,8 @@ def tile_moe_res_glu_silu_kernel(
         load_x(1, 0)
         load_scales(0, 0, 0, 4)
         load_words(0, 0, (0,), (0, 1))
-        load_x(1, 1)
+        load_x(1, 1, 0, CUTS[3])
+        load_x(1, 1, CUTS[3], T)
         load_scales(0, 1, 0, 4)
         load_words(0, 1, (0,), (0, 1))
         load_words(0, 0, (1,), (0, 1))
@@ -135,10 +138,12 @@ def tile_moe_res_glu_silu_kernel(
         def round_pairs(s, u):
             pairs[s, u] = keep.tile([P, T, 2], BF16, name=f"pairs{s}{u}", align_bytes=64)
             src = raw[s, u][:].rearrange("p d w -> p w d")
-            v = VEC_TOKENS[2 * s + u]
-            if v:
-                nc.vector.tensor_copy(pairs[s, u][:, 0:v, :], src[:, 0:v, :])
-            nc.scalar.copy(pairs[s, u][:, v:T, :], src[:, v:T, :])
+            cut, v = CUTS[2 * s + u], T - VEC_TOKENS[2 * s + u]
+            for first, last in ((0, min(cut, v)), (cut, v)):
+                if first < last:
+                    nc.scalar.copy(pairs[s, u][:, first:last, :], src[:, first:last, :])
+            if v < T:
+                nc.vector.tensor_copy(pairs[s, u][:, v:T, :], src[:, v:T, :])
 
         grouped, acts = {}, {}
         plain = keep.tile([P, 2 * C], U32, name="plain", align_bytes=64)

@@ -147,6 +147,7 @@ def tile_moe_res_glu_silu_kernel(
 
         grouped, acts = {}, {}
         plain = keep.tile([P, 2 * C], U32, name="plain", align_bytes=64)
+        rest = keep.tile([P, 2 * (SLOTS - P)], U32, name="rest", align_bytes=64)
 
         def table(s, u):
             return pairs[s, u][:].rearrange("p w d -> p (w d)").bitcast(U32)
@@ -164,19 +165,18 @@ def tile_moe_res_glu_silu_kernel(
             width = SLOTS - first
             nc.vector.tensor_copy(tile[:, u * width : (u + 1) * width], table(s, u).indirect(offsets[:, first // 16 :]))
 
-        def weave(copy, tile, s, first, tag):
-            width = SLOTS - first
-            woven = keep.tile([P, 2 * width], U32, name="woven", tag=tag, align_bytes=64)
+        def weave(tile, start, s, first, last, tag):
+            woven = keep.tile([P, 2 * (last - first)], U32, name="woven", tag=tag, align_bytes=64)
             grouped[s, first] = woven[:]
-            copy(
+            nc.scalar.copy(
                 woven[:].bitcast(F32).rearrange("p (r u) -> p r u", u=2),
-                tile[:, 0 : 2 * width].bitcast(F32).rearrange("p (u r) -> p r u", u=2),
+                tile[:].bitcast(F32).rearrange("p (u r) -> p r u", u=2)[:, first - start : last - start, :],
             )
 
         def quantise(s, first, last):
             e, cols = first // C, slice(first % C, (last - 1) % C + 1)
             if first % C == 0:
-                tag = "raw11" if (s, e) == (0, 1) else f"xq{s}{e}"
+                tag = f"xq{s}{e}"
                 xq[s, e] = keep.tile([P, C], U32, name="xq", tag=tag, align_bytes=64)
             nc.vector.quantize_mx(
                 out=xq[s, e][:, cols].bitcast(FP8X4), scales=xs[s, e][:, cols], in_=grouped[s, first].bitcast(BF16)
@@ -271,28 +271,28 @@ def tile_moe_res_glu_silu_kernel(
         quantise(0, 0, C)
         round_pairs(1, 0)
         gather(1, 0, 0, P)
-        gather(1, 0, P, C)
         round_pairs(1, 1)
         gather_plain(plain, 0, 0, C)
         gather_plain(plain, 0, 1, C)
-        weave(nc.scalar.copy, plain, 0, C, "raw10")
-        gather(1, 0, C, SLOTS)
+        weave(plain, C, 0, C, SLOTS, "raw10")
+        gather_plain(rest, 1, 0, P)
         for m in range(2):
             for j in range(2):
                 for g in range(G):
                     product(j, g, m, 0)
         gather(1, 1, 0, P)
+        gather_plain(rest, 1, 1, P)
         quantise(1, 0, P)
         quantise(0, C, SLOTS)
         for g in range(G):
             for m in range(2):
                 product(0, g, m, 1)
-        gather(1, 1, P, C)
+        weave(rest, P, 1, P, C, "woven1")
         quantise(1, P, C)
         for g in range(G):
             for m in range(2):
                 product(1, g, m, 1)
-        gather(1, 1, C, SLOTS)
+        weave(rest, P, 1, C, SLOTS, "woven2")
         quantise(1, C, SLOTS)
         hidden(0, 0)
         hidden(0, 1)

@@ -147,13 +147,16 @@ def tile_moe_res_glu_silu_kernel(
 
         grouped, acts = {}, {}
         plain = keep.tile([P, 2 * C], U32, name="plain", align_bytes=64)
-        rest = keep.tile([P, 2 * (SLOTS - P)], U32, name="rest", align_bytes=64)
+        rest = keep.tile([P, 2 * P], U32, name="rest", align_bytes=64)
+        held = keep.tile([P, 2 * C], U32, name="held", align_bytes=64)
 
         def table(s, u):
             return pairs[s, u][:].rearrange("p w d -> p (w d)").bitcast(U32)
 
         def gather(s, u, first, last):
-            if u == 0:
+            if u == 0 and s == 1:
+                grouped[s, first] = held[:, C : 2 * C]
+            elif u == 0:
                 own = keep.tile([P, 2 * (last - first)], U32, name=f"grouped{s}{first}", align_bytes=64)
                 grouped[s, first] = own[:]
             nc.vector.tensor_copy(
@@ -161,14 +164,16 @@ def tile_moe_res_glu_silu_kernel(
                 table(s, u).indirect(offsets[:, first // 16 : last // 16]),
             )
 
-        def gather_plain(tile, s, u, first):
-            width = SLOTS - first
-            nc.vector.tensor_copy(tile[:, u * width : (u + 1) * width], table(s, u).indirect(offsets[:, first // 16 :]))
+        def gather_plain(tile, s, u, first, last=SLOTS):
+            width = last - first
+            nc.vector.tensor_copy(
+                tile[:, u * width : (u + 1) * width], table(s, u).indirect(offsets[:, first // 16 : last // 16])
+            )
 
-        def weave(tile, start, s, first, last, tag):
+        def weave(tile, start, s, first, last, tag, copy=nc.scalar.copy):
             woven = keep.tile([P, 2 * (last - first)], U32, name="woven", tag=tag, align_bytes=64)
             grouped[s, first] = woven[:]
-            nc.scalar.copy(
+            copy(
                 woven[:].bitcast(F32).rearrange("p (r u) -> p r u", u=2),
                 tile[:].bitcast(F32).rearrange("p (u r) -> p r u", u=2)[:, first - start : last - start, :],
             )
@@ -275,14 +280,16 @@ def tile_moe_res_glu_silu_kernel(
         gather_plain(plain, 0, 0, C)
         gather_plain(plain, 0, 1, C)
         weave(plain, C, 0, C, SLOTS, "raw10")
-        gather_plain(rest, 1, 0, P)
+        gather_plain(rest, 1, 0, P, C)
+        gather_plain(held, 1, 0, C)
         for m in range(2):
             for j in range(2):
                 for g in range(G):
                     product(j, g, m, 0)
         gather(1, 1, 0, P)
-        gather_plain(rest, 1, 1, P)
+        gather_plain(rest, 1, 1, P, C)
         quantise(1, 0, P)
+        gather_plain(held, 1, 1, C)
         quantise(0, C, SLOTS)
         for g in range(G):
             for m in range(2):
@@ -292,7 +299,7 @@ def tile_moe_res_glu_silu_kernel(
         for g in range(G):
             for m in range(2):
                 product(1, g, m, 1)
-        weave(rest, P, 1, C, SLOTS, "woven2")
+        weave(held, C, 1, C, SLOTS, "woven2", nc.vector.tensor_copy)
         quantise(1, C, SLOTS)
         hidden(0, 0)
         hidden(0, 1)

@@ -291,13 +291,13 @@ def tile_moe_res_glu_silu_kernel(
         quantise(1, 0, P)
         gather_plain(held, 1, 1, C)
         quantise(0, C, SLOTS)
-        for g in range(G):
-            for m in range(2):
+        for m in range(2):
+            for g in range(G):
                 product(0, g, m, 1)
         weave(rest, P, 1, P, C, "woven1")
         quantise(1, P, C)
-        for g in range(G):
-            for m in range(2):
+        for m in range(2):
+            for g in range(G):
                 product(1, g, m, 1)
         weave(held, C, 1, C, SLOTS, "woven2", nc.vector.tensor_copy)
         quantise(1, C, SLOTS)

@@ -150,6 +150,8 @@ def tile_moe_res_glu_silu_kernel(
         rest = keep.tile([P, 2 * P], U32, name="rest", align_bytes=64)
         held = keep.tile([P, 2 * C], U32, name="held", align_bytes=64)
 
+        late = keep.tile([P, KP], F32, name="late", align_bytes=64)
+
         def table(s, u):
             return pairs[s, u][:].rearrange("p w d -> p (w d)").bitcast(U32)
 
@@ -171,10 +173,13 @@ def tile_moe_res_glu_silu_kernel(
             )
 
         def weave(tile, start, s, first, last, tag, copy=nc.scalar.copy):
-            woven = keep.tile([P, 2 * (last - first)], U32, name="woven", tag=tag, align_bytes=64)
-            grouped[s, first] = woven[:]
+            if tag is None:
+                woven = late[:, 0 : 2 * P].bitcast(U32)
+            else:
+                woven = keep.tile([P, 2 * (last - first)], U32, name="woven", tag=tag, align_bytes=64)[:]
+            grouped[s, first] = woven
             copy(
-                woven[:].bitcast(F32).rearrange("p (r u) -> p r u", u=2),
+                woven.bitcast(F32).rearrange("p (r u) -> p r u", u=2),
                 tile[:].bitcast(F32).rearrange("p (u r) -> p r u", u=2)[:, first - start : last - start, :],
             )
 
@@ -212,7 +217,7 @@ def tile_moe_res_glu_silu_kernel(
         def hidden(j, g):
             if g == 0:
                 h[j] = ring.tile([P, G, 2, P, 2], BF16, name="h", align_bytes=64, bufs=3)
-            act = ring.tile([P, KP], F32, name="act", bufs=3)
+            act = late if (j, g) == (1, 1) else ring.tile([P, KP], F32, name="act", bufs=3)
             nc.scalar.activation(
                 act[:].rearrange("r (u p e) -> r u p e", u=2, e=2),
                 acc[j, g, 0][:].rearrange("r (p u e) -> r u p e", u=2, e=2),
@@ -299,14 +304,16 @@ def tile_moe_res_glu_silu_kernel(
         for m in range(2):
             for g in range(G):
                 product(1, g, m, 1)
-        weave(held, C, 1, C, SLOTS, "woven2", nc.vector.tensor_copy)
-        quantise(1, C, SLOTS)
+        weave(held, C, 1, C, C + P, "woven2", nc.vector.tensor_copy)
+        quantise(1, C, C + P)
         hidden(0, 0)
         hidden(0, 1)
         first_layer(2, 0, (0,))
         turn(0, (0, 1))
         hidden(1, 0)
         hidden(1, 1)
+        weave(held, C, 1, C + P, SLOTS, None, nc.vector.tensor_copy)
+        quantise(1, C + P, SLOTS)
         first_layer(2, 0, (1,))
         turn(1, (0, 1))
         first_layer(2, 1)

@@ -59,7 +59,7 @@ def tile_moe_res_glu_silu_kernel(
         def load_w2_scales(e0, e1):
             rows = w2_scales[e0:e1].rearrange("e s (q r) n -> r q (e s) n", r=4)
             for r in range(4):
-                plane = w2sc[r:P:32, e0:e1].rearrange("p e s n -> p (e s) n")
+                plane = w2sc[e0][r:P:32]
                 nc.sync.dma_start(plane.bitcast(I32), rows[r].bitcast(I32))
 
         w2t = {}
@@ -75,8 +75,10 @@ def tile_moe_res_glu_silu_kernel(
         for s in range(PASSES):
             for e in range(E):
                 xs[s, e] = keep.tile([P, C], U8, name=f"xs{s}{e}", align_bytes=64)
-        w2sc = keep.tile([P, E, PASSES, N], U8, name="w2sc", align_bytes=64)
-        nc.vector.memset(w2sc[:].rearrange("p e s n -> p (e s n)").bitcast(I32), 0)
+        w2sc = {}
+        for e in range(E):
+            w2sc[e] = keep.tile([P, PASSES, N], U8, name=f"w2sc{e}", align_bytes=64)
+            nc.vector.memset(w2sc[e][:].rearrange("p s n -> p (s n)").bitcast(I32), 0)
         back = {}
         for n in range(NT):
             back[n] = keep.tile([P, T], F32, name=f"back{n}")
@@ -124,10 +126,11 @@ def tile_moe_res_glu_silu_kernel(
         load_words(1, 0, (0, 1), (1,))
         load_words(1, 1, (0, 1), (1,))
         load_w2(0)
-        load_w2_scales(0, 2)
+        load_w2_scales(0, 1)
         gates = keep.tile([P, SLOTS], F32, name="gates")
         nc.sync.dma_start(gates[:], gate[0:P, :])
         load_w2(1)
+        load_w2_scales(1, 2)
         res_in = {}
         for n in range(NT):
             res_in[n] = keep.tile([P, T], F32, name=f"res_in{n}")
@@ -260,7 +263,7 @@ def tile_moe_res_glu_silu_kernel(
                     nc.tensor.matmul_mx(
                         out=y[:, i, :],
                         lhsT=w2t[e][:, g, 2 * P * n : 2 * P * (n + 1)].bitcast(FP4X4),
-                        lhsT_scale=w2sc[:, e, g, P * n : P * (n + 1)],
+                        lhsT_scale=w2sc[e][:, g, P * n : P * (n + 1)],
                         rhs=hq[j][:, g, :].bitcast(FP8X4),
                         rhs_scale=hs[j][:, g, :],
                         start=(g == 0),

@@ -329,12 +329,10 @@ def tile_moe_res_glu_silu_kernel(
         first_layer(3, 1, (1,))
         second_layer(1, (0, 1))
         hidden(3, 0)
-        turn(3, (0,))
         hidden(3, 1)
-        turn(3, (1,))
+        turn(3, (0, 1))
         second_layer(2, (0, 1))
-        second_layer(3, (0,))
-        second_layer(3, (1,))
+        second_layer(3, (0, 1))
 
         for n in range(NT):
             done = keep.tile([P, T], F32, name=f"done{n}")

@@ -153,8 +153,6 @@ def tile_moe_res_glu_silu_kernel(
         rest = keep.tile([P, 2 * P], U32, name="rest", align_bytes=64)
         held = keep.tile([P, 2 * C], U32, name="held", align_bytes=64)
 
-        late = keep.tile([P, KP], F32, name="late", align_bytes=64)
-
         def table(s, u):
             return pairs[s, u][:].rearrange("p w d -> p (w d)").bitcast(U32)
 
@@ -176,13 +174,10 @@ def tile_moe_res_glu_silu_kernel(
             )
 
         def weave(tile, start, s, first, last, tag, copy=nc.scalar.copy):
-            if tag is None:
-                woven = late[:, 0 : 2 * P].bitcast(U32)
-            else:
-                woven = keep.tile([P, 2 * (last - first)], U32, name="woven", tag=tag, align_bytes=64)[:]
-            grouped[s, first] = woven
+            woven = keep.tile([P, 2 * (last - first)], U32, name="woven", tag=tag, align_bytes=64)
+            grouped[s, first] = woven[:]
             copy(
-                woven.bitcast(F32).rearrange("p (r u) -> p r u", u=2),
+                woven[:].bitcast(F32).rearrange("p (r u) -> p r u", u=2),
                 tile[:].bitcast(F32).rearrange("p (u r) -> p r u", u=2)[:, first - start : last - start, :],
             )
 
@@ -220,7 +215,7 @@ def tile_moe_res_glu_silu_kernel(
         def hidden(j, g):
             if g == 0:
                 h[j] = ring.tile([P, G, 2, P, 2], BF16, name="h", align_bytes=64, bufs=3)
-            act = late if (j, g) == (1, 1) else ring.tile([P, KP], F32, name="act", bufs=3)
+            act = ring.tile([P, KP], F32, name="act", bufs=3)
             nc.scalar.activation(
                 act[:].rearrange("r (u p e) -> r u p e", u=2, e=2),
                 acc[j, g, 0][:].rearrange("r (p u e) -> r u p e", u=2, e=2),
@@ -307,16 +302,14 @@ def tile_moe_res_glu_silu_kernel(
         for m in range(2):
             for g in range(G):
                 product(1, g, m, 1)
-        weave(held, C, 1, C, C + P, "woven2", nc.vector.tensor_copy)
-        quantise(1, C, C + P)
+        weave(held, C, 1, C, SLOTS, "woven2", nc.vector.tensor_copy)
+        quantise(1, C, SLOTS)
         hidden(0, 0)
         hidden(0, 1)
         first_layer(2, 0, (0,))
         turn(0, (0, 1))
         hidden(1, 0)
         hidden(1, 1)
-        weave(held, C, 1, C + P, SLOTS, None, nc.vector.tensor_copy)
-        quantise(1, C + P, SLOTS)
         first_layer(2, 0, (1,))
         turn(1, (0, 1))
         first_layer(2, 1)

@@ -25,9 +25,8 @@ G = H // KP
 UNITS = SLOTS // P
 NT = N // P
 STORES = (((0, 128), (128, 384), (384, T)), ((0, 512), (512, T)))
-QUANT = 256
-CUTS = (T, T, T, 384)
-VEC_TOKENS = (512, 384, 256, 256)
+VEC_TOKENS = (512, 512, 0, 384)
+WARM = 8
 
 
 def tile_moe_res_glu_silu_kernel(
@@ -41,41 +40,20 @@ def tile_moe_res_glu_silu_kernel(
 
         offsets = keep.tile([P, SLOTS // 16], U16, name="offsets")
 
+        def in_line(shape, dtype, name):
+            return ring.tile(shape, dtype, name=name, tag="line", bufs=52, align_bytes=64)
+
         words = (w1_words, w3_words)
         scales = (w1_scales, w3_scales)
-        wsc = {}
+        wsc, w2sc, w2t, wt = {}, {}, {}, {}
         for e in range(E):
             for m in range(2):
                 wsc[e, m] = keep.tile([P, PASSES, H], U8, name=f"wsc{e}{m}", align_bytes=64)
                 engine = nc.gpsimd if m == 0 else nc.vector
                 engine.memset(wsc[e, m][:].rearrange("p s i -> p (s i)").bitcast(I32), 0)
-
-        def load_scales(e, m, first, last, passes=(0, 1), halves=(0, 1)):
-            rows = scales[m][e].rearrange("s (q r) i -> r q s i", r=4)
-            s0, s1, i0, i1 = passes[0], passes[-1] + 1, halves[0] * KP, (halves[-1] + 1) * KP
-            for r in range(first, last):
-                nc.sync.dma_start(wsc[e, m][r:P:32, s0:s1, i0:i1].bitcast(I32), rows[r][:, s0:s1, i0:i1].bitcast(I32))
-
-        def load_w2_scales(e0, e1):
-            rows = w2_scales[e0:e1].rearrange("e s (q r) n -> r q (e s) n", r=4)
-            for r in range(4):
-                plane = w2sc[e0][r:P:32]
-                nc.sync.dma_start(plane.bitcast(I32), rows[r].bitcast(I32))
-
-        w2t = {}
-
-        def load_w2(e):
-            w2t[e] = keep.tile([P, PASSES, 2 * N], U8, name=f"w2t{e}", align_bytes=64)
-            nc.sync.dma_start(w2t[e][:].bitcast(I32), w2_words[e].rearrange("s p b -> p s b").bitcast(I32))
-
         warm = keep.tile([P, 1], F32, name="warm")
         nc.vector.memset(warm[:], 0.0)
         nc.scalar.activation(warm[:], warm[:], SILU)
-        xq, xs = {}, {}
-        for s in range(PASSES):
-            for e in range(E):
-                xs[s, e] = keep.tile([P, C], U8, name=f"xs{s}{e}", align_bytes=64)
-        w2sc = {}
         for e in range(E):
             w2sc[e] = keep.tile([P, PASSES, N], U8, name=f"w2sc{e}", align_bytes=64)
             nc.vector.memset(w2sc[e][:].rearrange("p s n -> p (s n)").bitcast(I32), 0)
@@ -86,6 +64,20 @@ def tile_moe_res_glu_silu_kernel(
         ident = keep.tile([P, P], F32, name="ident")
         make_identity(nc, ident[:])
 
+        def load_scales(e, m):
+            rows = scales[m][e].rearrange("s (q r) i -> r q s i", r=4)
+            for r in range(4):
+                nc.sync.dma_start(wsc[e, m][r:P:32].bitcast(I32), rows[r].bitcast(I32))
+
+        def load_w2_scales(e):
+            rows = w2_scales[e].rearrange("s (q r) n -> r q s n", r=4)
+            for r in range(4):
+                nc.sync.dma_start(w2sc[e][r:P:32].bitcast(I32), rows[r].bitcast(I32))
+
+        def load_w2(e):
+            w2t[e] = keep.tile([P, PASSES, 2 * N], U8, name=f"w2t{e}", align_bytes=64)
+            nc.sync.dma_start(w2t[e][:].bitcast(I32), w2_words[e].rearrange("s p b -> p s b").bitcast(I32))
+
         xview = xT.rearrange("(s p u d) w -> s u p d w", s=PASSES, p=P, u=2)
         raw = {}
 
@@ -93,8 +85,6 @@ def tile_moe_res_glu_silu_kernel(
             if first == 0:
                 raw[s, u] = keep.tile([P, 2, T], F32, name=f"raw{s}{u}", align_bytes=64)
             nc.sync.dma_start(raw[s, u][:, :, first:last], xview[s, u][:, :, first:last])
-
-        wt = {}
 
         def load_words(e, m, passes, halves):
             piece = keep.tile(
@@ -107,123 +97,112 @@ def tile_moe_res_glu_silu_kernel(
                 for g in halves:
                     wt[e, m, s, g] = piece[:, s - passes[0], (g - halves[0]) * 2 * KP : (g - halves[0] + 1) * 2 * KP]
 
-        load_x(0, 0)
-        nc.sync.dma_start(offsets[:], offs)
-        load_x(0, 1)
-        load_x(1, 0)
-        load_scales(0, 0, 0, 4)
-        load_words(0, 0, (0,), (0, 1))
-        load_x(1, 1, 0, CUTS[3])
-        load_x(1, 1, CUTS[3], T)
-        load_scales(0, 1, 0, 4)
-        load_words(0, 1, (0,), (0, 1))
-        load_words(0, 0, (1,), (0, 1))
-        load_words(0, 1, (1,), (0, 1))
-        load_scales(1, 0, 0, 4)
-        load_words(1, 0, (0, 1), (0,))
-        load_scales(1, 1, 0, 4)
-        load_words(1, 1, (0, 1), (0,))
-        load_words(1, 0, (0, 1), (1,))
-        load_words(1, 1, (0, 1), (1,))
-        load_w2(0)
-        load_w2_scales(0, 1)
-        gates = keep.tile([P, SLOTS], F32, name="gates")
-        nc.sync.dma_start(gates[:], gate[0:P, :])
-        load_w2(1)
-        load_w2_scales(1, 2)
-        res_in = {}
-        for n in range(NT):
+        gates, res_in = {}, {}
+
+        def load_gate(first, last):
+            piece = keep.tile([P, last - first], F32, name=f"gates{first}")
+            nc.sync.dma_start(piece[:], gate[0:P, first:last])
+            for j in range(first // P, last // P):
+                gates[j] = piece[:, j * P - first : (j + 1) * P - first]
+
+        def load_residual(n):
             res_in[n] = keep.tile([P, T], F32, name=f"res_in{n}")
             nc.sync.dma_start(res_in[n][:], xr[n * P : (n + 1) * P, :])
 
-        pairs = {}
+        grouped, plain, xq, xs = {}, {}, {}, {}
+        tables = {}
 
-        def round_pairs(s, u):
-            pairs[s, u] = keep.tile([P, T, 2], BF16, name=f"pairs{s}{u}", align_bytes=64)
+        def round_pairs(s, u, first=0, last=T):
             src = raw[s, u][:].rearrange("p d w -> p w d")
-            cut, v = CUTS[2 * s + u], T - VEC_TOKENS[2 * s + u]
-            for first, last in ((0, min(cut, v)), (cut, v)):
-                if first < last:
-                    nc.scalar.copy(pairs[s, u][:, first:last, :], src[:, first:last, :])
-            if v < T:
-                nc.vector.tensor_copy(pairs[s, u][:, v:T, :], src[:, v:T, :])
+            if first == 0:
+                tables[s, u] = in_line([P, T, 2], BF16, "pairs")
+            pairs = tables[s, u]
+            v = max(first, min(last, T - VEC_TOKENS[2 * s + u]))
+            if v > first:
+                nc.scalar.copy(pairs[:, first:v, :], src[:, first:v, :])
+            if v < last:
+                nc.vector.tensor_copy(pairs[:, v:last, :], src[:, v:last, :])
 
-        grouped, acts = {}, {}
-        plain = keep.tile([P, 2 * C], U32, name="plain", align_bytes=64)
-        rest = keep.tile([P, 2 * P], U32, name="rest", align_bytes=64)
-        held = keep.tile([P, 2 * C], U32, name="held", align_bytes=64)
+        def window(s, u, first, last):
+            table = tables[s, u][:].rearrange("p w d -> p (w d)").bitcast(U32)
+            return table.indirect(offsets[:, first // 16 : last // 16])
 
-        def table(s, u):
-            return pairs[s, u][:].rearrange("p w d -> p (w d)").bitcast(U32)
-
-        def gather(s, u, first, last):
-            if u == 0 and s == 1:
-                grouped[s, first] = held[:, C : 2 * C]
-            elif u == 0:
-                own = keep.tile([P, 2 * (last - first)], U32, name=f"grouped{s}{first}", align_bytes=64)
+        def gather_stepped(s, u, first, last):
+            if u == 0:
+                own = in_line([P, 2 * (last - first)], U32, "grouped")
                 grouped[s, first] = own[:]
             nc.vector.tensor_copy(
-                grouped[s, first].rearrange("p (r u) -> p r u", u=2)[:, :, u],
-                table(s, u).indirect(offsets[:, first // 16 : last // 16]),
+                grouped[s, first].rearrange("p (r u) -> p r u", u=2)[:, :, u], window(s, u, first, last)
             )
 
-        def gather_plain(tile, s, u, first, last=SLOTS):
+        def gather_both(s, u, first, last):
             width = last - first
-            nc.vector.tensor_copy(
-                tile[:, u * width : (u + 1) * width], table(s, u).indirect(offsets[:, first // 16 : last // 16])
-            )
+            if u == 0:
+                plain[s, first] = in_line([P, 2 * width], U32, "plain")
+            nc.vector.tensor_copy(plain[s, first][:, u * width : (u + 1) * width], window(s, u, first, last))
 
-        def weave(tile, start, s, first, last, tag, copy=nc.scalar.copy):
-            woven = keep.tile([P, 2 * (last - first)], U32, name="woven", tag=tag, align_bytes=64)
+        def weave(s, start, first, last, copy):
+            woven = in_line([P, 2 * (last - first)], U32, "woven")
             grouped[s, first] = woven[:]
             copy(
-                woven[:].bitcast(F32).rearrange("p (r u) -> p r u", u=2),
-                tile[:].bitcast(F32).rearrange("p (u r) -> p r u", u=2)[:, first - start : last - start, :],
+                grouped[s, first].bitcast(F32).rearrange("p (r u) -> p r u", u=2),
+                plain[s, start][:].bitcast(F32).rearrange("p (u r) -> p r u", u=2)[:, first - start : last - start, :],
             )
 
         def quantise(s, first, last):
-            e, cols = first // C, slice(first % C, (last - 1) % C + 1)
-            if first % C == 0:
-                tag = f"xq{s}{e}"
-                xq[s, e] = keep.tile([P, C], U32, name="xq", tag=tag, align_bytes=64)
-            nc.vector.quantize_mx(
-                out=xq[s, e][:, cols].bitcast(FP8X4), scales=xs[s, e][:, cols], in_=grouped[s, first].bitcast(BF16)
-            )
+            codes = in_line([P, last - first], U32, "codes")
+            plane = keep.tile([P, last - first], U8, name=f"xs{s}{first}", align_bytes=64)
+            nc.vector.quantize_mx(out=codes[:].bitcast(FP8X4), scales=plane[:], in_=grouped[s, first].bitcast(BF16))
+            for j in range(first // P, last // P):
+                xq[s, j] = codes[:, j * P - first : (j + 1) * P - first]
+                xs[s, j] = plane[:, j * P - first : (j + 1) * P - first]
 
-        acc, h, turned, hq, hs = {}, {}, {}, {}, {}
+        acc, act, h, hq, hs, ysb, pending = {}, {}, {}, {}, {}, {}, {}
 
         def product(j, g, m, s):
             e = j * P // C
-            cols = slice(j * P % C, j * P % C + P)
             if s == 0:
                 acc[j, g, m] = psum.tile([P, KP], F32, name="acc", tag="bank")
             nc.tensor.matmul_mx(
                 out=acc[j, g, m][:],
-                lhsT=xq[s, e][:, cols].bitcast(FP8X4),
-                lhsT_scale=xs[s, e][:, cols],
+                lhsT=xq[s, j].bitcast(FP8X4),
+                lhsT_scale=xs[s, j],
                 rhs=wt[e, m, s, g].bitcast(FP4X4),
                 rhs_scale=wsc[e, m][:, s, g * KP : (g + 1) * KP],
                 start=(s == 0),
                 stop=(s == PASSES - 1),
             )
 
-        def first_layer(j, g, matrices=(0, 1)):
-            for m in matrices:
-                for s in range(PASSES):
-                    product(j, g, m, s)
+        def warm_up(count):
+            spare = psum.tile([P, N], F32, name="spare", tag="bank")
+            for i in range(count):
+                nc.tensor.matmul_mx(
+                    out=spare[:],
+                    lhsT=xq[0, 0].bitcast(FP8X4),
+                    lhsT_scale=xs[0, 0],
+                    rhs=xq[0, 0].bitcast(U8).bitcast(FP4X4),
+                    rhs_scale=w2sc[1][:, 0, :],
+                    start=True,
+                    stop=True,
+                )
 
-        def hidden(j, g):
-            if g == 0:
-                h[j] = ring.tile([P, G, 2, P, 2], BF16, name="h", align_bytes=64, bufs=3)
-            act = ring.tile([P, KP], F32, name="act", bufs=3)
+        def both(j, g, m):
+            for s in range(PASSES):
+                product(j, g, m, s)
+
+        def silu(j, g):
+            act[j, g] = in_line([P, KP], F32, "act")
             nc.scalar.activation(
-                act[:].rearrange("r (u p e) -> r u p e", u=2, e=2),
+                act[j, g][:].rearrange("r (u p e) -> r u p e", u=2, e=2),
                 acc[j, g, 0][:].rearrange("r (p u e) -> r u p e", u=2, e=2),
                 SILU,
             )
+
+        def hidden(j, g):
+            h[j, g] = in_line([P, 2, P, 2], BF16, "h")
             nc.vector.tensor_tensor(
-                h[j][:, g, :, :, :],
-                act[:].rearrange("r (u p e) -> r u p e", u=2, e=2),
+                h[j, g][:],
+                act[j, g][:].rearrange("r (u p e) -> r u p e", u=2, e=2),
                 acc[j, g, 1][:].rearrange("r (p u e) -> r u p e", u=2, e=2),
                 MULT,
             )
@@ -231,24 +210,33 @@ def tile_moe_res_glu_silu_kernel(
         def turn(j, halves):
             count, g0 = len(halves), halves[0]
             turned = psum.tile([P, count, 2, P], F32, name="turned", tag="bank")
-            hq_in = ring.tile([P, count, P, 4], BF16, name="hq_in", align_bytes=64, bufs=3)
-            if g0 == 0:
-                hq[j] = ring.tile([P, G, P], U32, name="hq", align_bytes=64, bufs=3)
-                hs[j] = ring.tile([P, G, P], U8, name="hs", align_bytes=64, bufs=3)
-            hw = h[j][:].rearrange("r g u p e -> r (g u p e)").bitcast(F32)
             for g in halves:
+                hw = h[j, g][:].rearrange("r u p e -> r (u p e)").bitcast(F32)
                 for u in range(2):
-                    w0 = (2 * g + u) * P
-                    nc.tensor.transpose(turned[:, g - g0, u, :], hw[:, w0 : w0 + P], ident[:])
+                    nc.tensor.transpose(turned[:, g - g0, u, :], hw[:, u * P : (u + 1) * P], ident[:])
+            pending[j, g0, "turned"] = turned
+
+        def unturn(j, halves):
+            count, g0 = len(halves), halves[0]
+            turned = pending[j, g0, "turned"]
+            hq_in = in_line([P, count, P, 4], BF16, "hq_in")
             nc.scalar.copy(
                 hq_in[:].rearrange("p g r t -> p (g r t)").bitcast(F32).rearrange("p (g r u) -> p g r u", g=count, u=2),
                 turned[:].rearrange("p g u r -> p g r u"),
             )
+            pending[j, g0] = (hq_in, halves)
+
+        def requant(j, g0):
+            hq_in, halves = pending[j, g0]
+            codes = in_line([P, len(halves), P], U32, "hq")
+            plane = keep.tile([P, len(halves), P], U8, name=f"hs{j}{g0}", align_bytes=64)
             nc.vector.quantize_mx(
-                out=hq[j][:, g0 : g0 + count, :].rearrange("p g r -> p (g r)").bitcast(FP8X4),
-                scales=hs[j][:, g0 : g0 + count, :].rearrange("p g r -> p (g r)"),
+                out=codes[:].rearrange("p g r -> p (g r)").bitcast(FP8X4),
+                scales=plane[:].rearrange("p g r -> p (g r)"),
                 in_=hq_in[:].rearrange("p g r t -> p (g r t)"),
             )
+            for g in halves:
+                hq[j, g], hs[j, g] = codes[:, g - g0, :], plane[:, g - g0, :]
 
         def second_layer(j, tiles):
             e = j * P // C
@@ -259,77 +247,153 @@ def tile_moe_res_glu_silu_kernel(
                         out=y[:, i, :],
                         lhsT=w2t[e][:, g, 2 * P * n : 2 * P * (n + 1)].bitcast(FP4X4),
                         lhsT_scale=w2sc[e][:, g, P * n : P * (n + 1)],
-                        rhs=hq[j][:, g, :].bitcast(FP8X4),
-                        rhs_scale=hs[j][:, g, :],
+                        rhs=hq[j, g].bitcast(FP8X4),
+                        rhs_scale=hs[j, g],
                         start=(g == 0),
                         stop=(g == G - 1),
                     )
-            y_sb = keep.tile([P, len(tiles), P], F32, name=f"ys{j}{tiles[0]}")
-            nc.scalar.copy(y_sb[:], y[:])
-            cols = slice(j * P, (j + 1) * P)
+            pending[j, tiles] = y
+
+        def copy_out(j, tiles):
+            y_sb = in_line([P, len(tiles), P], F32, "y_sb")
+            nc.scalar.copy(y_sb[:], pending[j, tiles][:])
             for i, n in enumerate(tiles):
-                nc.vector.tensor_tensor(
-                    back[n][:].indirect(offsets[:, j * P // 16 : (j + 1) * P // 16]), y_sb[:, i, :], gates[:, cols], MULT
-                )
+                ysb[j, n] = y_sb[:, i, :]
 
-        round_pairs(0, 0)
-        gather(0, 0, 0, C)
-        round_pairs(0, 1)
-        gather(0, 1, 0, C)
-        quantise(0, 0, C)
-        round_pairs(1, 0)
-        gather(1, 0, 0, P)
-        round_pairs(1, 1)
-        gather_plain(plain, 0, 0, C)
-        gather_plain(plain, 0, 1, C)
-        weave(plain, C, 0, C, SLOTS, "raw10")
-        gather_plain(rest, 1, 0, P, C)
-        gather_plain(held, 1, 0, C)
-        for m in range(2):
-            for j in range(2):
-                for g in range(G):
-                    product(j, g, m, 0)
-        gather(1, 1, 0, P)
-        gather_plain(rest, 1, 1, P, C)
-        quantise(1, 0, P)
-        gather_plain(held, 1, 1, C)
-        quantise(0, C, SLOTS)
-        for m in range(2):
-            for g in range(G):
-                product(0, g, m, 1)
-        weave(rest, P, 1, P, C, "woven1")
-        quantise(1, P, C)
-        for m in range(2):
-            for g in range(G):
-                product(1, g, m, 1)
-        weave(held, C, 1, C, SLOTS, "woven2", nc.vector.tensor_copy)
-        quantise(1, C, SLOTS)
-        hidden(0, 0)
-        hidden(0, 1)
-        first_layer(2, 0, (0,))
-        turn(0, (0, 1))
-        hidden(1, 0)
-        hidden(1, 1)
-        first_layer(2, 0, (1,))
-        turn(1, (0, 1))
-        first_layer(2, 1)
-        second_layer(0, (0, 1))
-        hidden(2, 0)
-        hidden(2, 1)
-        first_layer(3, 0)
-        first_layer(3, 1, (0,))
-        turn(2, (0, 1))
-        first_layer(3, 1, (1,))
-        second_layer(1, (0, 1))
-        hidden(3, 0)
-        hidden(3, 1)
-        turn(3, (0, 1))
-        second_layer(2, (0, 1))
-        second_layer(3, (0, 1))
+        def put_back(j, n):
+            nc.vector.tensor_tensor(back[n][:].indirect(offsets[:, j * P // 16 : (j + 1) * P // 16]), ysb[j, n], gates[j], MULT)
 
-        for n in range(NT):
+        def finish(n):
             done = keep.tile([P, T], F32, name=f"done{n}")
             for first, last in STORES[n]:
                 cols = slice(first, last)
                 nc.vector.tensor_tensor(done[:, cols], back[n][:, cols], res_in[n][:, cols], ADD)
                 nc.sync.dma_start(out[n * P : (n + 1) * P, cols], done[:, cols])
+
+        load_x(0, 0)
+        nc.sync.dma_start(offsets[:], offs)
+        load_x(0, 1)
+        load_x(1, 0)
+        load_x(1, 1)
+        load_scales(0, 0)
+        load_words(0, 0, (0,), (0, 1))
+        load_words(0, 0, (1,), (0, 1))
+        load_scales(0, 1)
+        load_words(0, 1, (0, 1), (0,))
+        load_words(0, 1, (0, 1), (1,))
+        load_w2_scales(0)
+        load_words(1, 0, (0, 1), (0,))
+        load_scales(1, 0)
+        load_w2(0)
+        load_gate(0, C)
+        load_words(1, 1, (0, 1), (0,))
+        load_scales(1, 1)
+        load_words(1, 0, (0, 1), (1,))
+        load_words(1, 1, (0, 1), (1,))
+
+        round_pairs(0, 0)
+        gather_stepped(0, 0, 0, P)
+        gather_stepped(0, 0, P, C)
+        round_pairs(0, 1)
+        gather_stepped(0, 1, 0, P)
+        gather_stepped(0, 1, P, C)
+        quantise(0, 0, P)
+        warm_up(WARM)
+        load_w2(1)
+        load_w2_scales(1)
+        load_gate(C, SLOTS)
+        load_residual(0)
+        load_residual(1)
+        quantise(0, P, C)
+        gather_both(0, 0, C, SLOTS)
+        gather_both(0, 1, C, SLOTS)
+        round_pairs(1, 0)
+        round_pairs(1, 1)
+        gather_stepped(1, 0, 0, P)
+        gather_stepped(1, 0, P, C)
+        gather_stepped(1, 1, 0, P)
+        gather_stepped(1, 1, P, C)
+        weave(0, C, C, SLOTS, nc.scalar.copy)
+        quantise(1, 0, P)
+        quantise(1, P, C)
+        gather_both(1, 0, C, SLOTS)
+        gather_both(1, 1, C, SLOTS)
+        quantise(0, C, SLOTS)
+        weave(1, C, C, SLOTS, nc.vector.tensor_copy)
+
+        product(0, 0, 0, 0)
+        product(0, 1, 0, 0)
+        product(1, 0, 0, 0)
+        product(1, 1, 0, 0)
+        product(0, 0, 0, 1)
+        product(0, 1, 0, 1)
+        product(1, 0, 0, 1)
+        product(1, 1, 0, 1)
+        silu(0, 0)
+        silu(0, 1)
+        silu(1, 0)
+        silu(1, 1)
+        both(0, 0, 1)
+        both(0, 1, 1)
+        hidden(0, 0)
+        quantise(1, C, SLOTS)
+        hidden(0, 1)
+        both(1, 0, 1)
+        both(1, 1, 1)
+        hidden(1, 0)
+        hidden(1, 1)
+        turn(0, (0,))
+        turn(0, (1,))
+        unturn(0, (0,))
+        unturn(0, (1,))
+        requant(0, 0)
+        requant(0, 1)
+        both(2, 0, 0)
+        silu(2, 0)
+        both(3, 0, 0)
+        second_layer(0, (0,))
+        second_layer(0, (1,))
+        copy_out(0, (0,))
+        turn(1, (0, 1))
+        put_back(0, 0)
+        unturn(1, (0, 1))
+        silu(3, 0)
+        requant(1, 0)
+        both(2, 0, 1)
+        hidden(2, 0)
+        both(3, 0, 1)
+        hidden(3, 0)
+        both(2, 1, 0)
+        silu(2, 1)
+        both(2, 1, 1)
+        hidden(2, 1)
+        copy_out(0, (1,))
+        put_back(0, 1)
+        both(3, 1, 0)
+        silu(3, 1)
+        both(3, 1, 1)
+        hidden(3, 1)
+        second_layer(1, (0,))
+        second_layer(1, (1,))
+        copy_out(1, (0,))
+        put_back(1, 0)
+        turn(2, (0, 1))
+        unturn(2, (0, 1))
+        requant(2, 0)
+        copy_out(1, (1,))
+        put_back(1, 1)
+        turn(3, (0, 1))
+        unturn(3, (0, 1))
+        second_layer(2, (0,))
+        second_layer(2, (1,))
+        requant(3, 0)
+        copy_out(2, (0,))
+        copy_out(2, (1,))
+        put_back(2, 0)
+        put_back(2, 1)
+        second_layer(3, (0, 1))
+        copy_out(3, (0, 1))
+        put_back(3, 0)
+        put_back(3, 1)
+        finish(0)
+        finish(1)

@@ -25,8 +25,8 @@ G = H // KP
 UNITS = SLOTS // P
 NT = N // P
 STORES = (((0, 128), (128, 384), (384, T)), ((0, 512), (512, T)))
-VEC_TOKENS = (512, 512, 0, 384)
-WARM = 8
+VEC_TOKENS = (512, 448, 0, 448)
+WARM = 7
 
 
 def tile_moe_res_glu_silu_kernel(
@@ -41,7 +41,7 @@ def tile_moe_res_glu_silu_kernel(
         offsets = keep.tile([P, SLOTS // 16], U16, name="offsets")
 
         def in_line(shape, dtype, name):
-            return ring.tile(shape, dtype, name=name, tag="line", bufs=52, align_bytes=64)
+            return ring.tile(shape, dtype, name=name, tag="line", bufs=50, align_bytes=64)
 
         words = (w1_words, w3_words)
         scales = (w1_scales, w3_scales)
@@ -109,44 +109,37 @@ def tile_moe_res_glu_silu_kernel(
             res_in[n] = keep.tile([P, T], F32, name=f"res_in{n}")
             nc.sync.dma_start(res_in[n][:], xr[n * P : (n + 1) * P, :])
 
-        grouped, plain, xq, xs = {}, {}, {}, {}
-        tables = {}
+        tables, plain, grouped, xq, xs = {}, {}, {}, {}, {}
 
-        def round_pairs(s, u, first=0, last=T):
+        def round_pairs(s, u):
+            pairs = in_line([P, T, 2], BF16, "pairs")
+            tables[s, u] = pairs[:].rearrange("p w d -> p (w d)").bitcast(U32)
             src = raw[s, u][:].rearrange("p d w -> p w d")
-            if first == 0:
-                tables[s, u] = in_line([P, T, 2], BF16, "pairs")
-            pairs = tables[s, u]
-            v = max(first, min(last, T - VEC_TOKENS[2 * s + u]))
-            if v > first:
-                nc.scalar.copy(pairs[:, first:v, :], src[:, first:v, :])
-            if v < last:
-                nc.vector.tensor_copy(pairs[:, v:last, :], src[:, v:last, :])
+            v = T - VEC_TOKENS[2 * s + u]
+            if v > 0:
+                nc.scalar.copy(pairs[:, 0:v, :], src[:, 0:v, :])
+            if v < T:
+                nc.vector.tensor_copy(pairs[:, v:T, :], src[:, v:T, :])
 
-        def window(s, u, first, last):
-            table = tables[s, u][:].rearrange("p w d -> p (w d)").bitcast(U32)
-            return table.indirect(offsets[:, first // 16 : last // 16])
-
-        def gather_stepped(s, u, first, last):
-            if u == 0:
-                own = in_line([P, 2 * (last - first)], U32, "grouped")
-                grouped[s, first] = own[:]
+        def gather(s, u, first, last):
+            e = first // C
+            if (s, e) not in plain:
+                plain[s, e] = in_line([P, 2 * C], U32, "plain")
             nc.vector.tensor_copy(
-                grouped[s, first].rearrange("p (r u) -> p r u", u=2)[:, :, u], window(s, u, first, last)
+                plain[s, e][:, (u - e) * C + first : (u - e) * C + last],
+                tables[s, u].indirect(offsets[:, first // 16 : last // 16]),
             )
 
-        def gather_both(s, u, first, last):
-            width = last - first
-            if u == 0:
-                plain[s, first] = in_line([P, 2 * width], U32, "plain")
-            nc.vector.tensor_copy(plain[s, first][:, u * width : (u + 1) * width], window(s, u, first, last))
-
-        def weave(s, start, first, last, copy):
-            woven = in_line([P, 2 * (last - first)], U32, "woven")
-            grouped[s, first] = woven[:]
+        def weave(s, first, last, copy):
+            e = first // C
+            if first == P:
+                grouped[s, first] = plain[s, 1][:, C : 2 * C]
+            else:
+                grouped[s, first] = in_line([P, 2 * (last - first)], U32, "woven")[:]
+            both_rows = plain[s, e][:].bitcast(F32).rearrange("p (u r) -> p r u", u=2)
             copy(
                 grouped[s, first].bitcast(F32).rearrange("p (r u) -> p r u", u=2),
-                plain[s, start][:].bitcast(F32).rearrange("p (u r) -> p r u", u=2)[:, first - start : last - start, :],
+                both_rows[:, first - e * C : last - e * C, :],
             )
 
         def quantise(s, first, last):
@@ -292,34 +285,31 @@ def tile_moe_res_glu_silu_kernel(
         load_words(1, 1, (0, 1), (1,))
 
         round_pairs(0, 0)
-        gather_stepped(0, 0, 0, P)
-        gather_stepped(0, 0, P, C)
+        gather(0, 0, 0, C)
+        gather(0, 0, C, SLOTS)
         round_pairs(0, 1)
-        gather_stepped(0, 1, 0, P)
-        gather_stepped(0, 1, P, C)
+        gather(0, 1, 0, C)
+        weave(0, 0, P, nc.vector.tensor_copy)
+        weave(0, P, C, nc.vector.tensor_copy)
         quantise(0, 0, P)
-        warm_up(WARM)
-        load_w2(1)
-        load_w2_scales(1)
-        load_gate(C, SLOTS)
-        load_residual(0)
-        load_residual(1)
+        warm_up(WARM); load_w2(1); load_w2_scales(1); load_gate(C, SLOTS); load_residual(0); load_residual(1)
         quantise(0, P, C)
-        gather_both(0, 0, C, SLOTS)
-        gather_both(0, 1, C, SLOTS)
+        gather(0, 1, C, SLOTS)
         round_pairs(1, 0)
         round_pairs(1, 1)
-        gather_stepped(1, 0, 0, P)
-        gather_stepped(1, 0, P, C)
-        gather_stepped(1, 1, 0, P)
-        gather_stepped(1, 1, P, C)
-        weave(0, C, C, SLOTS, nc.scalar.copy)
+        gather(1, 0, 0, C)
+        gather(1, 1, 0, P)
+        gather(1, 1, P, C)
+        weave(0, C, SLOTS, nc.scalar.copy)
+        weave(1, 0, P, nc.scalar.copy)
+        gather(1, 0, C, SLOTS)
+        weave(1, P, C, nc.scalar.copy)
         quantise(1, 0, P)
         quantise(1, P, C)
-        gather_both(1, 0, C, SLOTS)
-        gather_both(1, 1, C, SLOTS)
         quantise(0, C, SLOTS)
-        weave(1, C, C, SLOTS, nc.vector.tensor_copy)
+        gather(1, 1, C, SLOTS)
+        weave(1, C, SLOTS, nc.vector.tensor_copy)
+        quantise(1, C, SLOTS)
 
         product(0, 0, 0, 0)
         product(0, 1, 0, 0)
@@ -336,7 +326,6 @@ def tile_moe_res_glu_silu_kernel(
         both(0, 0, 1)
         both(0, 1, 1)
         hidden(0, 0)
-        quantise(1, C, SLOTS)
         hidden(0, 1)
         both(1, 0, 1)
         both(1, 1, 1)
@@ -349,40 +338,40 @@ def tile_moe_res_glu_silu_kernel(
         requant(0, 0)
         requant(0, 1)
         both(2, 0, 0)
-        silu(2, 0)
-        both(3, 0, 0)
+        turn(1, (0, 1))
         second_layer(0, (0,))
         second_layer(0, (1,))
-        copy_out(0, (0,))
-        turn(1, (0, 1))
-        put_back(0, 0)
         unturn(1, (0, 1))
-        silu(3, 0)
+        copy_out(0, (0,))
+        both(3, 0, 0)
+        silu(2, 0)
         requant(1, 0)
+        put_back(0, 0)
         both(2, 0, 1)
         hidden(2, 0)
-        both(3, 0, 1)
-        hidden(3, 0)
-        both(2, 1, 0)
-        silu(2, 1)
-        both(2, 1, 1)
-        hidden(2, 1)
         copy_out(0, (1,))
         put_back(0, 1)
+        both(2, 1, 0)
+        silu(3, 0)
+        silu(2, 1)
         both(3, 1, 0)
         silu(3, 1)
+        both(2, 1, 1)
+        hidden(2, 1)
+        both(3, 0, 1)
+        hidden(3, 0)
         both(3, 1, 1)
-        hidden(3, 1)
         second_layer(1, (0,))
         second_layer(1, (1,))
-        copy_out(1, (0,))
-        put_back(1, 0)
+        hidden(3, 1)
         turn(2, (0, 1))
+        copy_out(1, (0,))
         unturn(2, (0, 1))
+        put_back(1, 0)
+        turn(3, (0, 1))
         requant(2, 0)
         copy_out(1, (1,))
         put_back(1, 1)
-        turn(3, (0, 1))
         unturn(3, (0, 1))
         second_layer(2, (0,))
         second_layer(2, (1,))

@@ -278,9 +278,9 @@ def tile_moe_res_glu_silu_kernel(
         load_words(1, 0, (0, 1), (0,))
         load_scales(1, 0)
         load_w2(0)
-        load_gate(0, C)
         load_words(1, 1, (0, 1), (0,))
         load_scales(1, 1)
+        load_gate(0, C)
         load_words(1, 0, (0, 1), (1,))
         load_words(1, 1, (0, 1), (1,))
 

@@ -43,6 +43,9 @@ def tile_moe_res_glu_silu_kernel(
         def in_line(shape, dtype, name):
             return ring.tile(shape, dtype, name=name, tag="line", bufs=50, align_bytes=64)
 
+        warm = keep.tile([P, 1], F32, name="warm")
+        nc.gpsimd.memset(warm[:], 0.0)
+        nc.scalar.activation(warm[:], warm[:], SILU)
         words = (w1_words, w3_words)
         scales = (w1_scales, w3_scales)
         wsc, w2sc, w2t, wt = {}, {}, {}, {}
@@ -51,12 +54,9 @@ def tile_moe_res_glu_silu_kernel(
                 wsc[e, m] = keep.tile([P, PASSES, H], U8, name=f"wsc{e}{m}", align_bytes=64)
                 engine = nc.gpsimd if m == 0 else nc.vector
                 engine.memset(wsc[e, m][:].rearrange("p s i -> p (s i)").bitcast(I32), 0)
-        warm = keep.tile([P, 1], F32, name="warm")
-        nc.vector.memset(warm[:], 0.0)
-        nc.scalar.activation(warm[:], warm[:], SILU)
         for e in range(E):
             w2sc[e] = keep.tile([P, PASSES, N], U8, name=f"w2sc{e}", align_bytes=64)
-            nc.vector.memset(w2sc[e][:].rearrange("p s n -> p (s n)").bitcast(I32), 0)
+            nc.gpsimd.memset(w2sc[e][:].rearrange("p s n -> p (s n)").bitcast(I32), 0)
         back = {}
         for n in range(NT):
             back[n] = keep.tile([P, T], F32, name=f"back{n}")

@@ -25,8 +25,8 @@ G = H // KP
 UNITS = SLOTS // P
 NT = N // P
 STORES = (((0, 128), (128, 384), (384, T)), ((0, 512), (512, T)))
-VEC_TOKENS = (512, 448, 0, 448)
-WARM = 7
+VEC_TOKENS = (512, 512, 384, 448)
+WARM = 8
 
 
 def tile_moe_res_glu_silu_kernel(
@@ -59,7 +59,7 @@ def tile_moe_res_glu_silu_kernel(
             nc.gpsimd.memset(w2sc[e][:].rearrange("p s n -> p (s n)").bitcast(I32), 0)
         back = {}
         for n in range(NT):
-            back[n] = keep.tile([P, T], F32, name=f"back{n}")
+            back[n] = keep.tile([P, T], F32, name=f"back{n}", align_bytes=64)
             nc.vector.memset(back[n][:], 0.0)
         ident = keep.tile([P, P], F32, name="ident")
         make_identity(nc, ident[:])
@@ -121,25 +121,34 @@ def tile_moe_res_glu_silu_kernel(
             if v < T:
                 nc.vector.tensor_copy(pairs[:, v:T, :], src[:, v:T, :])
 
-        def gather(s, u, first, last):
-            e = first // C
-            if (s, e) not in plain:
-                plain[s, e] = in_line([P, 2 * C], U32, "plain")
+        def gather(s, u, key, first, last):
+            start, width = key
+            if (s, start) not in plain:
+                if width == SLOTS:
+                    plain[s, start] = keep.tile([P, 2 * width], U32, name="plain_all", align_bytes=64)
+                else:
+                    plain[s, start] = in_line([P, 2 * width], U32, "plain")
             nc.vector.tensor_copy(
-                plain[s, e][:, (u - e) * C + first : (u - e) * C + last],
+                plain[s, start][:, u * width + first - start : u * width + last - start],
                 tables[s, u].indirect(offsets[:, first // 16 : last // 16]),
             )
 
-        def weave(s, first, last, copy):
-            e = first // C
-            if first == P:
-                grouped[s, first] = plain[s, 1][:, C : 2 * C]
-            else:
-                grouped[s, first] = in_line([P, 2 * (last - first)], U32, "woven")[:]
-            both_rows = plain[s, e][:].bitcast(F32).rearrange("p (u r) -> p r u", u=2)
+        def gather_stepped(s, u, first, last):
+            if u == 0:
+                grouped[s, first] = in_line([P, 2 * (last - first)], U32, "grouped")[:]
+            nc.vector.tensor_copy(
+                grouped[s, first].rearrange("p (r u) -> p r u", u=2)[:, :, u],
+                tables[s, u].indirect(offsets[:, first // 16 : last // 16]),
+            )
+
+        def weave(s, start, first, last, copy, into=None):
+            if into is None:
+                into = in_line([P, 2 * (last - first)], U32, "woven")[:]
+            grouped[s, first] = into
+            both_rows = plain[s, start][:].bitcast(F32).rearrange("p (u r) -> p r u", u=2)
             copy(
-                grouped[s, first].bitcast(F32).rearrange("p (r u) -> p r u", u=2),
-                both_rows[:, first - e * C : last - e * C, :],
+                into.bitcast(F32).rearrange("p (r u) -> p r u", u=2),
+                both_rows[:, first - start : last - start, :],
             )
 
         def quantise(s, first, last):
@@ -167,13 +176,16 @@ def tile_moe_res_glu_silu_kernel(
             )
 
         def warm_up(count):
+            codes = in_line([P, P], U32, "zero_codes")
+            plane = keep.tile([P, P], U8, name="zero_plane", align_bytes=64)
+            nc.vector.quantize_mx(out=codes[:].bitcast(FP8X4), scales=plane[:], in_=back[1][:, 0:N].bitcast(BF16))
             spare = psum.tile([P, N], F32, name="spare", tag="bank")
             for i in range(count):
                 nc.tensor.matmul_mx(
                     out=spare[:],
-                    lhsT=xq[0, 0].bitcast(FP8X4),
-                    lhsT_scale=xs[0, 0],
-                    rhs=xq[0, 0].bitcast(U8).bitcast(FP4X4),
+                    lhsT=codes[:].bitcast(FP8X4),
+                    lhsT_scale=plane[:],
+                    rhs=codes[:].bitcast(U8).bitcast(FP4X4),
                     rhs_scale=w2sc[1][:, 0, :],
                     start=True,
                     stop=True,
@@ -285,30 +297,26 @@ def tile_moe_res_glu_silu_kernel(
         load_words(1, 1, (0, 1), (1,))
 
         round_pairs(0, 0)
-        gather(0, 0, 0, C)
-        gather(0, 0, C, SLOTS)
+        gather(0, 0, (0, SLOTS), 0, SLOTS)
         round_pairs(0, 1)
-        gather(0, 1, 0, C)
-        weave(0, 0, P, nc.vector.tensor_copy)
-        weave(0, P, C, nc.vector.tensor_copy)
-        quantise(0, 0, P)
         warm_up(WARM); load_w2(1); load_w2_scales(1); load_gate(C, SLOTS); load_residual(0); load_residual(1)
-        quantise(0, P, C)
-        gather(0, 1, C, SLOTS)
+        gather(0, 1, (0, SLOTS), 0, SLOTS)
         round_pairs(1, 0)
+        weave(0, 0, 0, C, nc.scalar.copy)
+        gather_stepped(1, 0, 0, P)
+        quantise(0, 0, C)
         round_pairs(1, 1)
-        gather(1, 0, 0, C)
-        gather(1, 1, 0, P)
-        gather(1, 1, P, C)
-        weave(0, C, SLOTS, nc.scalar.copy)
-        weave(1, 0, P, nc.scalar.copy)
-        gather(1, 0, C, SLOTS)
-        weave(1, P, C, nc.scalar.copy)
+        gather(1, 0, (P, P), P, C)
+        gather_stepped(1, 1, 0, P)
+        gather(1, 1, (P, P), P, C)
+        weave(0, 0, C, SLOTS, nc.scalar.copy)
         quantise(1, 0, P)
+        gather(1, 0, (C, C), C, SLOTS)
+        weave(1, P, P, C, nc.scalar.copy, plain[1, C][:, C : 2 * C])
         quantise(1, P, C)
         quantise(0, C, SLOTS)
-        gather(1, 1, C, SLOTS)
-        weave(1, C, SLOTS, nc.vector.tensor_copy)
+        gather(1, 1, (C, C), C, SLOTS)
+        weave(1, C, C, SLOTS, nc.vector.tensor_copy)
         quantise(1, C, SLOTS)
 
         product(0, 0, 0, 0)

@@ -41,7 +41,7 @@ def tile_moe_res_glu_silu_kernel(
         offsets = keep.tile([P, SLOTS // 16], U16, name="offsets")
 
         def in_line(shape, dtype, name):
-            return ring.tile(shape, dtype, name=name, tag="line", bufs=50, align_bytes=64)
+            return ring.tile(shape, dtype, name=name, tag="line", bufs=52, align_bytes=64)
 
         warm = keep.tile([P, 1], F32, name="warm")
         nc.gpsimd.memset(warm[:], 0.0)
@@ -52,27 +52,28 @@ def tile_moe_res_glu_silu_kernel(
         for e in range(E):
             for m in range(2):
                 wsc[e, m] = keep.tile([P, PASSES, H], U8, name=f"wsc{e}{m}", align_bytes=64)
-                engine = nc.gpsimd if m == 0 else nc.vector
+                engine = nc.gpsimd if (e, m) == (0, 0) else nc.vector
                 engine.memset(wsc[e, m][:].rearrange("p s i -> p (s i)").bitcast(I32), 0)
-        for e in range(E):
-            w2sc[e] = keep.tile([P, PASSES, N], U8, name=f"w2sc{e}", align_bytes=64)
-            nc.gpsimd.memset(w2sc[e][:].rearrange("p s n -> p (s n)").bitcast(I32), 0)
         back = {}
         for n in range(NT):
             back[n] = keep.tile([P, T], F32, name=f"back{n}", align_bytes=64)
             nc.vector.memset(back[n][:], 0.0)
         ident = keep.tile([P, P], F32, name="ident")
         make_identity(nc, ident[:])
+        w2sc_all = keep.tile([P, E, PASSES, N], U8, name="w2sc", align_bytes=64)
+        nc.gpsimd.memset(w2sc_all[:].rearrange("p e s n -> p (e s n)").bitcast(I32), 0)
+        w2sc = [w2sc_all[:, e] for e in range(E)]
 
         def load_scales(e, m):
             rows = scales[m][e].rearrange("s (q r) i -> r q s i", r=4)
             for r in range(4):
                 nc.sync.dma_start(wsc[e, m][r:P:32].bitcast(I32), rows[r].bitcast(I32))
 
-        def load_w2_scales(e):
-            rows = w2_scales[e].rearrange("s (q r) n -> r q s n", r=4)
+        def load_w2_scales():
+            rows = w2_scales.rearrange("e s (q r) n -> r q (e s) n", r=4)
+            planes = w2sc_all[:].rearrange("p e s n -> p (e s) n")
             for r in range(4):
-                nc.sync.dma_start(w2sc[e][r:P:32].bitcast(I32), rows[r].bitcast(I32))
+                nc.gpsimd.dma_start(planes[r:P:32].bitcast(I32), rows[r].bitcast(I32))
 
         def load_w2(e):
             w2t[e] = keep.tile([P, PASSES, 2 * N], U8, name=f"w2t{e}", align_bytes=64)
@@ -186,7 +187,7 @@ def tile_moe_res_glu_silu_kernel(
                     lhsT=codes[:].bitcast(FP8X4),
                     lhsT_scale=plane[:],
                     rhs=codes[:].bitcast(U8).bitcast(FP4X4),
-                    rhs_scale=w2sc[1][:, 0, :],
+                    rhs_scale=wsc[1, 1][:, 0, 0:N],
                     start=True,
                     stop=True,
                 )
@@ -275,6 +276,7 @@ def tile_moe_res_glu_silu_kernel(
                 nc.vector.tensor_tensor(done[:, cols], back[n][:, cols], res_in[n][:, cols], ADD)
                 nc.sync.dma_start(out[n * P : (n + 1) * P, cols], done[:, cols])
 
+        load_w2_scales()
         load_x(0, 0)
         nc.sync.dma_start(offsets[:], offs)
         load_x(0, 1)
@@ -286,20 +288,14 @@ def tile_moe_res_glu_silu_kernel(
         load_scales(0, 1)
         load_words(0, 1, (0, 1), (0,))
         load_words(0, 1, (0, 1), (1,))
-        load_w2_scales(0)
         load_words(1, 0, (0, 1), (0,))
         load_scales(1, 0)
-        load_w2(0)
         load_words(1, 1, (0, 1), (0,))
-        load_scales(1, 1)
-        load_gate(0, C)
-        load_words(1, 0, (0, 1), (1,))
-        load_words(1, 1, (0, 1), (1,))
 
         round_pairs(0, 0)
         gather(0, 0, (0, SLOTS), 0, SLOTS)
         round_pairs(0, 1)
-        warm_up(WARM); load_w2(1); load_w2_scales(1); load_gate(C, SLOTS); load_residual(0); load_residual(1)
+        warm_up(WARM); load_scales(1, 1); load_w2(0); load_gate(0, C); load_words(1, 0, (0, 1), (1,)); load_words(1, 1, (0, 1), (1,)); load_w2(1); load_gate(C, SLOTS); load_residual(0); load_residual(1)
         gather(0, 1, (0, SLOTS), 0, SLOTS)
         round_pairs(1, 0)
         weave(0, 0, 0, C, nc.scalar.copy)
@@ -317,7 +313,6 @@ def tile_moe_res_glu_silu_kernel(
         quantise(0, C, SLOTS)
         gather(1, 1, (C, C), C, SLOTS)
         weave(1, C, C, SLOTS, nc.vector.tensor_copy)
-        quantise(1, C, SLOTS)
 
         product(0, 0, 0, 0)
         product(0, 1, 0, 0)
@@ -335,6 +330,7 @@ def tile_moe_res_glu_silu_kernel(
         both(0, 1, 1)
         hidden(0, 0)
         hidden(0, 1)
+        quantise(1, C, SLOTS)
         both(1, 0, 1)
         both(1, 1, 1)
         hidden(1, 0)
@@ -346,50 +342,55 @@ def tile_moe_res_glu_silu_kernel(
         requant(0, 0)
         requant(0, 1)
         both(2, 0, 0)
-        turn(1, (0, 1))
-        second_layer(0, (0,))
-        second_layer(0, (1,))
-        unturn(1, (0, 1))
-        copy_out(0, (0,))
-        both(3, 0, 0)
         silu(2, 0)
-        requant(1, 0)
-        put_back(0, 0)
         both(2, 0, 1)
         hidden(2, 0)
+        second_layer(0, (0,))
+        second_layer(0, (1,))
+        copy_out(0, (0,))
+        put_back(0, 0)
+        turn(1, (0, 1))
+        unturn(1, (0, 1))
+        requant(1, 0)
         copy_out(0, (1,))
         put_back(0, 1)
-        both(2, 1, 0)
+        both(3, 0, 0)
         silu(3, 0)
-        silu(2, 1)
-        both(3, 1, 0)
-        silu(3, 1)
-        both(2, 1, 1)
-        hidden(2, 1)
         both(3, 0, 1)
         hidden(3, 0)
+        both(2, 1, 0)
+        silu(2, 1)
+        both(2, 1, 1)
+        hidden(2, 1)
+        both(3, 1, 0)
+        silu(3, 1)
         both(3, 1, 1)
-        second_layer(1, (0,))
-        second_layer(1, (1,))
         hidden(3, 1)
+        second_layer(1, (0,))
         turn(2, (0, 1))
+        turn(3, (0,))
+        second_layer(1, (1,))
         copy_out(1, (0,))
-        unturn(2, (0, 1))
         put_back(1, 0)
-        turn(3, (0, 1))
+        unturn(2, (0, 1))
+        turn(3, (1,))
         requant(2, 0)
+        unturn(3, (0,))
+        unturn(3, (1,))
         copy_out(1, (1,))
+        requant(3, 0)
+        requant(3, 1)
         put_back(1, 1)
-        unturn(3, (0, 1))
         second_layer(2, (0,))
         second_layer(2, (1,))
-        requant(3, 0)
+        second_layer(3, (0,))
+        second_layer(3, (1,))
         copy_out(2, (0,))
         copy_out(2, (1,))
+        copy_out(3, (0,))
+        copy_out(3, (1,))
         put_back(2, 0)
         put_back(2, 1)
-        second_layer(3, (0, 1))
-        copy_out(3, (0, 1))
         put_back(3, 0)
         put_back(3, 1)
         finish(0)

@@ -26,7 +26,7 @@ UNITS = SLOTS // P
 NT = N // P
 STORES = (((0, 128), (128, 384), (384, T)), ((0, 512), (512, T)))
 VEC_TOKENS = (512, 512, 384, 448)
-WARM = 8
+WARM = 10
 
 
 def tile_moe_res_glu_silu_kernel(
@@ -52,28 +52,27 @@ def tile_moe_res_glu_silu_kernel(
         for e in range(E):
             for m in range(2):
                 wsc[e, m] = keep.tile([P, PASSES, H], U8, name=f"wsc{e}{m}", align_bytes=64)
-                engine = nc.gpsimd if (e, m) == (0, 0) else nc.vector
+                engine = nc.gpsimd if m == 0 else nc.vector
                 engine.memset(wsc[e, m][:].rearrange("p s i -> p (s i)").bitcast(I32), 0)
+        for e in range(E):
+            w2sc[e] = keep.tile([P, PASSES, N], U8, name=f"w2sc{e}", align_bytes=64)
+            nc.gpsimd.memset(w2sc[e][:].rearrange("p s n -> p (s n)").bitcast(I32), 0)
         back = {}
         for n in range(NT):
             back[n] = keep.tile([P, T], F32, name=f"back{n}", align_bytes=64)
             nc.vector.memset(back[n][:], 0.0)
         ident = keep.tile([P, P], F32, name="ident")
         make_identity(nc, ident[:])
-        w2sc_all = keep.tile([P, E, PASSES, N], U8, name="w2sc", align_bytes=64)
-        nc.gpsimd.memset(w2sc_all[:].rearrange("p e s n -> p (e s n)").bitcast(I32), 0)
-        w2sc = [w2sc_all[:, e] for e in range(E)]
 
         def load_scales(e, m):
             rows = scales[m][e].rearrange("s (q r) i -> r q s i", r=4)
             for r in range(4):
                 nc.sync.dma_start(wsc[e, m][r:P:32].bitcast(I32), rows[r].bitcast(I32))
 
-        def load_w2_scales():
-            rows = w2_scales.rearrange("e s (q r) n -> r q (e s) n", r=4)
-            planes = w2sc_all[:].rearrange("p e s n -> p (e s) n")
+        def load_w2_scales(e):
+            rows = w2_scales[e].rearrange("s (q r) n -> r q s n", r=4)
             for r in range(4):
-                nc.gpsimd.dma_start(planes[r:P:32].bitcast(I32), rows[r].bitcast(I32))
+                nc.sync.dma_start(w2sc[e][r:P:32].bitcast(I32), rows[r].bitcast(I32))
 
         def load_w2(e):
             w2t[e] = keep.tile([P, PASSES, 2 * N], U8, name=f"w2t{e}", align_bytes=64)
@@ -187,7 +186,7 @@ def tile_moe_res_glu_silu_kernel(
                     lhsT=codes[:].bitcast(FP8X4),
                     lhsT_scale=plane[:],
                     rhs=codes[:].bitcast(U8).bitcast(FP4X4),
-                    rhs_scale=wsc[1, 1][:, 0, 0:N],
+                    rhs_scale=w2sc[1][:, 0, :],
                     start=True,
                     stop=True,
                 )
@@ -276,11 +275,11 @@ def tile_moe_res_glu_silu_kernel(
                 nc.vector.tensor_tensor(done[:, cols], back[n][:, cols], res_in[n][:, cols], ADD)
                 nc.sync.dma_start(out[n * P : (n + 1) * P, cols], done[:, cols])
 
-        load_w2_scales()
         load_x(0, 0)
         nc.sync.dma_start(offsets[:], offs)
         load_x(0, 1)
         load_x(1, 0)
+        load_w2_scales(0)
         load_x(1, 1)
         load_scales(0, 0)
         load_words(0, 0, (0,), (0, 1))
@@ -291,11 +290,16 @@ def tile_moe_res_glu_silu_kernel(
         load_words(1, 0, (0, 1), (0,))
         load_scales(1, 0)
         load_words(1, 1, (0, 1), (0,))
+        load_scales(1, 1)
+        load_w2(0)
+        load_gate(0, C)
+        load_words(1, 0, (0, 1), (1,))
+        load_words(1, 1, (0, 1), (1,))
 
         round_pairs(0, 0)
         gather(0, 0, (0, SLOTS), 0, SLOTS)
         round_pairs(0, 1)
-        warm_up(WARM); load_scales(1, 1); load_w2(0); load_gate(0, C); load_words(1, 0, (0, 1), (1,)); load_words(1, 1, (0, 1), (1,)); load_w2(1); load_gate(C, SLOTS); load_residual(0); load_residual(1)
+        warm_up(WARM); load_w2(1); load_w2_scales(1); load_gate(C, SLOTS); load_residual(0); load_residual(1)
         gather(0, 1, (0, SLOTS), 0, SLOTS)
         round_pairs(1, 0)
         weave(0, 0, 0, C, nc.scalar.copy)

@@ -26,7 +26,7 @@ UNITS = SLOTS // P
 NT = N // P
 STORES = (((0, 128), (128, 384), (384, T)), ((0, 512), (512, T)))
 VEC_TOKENS = (512, 512, 384, 448)
-WARM = 10
+WARM = 13
 
 
 def tile_moe_res_glu_silu_kernel(
@@ -41,7 +41,7 @@ def tile_moe_res_glu_silu_kernel(
         offsets = keep.tile([P, SLOTS // 16], U16, name="offsets")
 
         def in_line(shape, dtype, name):
-            return ring.tile(shape, dtype, name=name, tag="line", bufs=52, align_bytes=64)
+            return ring.tile(shape, dtype, name=name, tag="line", bufs=50, align_bytes=64)
 
         warm = keep.tile([P, 1], F32, name="warm")
         nc.gpsimd.memset(warm[:], 0.0)
@@ -347,50 +347,53 @@ def tile_moe_res_glu_silu_kernel(
         requant(0, 1)
         both(2, 0, 0)
         silu(2, 0)
+        turn(1, (0,))
         both(2, 0, 1)
         hidden(2, 0)
         second_layer(0, (0,))
-        second_layer(0, (1,))
+        turn(1, (1,))
+        unturn(1, (0,))
         copy_out(0, (0,))
         put_back(0, 0)
-        turn(1, (0, 1))
-        unturn(1, (0, 1))
+        unturn(1, (1,))
         requant(1, 0)
-        copy_out(0, (1,))
-        put_back(0, 1)
+        requant(1, 1)
+        second_layer(0, (1,))
         both(3, 0, 0)
+        copy_out(0, (1,))
         silu(3, 0)
+        put_back(0, 1)
         both(3, 0, 1)
         hidden(3, 0)
         both(2, 1, 0)
         silu(2, 1)
+        second_layer(1, (0,))
         both(2, 1, 1)
         hidden(2, 1)
+        copy_out(1, (0,))
+        put_back(1, 0)
         both(3, 1, 0)
         silu(3, 1)
         both(3, 1, 1)
         hidden(3, 1)
-        second_layer(1, (0,))
         turn(2, (0, 1))
         turn(3, (0,))
         second_layer(1, (1,))
-        copy_out(1, (0,))
-        put_back(1, 0)
         unturn(2, (0, 1))
         turn(3, (1,))
-        requant(2, 0)
         unturn(3, (0,))
-        unturn(3, (1,))
-        copy_out(1, (1,))
+        requant(2, 0)
         requant(3, 0)
-        requant(3, 1)
+        copy_out(1, (1,))
         put_back(1, 1)
+        unturn(3, (1,))
         second_layer(2, (0,))
         second_layer(2, (1,))
-        second_layer(3, (0,))
-        second_layer(3, (1,))
+        requant(3, 1)
         copy_out(2, (0,))
         copy_out(2, (1,))
+        second_layer(3, (0,))
+        second_layer(3, (1,))
         copy_out(3, (0,))
         copy_out(3, (1,))
         put_back(2, 0)

@@ -105,6 +105,12 @@ def tile_moe_res_glu_silu_kernel(
             for j in range(first // P, last // P):
                 gates[j] = piece[:, j * P - first : (j + 1) * P - first]
 
+        def load_residuals():
+            both_tiles = keep.tile([P, NT, T], F32, name="res")
+            nc.sync.dma_start(both_tiles[:], xr.rearrange("(n p) t -> p n t", p=P))
+            for n in range(NT):
+                res_in[n] = both_tiles[:, n, :]
+
         def load_residual(n):
             res_in[n] = keep.tile([P, T], F32, name=f"res_in{n}")
             nc.sync.dma_start(res_in[n][:], xr[n * P : (n + 1) * P, :])
@@ -376,13 +382,16 @@ def tile_moe_res_glu_silu_kernel(
         silu(3, 1)
         both(3, 1, 1)
         hidden(3, 1)
-        turn(2, (0, 1))
+        turn(2, (0,))
+        turn(2, (1,))
         turn(3, (0,))
         second_layer(1, (1,))
-        unturn(2, (0, 1))
+        unturn(2, (0,))
+        unturn(2, (1,))
         turn(3, (1,))
         unturn(3, (0,))
         requant(2, 0)
+        requant(2, 1)
         requant(3, 0)
         copy_out(1, (1,))
         put_back(1, 1)

@@ -64,9 +64,9 @@ def tile_moe_res_glu_silu_kernel(
         ident = keep.tile([P, P], F32, name="ident")
         make_identity(nc, ident[:])
 
-        def load_scales(e, m):
+        def load_scales(e, m, first=0, last=4):
             rows = scales[m][e].rearrange("s (q r) i -> r q s i", r=4)
-            for r in range(4):
+            for r in range(first, last):
                 nc.sync.dma_start(wsc[e, m][r:P:32].bitcast(I32), rows[r].bitcast(I32))
 
         def load_w2_scales(e):
@@ -293,10 +293,12 @@ def tile_moe_res_glu_silu_kernel(
         load_scales(0, 1)
         load_words(0, 1, (0, 1), (0,))
         load_words(0, 1, (0, 1), (1,))
+        load_scales(1, 0, 0, 2)
         load_words(1, 0, (0, 1), (0,))
-        load_scales(1, 0)
+        load_scales(1, 0, 2, 4)
+        load_scales(1, 1, 0, 1)
         load_words(1, 1, (0, 1), (0,))
-        load_scales(1, 1)
+        load_scales(1, 1, 1, 4)
         load_w2(0)
         load_gate(0, C)
         load_words(1, 0, (0, 1), (1,))
@@ -353,18 +355,18 @@ def tile_moe_res_glu_silu_kernel(
         requant(0, 1)
         both(2, 0, 0)
         silu(2, 0)
-        turn(1, (0,))
         both(2, 0, 1)
         hidden(2, 0)
         second_layer(0, (0,))
-        turn(1, (1,))
-        unturn(1, (0,))
+        second_layer(0, (1,))
         copy_out(0, (0,))
         put_back(0, 0)
+        turn(1, (0,))
+        turn(1, (1,))
+        unturn(1, (0,))
         unturn(1, (1,))
         requant(1, 0)
         requant(1, 1)
-        second_layer(0, (1,))
         both(3, 0, 0)
         copy_out(0, (1,))
         silu(3, 0)

@@ -24,7 +24,7 @@ PASSES = K // KP
 G = H // KP
 UNITS = SLOTS // P
 NT = N // P
-STORES = (((0, 128), (128, 384), (384, T)), ((0, 512), (512, T)))
+STORES = (((0, 192), (192, 448), (448, T)), ((0, 448), (448, T)))
 VEC_TOKENS = (512, 512, 384, 448)
 WARM = 13
 
@@ -293,9 +293,9 @@ def tile_moe_res_glu_silu_kernel(
         load_scales(0, 1)
         load_words(0, 1, (0, 1), (0,))
         load_words(0, 1, (0, 1), (1,))
-        load_scales(1, 0, 0, 2)
+        load_scales(1, 0, 0, 3)
         load_words(1, 0, (0, 1), (0,))
-        load_scales(1, 0, 2, 4)
+        load_scales(1, 0, 3, 4)
         load_scales(1, 1, 0, 1)
         load_words(1, 1, (0, 1), (0,))
         load_scales(1, 1, 1, 4)
@@ -361,22 +361,25 @@ def tile_moe_res_glu_silu_kernel(
         second_layer(0, (1,))
         copy_out(0, (0,))
         put_back(0, 0)
+        both(3, 0, 0)
+        copy_out(0, (1,))
+        put_back(0, 1)
+        silu(3, 0)
         turn(1, (0,))
         turn(1, (1,))
+        turn(2, (0,))
         unturn(1, (0,))
         unturn(1, (1,))
         requant(1, 0)
         requant(1, 1)
-        both(3, 0, 0)
-        copy_out(0, (1,))
-        silu(3, 0)
-        put_back(0, 1)
-        both(3, 0, 1)
-        hidden(3, 0)
         both(2, 1, 0)
+        unturn(2, (0,))
         silu(2, 1)
-        second_layer(1, (0,))
+        both(3, 0, 1)
+        requant(2, 0)
+        hidden(3, 0)
         both(2, 1, 1)
+        second_layer(1, (0,))
         hidden(2, 1)
         copy_out(1, (0,))
         put_back(1, 0)
@@ -384,15 +387,12 @@ def tile_moe_res_glu_silu_kernel(
         silu(3, 1)
         both(3, 1, 1)
         hidden(3, 1)
-        turn(2, (0,))
         turn(2, (1,))
         turn(3, (0,))
         second_layer(1, (1,))
-        unturn(2, (0,))
         unturn(2, (1,))
         turn(3, (1,))
         unturn(3, (0,))
-        requant(2, 0)
         requant(2, 1)
         requant(3, 0)
         copy_out(1, (1,))

@@ -227,11 +227,11 @@ def tile_moe_res_glu_silu_kernel(
                     nc.tensor.transpose(turned[:, g - g0, u, :], hw[:, u * P : (u + 1) * P], ident[:])
             pending[j, g0, "turned"] = turned
 
-        def unturn(j, halves):
+        def unturn(j, halves, copy=nc.scalar.copy):
             count, g0 = len(halves), halves[0]
             turned = pending[j, g0, "turned"]
             hq_in = in_line([P, count, P, 4], BF16, "hq_in")
-            nc.scalar.copy(
+            copy(
                 hq_in[:].rearrange("p g r t -> p (g r t)").bitcast(F32).rearrange("p (g r u) -> p g r u", g=count, u=2),
                 turned[:].rearrange("p g u r -> p g r u"),
             )
@@ -264,6 +264,35 @@ def tile_moe_res_glu_silu_kernel(
                         stop=(g == G - 1),
                     )
             pending[j, tiles] = y
+
+        def second_layers(j):
+            e = j * P // C
+            for g in range(G):
+                for n in range(NT):
+                    if g == 0:
+                        pending[j, (n,)] = psum.tile([P, 1, P], F32, name="y", tag="bank")
+                    nc.tensor.matmul_mx(
+                        out=pending[j, (n,)][:, 0, :],
+                        lhsT=w2t[e][:, g, 2 * P * n : 2 * P * (n + 1)].bitcast(FP4X4),
+                        lhsT_scale=w2sc[e][:, g, P * n : P * (n + 1)],
+                        rhs=hq[j, g].bitcast(FP8X4),
+                        rhs_scale=hs[j, g],
+                        start=(g == 0),
+                        stop=(g == G - 1),
+                    )
+
+        def silu_part(j, g, u):
+            act[j, g, u] = in_line([P, P, 2], F32, "act")
+            nc.scalar.activation(
+                act[j, g, u][:], acc[j, g, 0][:].rearrange("r (p u e) -> r u p e", u=2, e=2)[:, u], SILU
+            )
+
+        def hidden_part(j, g, u):
+            if u == 0:
+                h[j, g] = in_line([P, 2, P, 2], BF16, "h")
+            nc.vector.tensor_tensor(
+                h[j, g][:, u], act[j, g, u][:], acc[j, g, 1][:].rearrange("r (p u e) -> r u p e", u=2, e=2)[:, u], MULT
+            )
 
         def copy_out(j, tiles):
             y_sb = in_line([P, len(tiles), P], F32, "y_sb")
@@ -346,19 +375,20 @@ def tile_moe_res_glu_silu_kernel(
         both(1, 0, 1)
         both(1, 1, 1)
         hidden(1, 0)
-        hidden(1, 1)
         turn(0, (0,))
         turn(0, (1,))
         unturn(0, (0,))
-        unturn(0, (1,))
+        unturn(0, (1,), nc.vector.tensor_copy)
         requant(0, 0)
         requant(0, 1)
+        hidden(1, 1)
         both(2, 0, 0)
-        silu(2, 0)
+        silu_part(2, 0, 0)
+        silu_part(2, 0, 1)
         both(2, 0, 1)
-        hidden(2, 0)
-        second_layer(0, (0,))
-        second_layer(0, (1,))
+        hidden_part(2, 0, 0)
+        hidden_part(2, 0, 1)
+        second_layers(0)
         copy_out(0, (0,))
         put_back(0, 0)
         both(3, 0, 0)

@@ -24,7 +24,7 @@ PASSES = K // KP
 G = H // KP
 UNITS = SLOTS // P
 NT = N // P
-STORES = (((0, 192), (192, 448), (448, T)), ((0, 448), (448, T)))
+STORES = (((0, 192), (192, 448), (448, 768)), ((0, 384), (384, 768)))
 VEC_TOKENS = (512, 512, 384, 448)
 WARM = 13
 

@@ -25,7 +25,7 @@ G = H // KP
 UNITS = SLOTS // P
 NT = N // P
 STORES = (((0, 192), (192, 448), (448, 768)), ((0, 384), (384, 768)))
-VEC_TOKENS = (512, 512, 384, 448)
+VEC_TOKENS = (512, 512, 384, 384)
 WARM = 13
 
 
@@ -343,16 +343,15 @@ def tile_moe_res_glu_silu_kernel(
         gather_stepped(1, 0, 0, P)
         quantise(0, 0, C)
         round_pairs(1, 1)
-        gather(1, 0, (P, P), P, C)
+        gather_stepped(1, 0, P, C)
         gather_stepped(1, 1, 0, P)
-        gather(1, 1, (P, P), P, C)
+        gather_stepped(1, 1, P, C)
         weave(0, 0, C, SLOTS, nc.scalar.copy)
         quantise(1, 0, P)
-        gather(1, 0, (C, C), C, SLOTS)
-        weave(1, P, P, C, nc.scalar.copy, plain[1, C][:, C : 2 * C])
         quantise(1, P, C)
-        quantise(0, C, SLOTS)
+        gather(1, 0, (C, C), C, SLOTS)
         gather(1, 1, (C, C), C, SLOTS)
+        quantise(0, C, SLOTS)
         weave(1, C, C, SLOTS, nc.vector.tensor_copy)
 
         product(0, 0, 0, 0)

@@ -25,7 +25,7 @@ G = H // KP
 UNITS = SLOTS // P
 NT = N // P
 STORES = (((0, 192), (192, 448), (448, 768)), ((0, 384), (384, 768)))
-VEC_TOKENS = (512, 512, 384, 384)
+VEC_TOKENS = (512, 384, 384, 384)
 WARM = 13
 
 
@@ -139,9 +139,9 @@ def tile_moe_res_glu_silu_kernel(
                 tables[s, u].indirect(offsets[:, first // 16 : last // 16]),
             )
 
-        def gather_stepped(s, u, first, last):
+        def gather_stepped(s, u, first, last, into=None):
             if u == 0:
-                grouped[s, first] = in_line([P, 2 * (last - first)], U32, "grouped")[:]
+                grouped[s, first] = in_line([P, 2 * (last - first)], U32, "grouped")[:] if into is None else into
             nc.vector.tensor_copy(
                 grouped[s, first].rearrange("p (r u) -> p r u", u=2)[:, :, u],
                 tables[s, u].indirect(offsets[:, first // 16 : last // 16]),
@@ -157,10 +157,11 @@ def tile_moe_res_glu_silu_kernel(
                 both_rows[:, first - start : last - start, :],
             )
 
-        def quantise(s, first, last):
+        def quantise(s, first, last, start=None):
+            start = first if start is None else start
             codes = in_line([P, last - first], U32, "codes")
             plane = keep.tile([P, last - first], U8, name=f"xs{s}{first}", align_bytes=64)
-            nc.vector.quantize_mx(out=codes[:].bitcast(FP8X4), scales=plane[:], in_=grouped[s, first].bitcast(BF16))
+            nc.vector.quantize_mx(out=codes[:].bitcast(FP8X4), scales=plane[:], in_=grouped[s, start][:, 2 * (first - start) : 2 * (last - start)].bitcast(BF16))
             for j in range(first // P, last // P):
                 xq[s, j] = codes[:, j * P - first : (j + 1) * P - first]
                 xs[s, j] = plane[:, j * P - first : (j + 1) * P - first]

@@ -43,9 +43,6 @@ def tile_moe_res_glu_silu_kernel(
         def in_line(shape, dtype, name):
             return ring.tile(shape, dtype, name=name, tag="line", bufs=50, align_bytes=64)
 
-        warm = keep.tile([P, 1], F32, name="warm")
-        nc.gpsimd.memset(warm[:], 0.0)
-        nc.scalar.activation(warm[:], warm[:], SILU)
         words = (w1_words, w3_words)
         scales = (w1_scales, w3_scales)
         wsc, w2sc, w2t, wt = {}, {}, {}, {}

@@ -22,11 +22,14 @@ P = 128
 KP = 512
 PASSES = K // KP
 G = H // KP
-UNITS = SLOTS // P
 NT = N // P
-STORES = (((0, 192), (192, 448), (448, 768)), ((0, 384), (384, 768)))
-VEC_TOKENS = (512, 384, 384, 384)
-WARM = 13
+W1, W3 = 0, 1
+
+VECTOR_TOKENS_FIRST = 2 * T // 3
+VECTOR_TOKENS = T // 2
+SPARE_PRODUCTS = 13
+CUTS = ((0, 192, 448, T), (0, T // 2, T))
+LINE_SLOTS = 50
 
 
 def tile_moe_res_glu_silu_kernel(
@@ -38,153 +41,112 @@ def tile_moe_res_glu_silu_kernel(
         ring = ctx.enter_context(tc.tile_pool(name="ring", bufs=2))
         psum = ctx.enter_context(tc.psum_pool(name="psum", bufs=8))
 
+        def in_line(shape, dtype, name):
+            return ring.tile(shape, dtype, name=name, tag="line", bufs=LINE_SLOTS, align_bytes=64)
+
+        def bank(shape, name):
+            return psum.tile(shape, F32, name=name, tag="bank")
+
         offsets = keep.tile([P, SLOTS // 16], U16, name="offsets")
 
-        def in_line(shape, dtype, name):
-            return ring.tile(shape, dtype, name=name, tag="line", bufs=50, align_bytes=64)
+        def listed(first, last):
+            return offsets[:, first // 16 : last // 16]
 
-        words = (w1_words, w3_words)
-        scales = (w1_scales, w3_scales)
-        wsc, w2sc, w2t, wt = {}, {}, {}, {}
+        words, scales = (w1_words, w3_words), (w1_scales, w3_scales)
+        wsc, w2sc, back = {}, {}, {}
         for e in range(E):
-            for m in range(2):
+            for m in (W1, W3):
                 wsc[e, m] = keep.tile([P, PASSES, H], U8, name=f"wsc{e}{m}", align_bytes=64)
-                engine = nc.gpsimd if m == 0 else nc.vector
+                engine = nc.gpsimd if m == W1 else nc.vector
                 engine.memset(wsc[e, m][:].rearrange("p s i -> p (s i)").bitcast(I32), 0)
         for e in range(E):
             w2sc[e] = keep.tile([P, PASSES, N], U8, name=f"w2sc{e}", align_bytes=64)
             nc.gpsimd.memset(w2sc[e][:].rearrange("p s n -> p (s n)").bitcast(I32), 0)
-        back = {}
         for n in range(NT):
             back[n] = keep.tile([P, T], F32, name=f"back{n}", align_bytes=64)
             nc.vector.memset(back[n][:], 0.0)
         ident = keep.tile([P, P], F32, name="ident")
         make_identity(nc, ident[:])
 
-        def load_scales(e, m, first=0, last=4):
-            rows = scales[m][e].rearrange("s (q r) i -> r q s i", r=4)
-            for r in range(first, last):
-                nc.sync.dma_start(wsc[e, m][r:P:32].bitcast(I32), rows[r].bitcast(I32))
+        raw, wt, w2t, gates, residual = {}, {}, {}, {}, {}
+        pieces = xT.rearrange("(s p u d) w -> s u p d w", s=PASSES, p=P, u=2)
 
-        def load_w2_scales(e):
-            rows = w2_scales[e].rearrange("s (q r) n -> r q s n", r=4)
-            for r in range(4):
-                nc.sync.dma_start(w2sc[e][r:P:32].bitcast(I32), rows[r].bitcast(I32))
+        def load_x(s, u):
+            raw[s, u] = keep.tile([P, 2, T], F32, name=f"raw{s}{u}", align_bytes=64)
+            nc.sync.dma_start(raw[s, u][:], pieces[s, u])
+
+        def load_rows(plane, source, rows):
+            by_row = source.rearrange("s (q r) i -> r q s i", r=4)
+            for r in rows:
+                nc.sync.dma_start(plane[r:P:32].bitcast(I32), by_row[r].bitcast(I32))
+
+        def load_pass(e, m, s):
+            piece = keep.tile([P, 2 * H], U8, name=f"wp{e}{m}{s}", align_bytes=64)
+            nc.sync.dma_start(piece[:].bitcast(I32), words[m][e, s].bitcast(I32))
+            for g in range(G):
+                wt[e, m, s, g] = piece[:, 2 * KP * g : 2 * KP * (g + 1)]
+
+        def load_half(e, m, g):
+            piece = keep.tile([P, PASSES, 2 * KP], U8, name=f"wh{e}{m}{g}", align_bytes=64)
+            source = words[m][e].rearrange("s p b -> p s b")[:, :, 2 * KP * g : 2 * KP * (g + 1)]
+            nc.sync.dma_start(piece[:].bitcast(I32), source.bitcast(I32))
+            for s in range(PASSES):
+                wt[e, m, s, g] = piece[:, s, :]
 
         def load_w2(e):
             w2t[e] = keep.tile([P, PASSES, 2 * N], U8, name=f"w2t{e}", align_bytes=64)
             nc.sync.dma_start(w2t[e][:].bitcast(I32), w2_words[e].rearrange("s p b -> p s b").bitcast(I32))
 
-        xview = xT.rearrange("(s p u d) w -> s u p d w", s=PASSES, p=P, u=2)
-        raw = {}
-
-        def load_x(s, u, first=0, last=T):
-            if first == 0:
-                raw[s, u] = keep.tile([P, 2, T], F32, name=f"raw{s}{u}", align_bytes=64)
-            nc.sync.dma_start(raw[s, u][:, :, first:last], xview[s, u][:, :, first:last])
-
-        def load_words(e, m, passes, halves):
-            piece = keep.tile(
-                [P, len(passes), len(halves) * 2 * KP], U8, name=f"wt{e}{m}{passes[0]}{halves[0]}", align_bytes=64
-            )
-            source = words[m][e].rearrange("s p b -> p s b")
-            cols = slice(halves[0] * 2 * KP, (halves[-1] + 1) * 2 * KP)
-            nc.sync.dma_start(piece[:].bitcast(I32), source[:, passes[0] : passes[-1] + 1, cols].bitcast(I32))
-            for s in passes:
-                for g in halves:
-                    wt[e, m, s, g] = piece[:, s - passes[0], (g - halves[0]) * 2 * KP : (g - halves[0] + 1) * 2 * KP]
-
-        gates, res_in = {}, {}
-
-        def load_gate(first, last):
-            piece = keep.tile([P, last - first], F32, name=f"gates{first}")
-            nc.sync.dma_start(piece[:], gate[0:P, first:last])
-            for j in range(first // P, last // P):
-                gates[j] = piece[:, j * P - first : (j + 1) * P - first]
-
-        def load_residuals():
-            both_tiles = keep.tile([P, NT, T], F32, name="res")
-            nc.sync.dma_start(both_tiles[:], xr.rearrange("(n p) t -> p n t", p=P))
-            for n in range(NT):
-                res_in[n] = both_tiles[:, n, :]
+        def load_gate(e):
+            piece = keep.tile([P, C], F32, name=f"gate{e}")
+            nc.sync.dma_start(piece[:], gate[0:P, e * C : (e + 1) * C])
+            for c in range(C // P):
+                gates[e * C // P + c] = piece[:, c * P : (c + 1) * P]
 
         def load_residual(n):
-            res_in[n] = keep.tile([P, T], F32, name=f"res_in{n}")
-            nc.sync.dma_start(res_in[n][:], xr[n * P : (n + 1) * P, :])
+            residual[n] = keep.tile([P, T], F32, name=f"residual{n}")
+            nc.sync.dma_start(residual[n][:], xr[n * P : (n + 1) * P, :])
 
-        tables, plain, grouped, xq, xs = {}, {}, {}, {}, {}
+        tables, quads, xq, xs = {}, {}, {}, {}
 
-        def round_pairs(s, u):
+        def round_pairs(s, u, vector_tokens):
             pairs = in_line([P, T, 2], BF16, "pairs")
             tables[s, u] = pairs[:].rearrange("p w d -> p (w d)").bitcast(U32)
-            src = raw[s, u][:].rearrange("p d w -> p w d")
-            v = T - VEC_TOKENS[2 * s + u]
-            if v > 0:
-                nc.scalar.copy(pairs[:, 0:v, :], src[:, 0:v, :])
-            if v < T:
-                nc.vector.tensor_copy(pairs[:, v:T, :], src[:, v:T, :])
+            rows = raw[s, u][:].rearrange("p d w -> p w d")
+            cut = T - vector_tokens
+            nc.scalar.copy(pairs[:, 0:cut, :], rows[:, 0:cut, :])
+            nc.vector.tensor_copy(pairs[:, cut:T, :], rows[:, cut:T, :])
 
-        def gather(s, u, key, first, last):
-            start, width = key
-            if (s, start) not in plain:
-                if width == SLOTS:
-                    plain[s, start] = keep.tile([P, 2 * width], U32, name="plain_all", align_bytes=64)
-                else:
-                    plain[s, start] = in_line([P, 2 * width], U32, "plain")
-            nc.vector.tensor_copy(
-                plain[s, start][:, u * width + first - start : u * width + last - start],
-                tables[s, u].indirect(offsets[:, first // 16 : last // 16]),
-            )
+        def gather(planes, s, u, first, last):
+            nc.vector.tensor_copy(planes[:, u, :], tables[s, u].indirect(listed(first, last)))
 
-        def gather_stepped(s, u, first, last, into=None):
+        def gather_at_a_step(s, u, j):
             if u == 0:
-                grouped[s, first] = in_line([P, 2 * (last - first)], U32, "grouped")[:] if into is None else into
-            nc.vector.tensor_copy(
-                grouped[s, first].rearrange("p (r u) -> p r u", u=2)[:, :, u],
-                tables[s, u].indirect(offsets[:, first // 16 : last // 16]),
-            )
+                quads[s, j * P] = in_line([P, P, 2], U32, "quads")
+            nc.vector.tensor_copy(quads[s, j * P][:, :, u], tables[s, u].indirect(listed(j * P, (j + 1) * P)))
 
-        def weave(s, start, first, last, copy, into=None):
-            if into is None:
-                into = in_line([P, 2 * (last - first)], U32, "woven")[:]
-            grouped[s, first] = into
-            both_rows = plain[s, start][:].bitcast(F32).rearrange("p (u r) -> p r u", u=2)
-            copy(
-                into.bitcast(F32).rearrange("p (r u) -> p r u", u=2),
-                both_rows[:, first - start : last - start, :],
-            )
+        def weave(s, first, planes, copy):
+            quads[s, first] = in_line([P, C, 2], U32, "quads")
+            copy(quads[s, first][:].bitcast(F32), planes.bitcast(F32).rearrange("p u r -> p r u"))
 
-        def quantise(s, first, last, start=None):
-            start = first if start is None else start
+        def quantise(s, first, last):
             codes = in_line([P, last - first], U32, "codes")
             plane = keep.tile([P, last - first], U8, name=f"xs{s}{first}", align_bytes=64)
-            nc.vector.quantize_mx(out=codes[:].bitcast(FP8X4), scales=plane[:], in_=grouped[s, start][:, 2 * (first - start) : 2 * (last - start)].bitcast(BF16))
+            nc.vector.quantize_mx(
+                out=codes[:].bitcast(FP8X4),
+                scales=plane[:],
+                in_=quads[s, first][:].rearrange("p r u -> p (r u)").bitcast(BF16),
+            )
             for j in range(first // P, last // P):
                 xq[s, j] = codes[:, j * P - first : (j + 1) * P - first]
                 xs[s, j] = plane[:, j * P - first : (j + 1) * P - first]
 
-        acc, act, h, hq, hs, ysb, pending = {}, {}, {}, {}, {}, {}, {}
-
-        def product(j, g, m, s):
-            e = j * P // C
-            if s == 0:
-                acc[j, g, m] = psum.tile([P, KP], F32, name="acc", tag="bank")
-            nc.tensor.matmul_mx(
-                out=acc[j, g, m][:],
-                lhsT=xq[s, j].bitcast(FP8X4),
-                lhsT_scale=xs[s, j],
-                rhs=wt[e, m, s, g].bitcast(FP4X4),
-                rhs_scale=wsc[e, m][:, s, g * KP : (g + 1) * KP],
-                start=(s == 0),
-                stop=(s == PASSES - 1),
-            )
-
-        def warm_up(count):
+        def warm_up():
             codes = in_line([P, P], U32, "zero_codes")
             plane = keep.tile([P, P], U8, name="zero_plane", align_bytes=64)
             nc.vector.quantize_mx(out=codes[:].bitcast(FP8X4), scales=plane[:], in_=back[1][:, 0:N].bitcast(BF16))
-            spare = psum.tile([P, N], F32, name="spare", tag="bank")
-            for i in range(count):
+            spare = bank([P, N], "spare")
+            for _ in range(SPARE_PRODUCTS):
                 nc.tensor.matmul_mx(
                     out=spare[:],
                     lhsT=codes[:].bitcast(FP8X4),
@@ -195,248 +157,225 @@ def tile_moe_res_glu_silu_kernel(
                     stop=True,
                 )
 
-        def both(j, g, m):
+        acc, act, h = {}, {}, {}
+
+        def product(j, g, m, s):
+            e = j * P // C
+            if s == 0:
+                acc[j, g, m] = bank([P, KP], "acc")
+            nc.tensor.matmul_mx(
+                out=acc[j, g, m][:],
+                lhsT=xq[s, j].bitcast(FP8X4),
+                lhsT_scale=xs[s, j],
+                rhs=wt[e, m, s, g].bitcast(FP4X4),
+                rhs_scale=wsc[e, m][:, s, g * KP : (g + 1) * KP],
+                start=(s == 0),
+                stop=(s == PASSES - 1),
+            )
+
+        def both_passes(j, g, m):
             for s in range(PASSES):
                 product(j, g, m, s)
 
-        def silu(j, g):
-            act[j, g] = in_line([P, KP], F32, "act")
-            nc.scalar.activation(
-                act[j, g][:].rearrange("r (u p e) -> r u p e", u=2, e=2),
-                acc[j, g, 0][:].rearrange("r (p u e) -> r u p e", u=2, e=2),
-                SILU,
-            )
+        def by_pairs(j, g, m):
+            return acc[j, g, m][:].rearrange("r (p u e) -> r u p e", u=2, e=2)
 
-        def hidden(j, g):
+        def silu(j, g, parts=(slice(0, 2),)):
+            for part in parts:
+                act[j, g, part.start] = in_line([P, part.stop - part.start, P, 2], F32, "act")
+                nc.scalar.activation(act[j, g, part.start][:], by_pairs(j, g, W1)[:, part], SILU)
+
+        def hidden(j, g, parts=(slice(0, 2),)):
             h[j, g] = in_line([P, 2, P, 2], BF16, "h")
-            nc.vector.tensor_tensor(
-                h[j, g][:],
-                act[j, g][:].rearrange("r (u p e) -> r u p e", u=2, e=2),
-                acc[j, g, 1][:].rearrange("r (p u e) -> r u p e", u=2, e=2),
-                MULT,
-            )
+            for part in parts:
+                nc.vector.tensor_tensor(h[j, g][:, part], act[j, g, part.start][:], by_pairs(j, g, W3)[:, part], MULT)
 
-        def turn(j, halves):
-            count, g0 = len(halves), halves[0]
-            turned = psum.tile([P, count, 2, P], F32, name="turned", tag="bank")
-            for g in halves:
-                hw = h[j, g][:].rearrange("r u p e -> r (u p e)").bitcast(F32)
-                for u in range(2):
-                    nc.tensor.transpose(turned[:, g - g0, u, :], hw[:, u * P : (u + 1) * P], ident[:])
-            pending[j, g0, "turned"] = turned
+        turned, h_quads, hq, hs, y, y_sb = {}, {}, {}, {}, {}, {}
 
-        def unturn(j, halves, copy=nc.scalar.copy):
-            count, g0 = len(halves), halves[0]
-            turned = pending[j, g0, "turned"]
-            hq_in = in_line([P, count, P, 4], BF16, "hq_in")
+        def turn(j, g):
+            turned[j, g] = bank([P, 2, P], "turned")
+            pairs = h[j, g][:].rearrange("r u p e -> r (u p e)").bitcast(F32)
+            for u in range(2):
+                nc.tensor.transpose(turned[j, g][:, u, :], pairs[:, u * P : (u + 1) * P], ident[:])
+
+        def leave_psum(j, g, copy=nc.scalar.copy):
+            h_quads[j, g] = in_line([P, 4 * P], BF16, "h_quads")
             copy(
-                hq_in[:].rearrange("p g r t -> p (g r t)").bitcast(F32).rearrange("p (g r u) -> p g r u", g=count, u=2),
-                turned[:].rearrange("p g u r -> p g r u"),
+                h_quads[j, g][:].bitcast(F32).rearrange("p (r u) -> p r u", u=2),
+                turned[j, g][:].rearrange("p u r -> p r u"),
             )
-            pending[j, g0] = (hq_in, halves)
 
-        def requant(j, g0):
-            hq_in, halves = pending[j, g0]
-            codes = in_line([P, len(halves), P], U32, "hq")
-            plane = keep.tile([P, len(halves), P], U8, name=f"hs{j}{g0}", align_bytes=64)
-            nc.vector.quantize_mx(
-                out=codes[:].rearrange("p g r -> p (g r)").bitcast(FP8X4),
-                scales=plane[:].rearrange("p g r -> p (g r)"),
-                in_=hq_in[:].rearrange("p g r t -> p (g r t)"),
+        def quantise_h(j, g):
+            hq[j, g] = in_line([P, P], U32, "hq")
+            hs[j, g] = keep.tile([P, P], U8, name=f"hs{j}{g}", align_bytes=64)
+            nc.vector.quantize_mx(out=hq[j, g][:].bitcast(FP8X4), scales=hs[j, g][:], in_=h_quads[j, g][:])
+
+        def second_product(j, n, g):
+            e = j * P // C
+            if g == 0:
+                y[j, n] = bank([P, P], "y")
+            nc.tensor.matmul_mx(
+                out=y[j, n][:],
+                lhsT=w2t[e][:, g, 2 * P * n : 2 * P * (n + 1)].bitcast(FP4X4),
+                lhsT_scale=w2sc[e][:, g, P * n : P * (n + 1)],
+                rhs=hq[j, g][:].bitcast(FP8X4),
+                rhs_scale=hs[j, g][:],
+                start=(g == 0),
+                stop=(g == G - 1),
             )
-            for g in halves:
-                hq[j, g], hs[j, g] = codes[:, g - g0, :], plane[:, g - g0, :]
 
-        def second_layer(j, tiles):
-            e = j * P // C
-            y = psum.tile([P, len(tiles), P], F32, name="y", tag="bank")
-            for i, n in enumerate(tiles):
-                for g in range(G):
-                    nc.tensor.matmul_mx(
-                        out=y[:, i, :],
-                        lhsT=w2t[e][:, g, 2 * P * n : 2 * P * (n + 1)].bitcast(FP4X4),
-                        lhsT_scale=w2sc[e][:, g, P * n : P * (n + 1)],
-                        rhs=hq[j, g].bitcast(FP8X4),
-                        rhs_scale=hs[j, g],
-                        start=(g == 0),
-                        stop=(g == G - 1),
-                    )
-            pending[j, tiles] = y
-
-        def second_layers(j):
-            e = j * P // C
+        def second_layer(j, n):
             for g in range(G):
-                for n in range(NT):
-                    if g == 0:
-                        pending[j, (n,)] = psum.tile([P, 1, P], F32, name="y", tag="bank")
-                    nc.tensor.matmul_mx(
-                        out=pending[j, (n,)][:, 0, :],
-                        lhsT=w2t[e][:, g, 2 * P * n : 2 * P * (n + 1)].bitcast(FP4X4),
-                        lhsT_scale=w2sc[e][:, g, P * n : P * (n + 1)],
-                        rhs=hq[j, g].bitcast(FP8X4),
-                        rhs_scale=hs[j, g],
-                        start=(g == 0),
-                        stop=(g == G - 1),
-                    )
+                second_product(j, n, g)
 
-        def silu_part(j, g, u):
-            act[j, g, u] = in_line([P, P, 2], F32, "act")
-            nc.scalar.activation(
-                act[j, g, u][:], acc[j, g, 0][:].rearrange("r (p u e) -> r u p e", u=2, e=2)[:, u], SILU
-            )
-
-        def hidden_part(j, g, u):
-            if u == 0:
-                h[j, g] = in_line([P, 2, P, 2], BF16, "h")
-            nc.vector.tensor_tensor(
-                h[j, g][:, u], act[j, g, u][:], acc[j, g, 1][:].rearrange("r (p u e) -> r u p e", u=2, e=2)[:, u], MULT
-            )
-
-        def copy_out(j, tiles):
-            y_sb = in_line([P, len(tiles), P], F32, "y_sb")
-            nc.scalar.copy(y_sb[:], pending[j, tiles][:])
-            for i, n in enumerate(tiles):
-                ysb[j, n] = y_sb[:, i, :]
+        def copy_y(j, n):
+            y_sb[j, n] = in_line([P, P], F32, "y_sb")
+            nc.scalar.copy(y_sb[j, n][:], y[j, n][:])
 
         def put_back(j, n):
-            nc.vector.tensor_tensor(back[n][:].indirect(offsets[:, j * P // 16 : (j + 1) * P // 16]), ysb[j, n], gates[j], MULT)
+            nc.vector.tensor_tensor(back[n][:].indirect(listed(j * P, (j + 1) * P)), y_sb[j, n][:], gates[j], MULT)
 
         def finish(n):
             done = keep.tile([P, T], F32, name=f"done{n}")
-            for first, last in STORES[n]:
+            for first, last in zip(CUTS[n], CUTS[n][1:]):
                 cols = slice(first, last)
-                nc.vector.tensor_tensor(done[:, cols], back[n][:, cols], res_in[n][:, cols], ADD)
+                nc.vector.tensor_tensor(done[:, cols], back[n][:, cols], residual[n][:, cols], ADD)
                 nc.sync.dma_start(out[n * P : (n + 1) * P, cols], done[:, cols])
 
         load_x(0, 0)
         nc.sync.dma_start(offsets[:], offs)
         load_x(0, 1)
         load_x(1, 0)
-        load_w2_scales(0)
+        load_rows(w2sc[0], w2_scales[0], range(4))
         load_x(1, 1)
-        load_scales(0, 0)
-        load_words(0, 0, (0,), (0, 1))
-        load_words(0, 0, (1,), (0, 1))
-        load_scales(0, 1)
-        load_words(0, 1, (0, 1), (0,))
-        load_words(0, 1, (0, 1), (1,))
-        load_scales(1, 0, 0, 3)
-        load_words(1, 0, (0, 1), (0,))
-        load_scales(1, 0, 3, 4)
-        load_scales(1, 1, 0, 1)
-        load_words(1, 1, (0, 1), (0,))
-        load_scales(1, 1, 1, 4)
+        load_rows(wsc[0, W1], w1_scales[0], range(4))
+        for s in range(PASSES):
+            load_pass(0, W1, s)
+        load_rows(wsc[0, W3], w3_scales[0], range(4))
+        for g in range(G):
+            load_half(0, W3, g)
+        load_rows(wsc[1, W1], w1_scales[1], range(0, 3))
+        load_half(1, W1, 0)
+        load_rows(wsc[1, W1], w1_scales[1], range(3, 4))
+        load_rows(wsc[1, W3], w3_scales[1], range(0, 1))
+        load_half(1, W3, 0)
+        load_rows(wsc[1, W3], w3_scales[1], range(1, 4))
         load_w2(0)
-        load_gate(0, C)
-        load_words(1, 0, (0, 1), (1,))
-        load_words(1, 1, (0, 1), (1,))
+        load_gate(0)
+        for m in (W1, W3):
+            load_half(1, m, 1)
 
-        round_pairs(0, 0)
-        gather(0, 0, (0, SLOTS), 0, SLOTS)
-        round_pairs(0, 1)
-        warm_up(WARM); load_w2(1); load_w2_scales(1); load_gate(C, SLOTS); load_residual(0); load_residual(1)
-        gather(0, 1, (0, SLOTS), 0, SLOTS)
-        round_pairs(1, 0)
-        weave(0, 0, 0, C, nc.scalar.copy)
-        gather_stepped(1, 0, 0, P)
+        planes0 = keep.tile([P, 2, SLOTS], U32, name="planes0", align_bytes=64)
+        round_pairs(0, 0, VECTOR_TOKENS_FIRST)
+        gather(planes0, 0, 0, 0, SLOTS)
+        round_pairs(0, 1, VECTOR_TOKENS)
+        warm_up()
+        load_w2(1)
+        load_rows(w2sc[1], w2_scales[1], range(4))
+        load_gate(1)
+        for n in range(NT):
+            load_residual(n)
+        gather(planes0, 0, 1, 0, SLOTS)
+        round_pairs(1, 0, VECTOR_TOKENS)
+        weave(0, 0, planes0[:, :, 0:C], nc.scalar.copy)
+        gather_at_a_step(1, 0, 0)
         quantise(0, 0, C)
-        round_pairs(1, 1)
-        gather_stepped(1, 0, P, C)
-        gather_stepped(1, 1, 0, P)
-        gather_stepped(1, 1, P, C)
-        weave(0, 0, C, SLOTS, nc.scalar.copy)
-        quantise(1, 0, P)
-        quantise(1, P, C)
-        gather(1, 0, (C, C), C, SLOTS)
-        gather(1, 1, (C, C), C, SLOTS)
+        round_pairs(1, 1, VECTOR_TOKENS)
+        gather_at_a_step(1, 0, 1)
+        for j in range(2):
+            gather_at_a_step(1, 1, j)
+        weave(0, C, planes0[:, :, C:SLOTS], nc.scalar.copy)
+        for j in range(2):
+            quantise(1, j * P, (j + 1) * P)
+        planes1 = in_line([P, 2, C], U32, "planes1")
+        for u in range(2):
+            gather(planes1, 1, u, C, SLOTS)
         quantise(0, C, SLOTS)
-        weave(1, C, C, SLOTS, nc.vector.tensor_copy)
+        weave(1, C, planes1[:], nc.vector.tensor_copy)
 
-        product(0, 0, 0, 0)
-        product(0, 1, 0, 0)
-        product(1, 0, 0, 0)
-        product(1, 1, 0, 0)
-        product(0, 0, 0, 1)
-        product(0, 1, 0, 1)
-        product(1, 0, 0, 1)
-        product(1, 1, 0, 1)
-        silu(0, 0)
-        silu(0, 1)
-        silu(1, 0)
-        silu(1, 1)
-        both(0, 0, 1)
-        both(0, 1, 1)
-        hidden(0, 0)
-        hidden(0, 1)
+        for s in range(PASSES):
+            for j in range(2):
+                for g in range(G):
+                    product(j, g, W1, s)
+        for j in range(2):
+            for g in range(G):
+                silu(j, g)
+        for g in range(G):
+            both_passes(0, g, W3)
+        for g in range(G):
+            hidden(0, g)
         quantise(1, C, SLOTS)
-        both(1, 0, 1)
-        both(1, 1, 1)
+        for g in range(G):
+            both_passes(1, g, W3)
         hidden(1, 0)
-        turn(0, (0,))
-        turn(0, (1,))
-        unturn(0, (0,))
-        unturn(0, (1,), nc.vector.tensor_copy)
-        requant(0, 0)
-        requant(0, 1)
+
+        for g in range(G):
+            turn(0, g)
+        leave_psum(0, 0)
+        leave_psum(0, 1, nc.vector.tensor_copy)
+        for g in range(G):
+            quantise_h(0, g)
         hidden(1, 1)
-        both(2, 0, 0)
-        silu_part(2, 0, 0)
-        silu_part(2, 0, 1)
-        both(2, 0, 1)
-        hidden_part(2, 0, 0)
-        hidden_part(2, 0, 1)
-        second_layers(0)
-        copy_out(0, (0,))
+        in_two = (slice(0, 1), slice(1, 2))
+        both_passes(2, 0, W1)
+        silu(2, 0, in_two)
+        both_passes(2, 0, W3)
+        hidden(2, 0, in_two)
+        for g in range(G):
+            for n in range(NT):
+                second_product(0, n, g)
+        copy_y(0, 0)
         put_back(0, 0)
-        both(3, 0, 0)
-        copy_out(0, (1,))
+        both_passes(3, 0, W1)
+        copy_y(0, 1)
         put_back(0, 1)
         silu(3, 0)
-        turn(1, (0,))
-        turn(1, (1,))
-        turn(2, (0,))
-        unturn(1, (0,))
-        unturn(1, (1,))
-        requant(1, 0)
-        requant(1, 1)
-        both(2, 1, 0)
-        unturn(2, (0,))
+
+        ready = ((1, 0), (1, 1), (2, 0))
+        for j, g in ready:
+            turn(j, g)
+        for g in range(G):
+            leave_psum(1, g)
+        for g in range(G):
+            quantise_h(1, g)
+        both_passes(2, 1, W1)
+        leave_psum(2, 0)
         silu(2, 1)
-        both(3, 0, 1)
-        requant(2, 0)
+        both_passes(3, 0, W3)
+        quantise_h(2, 0)
         hidden(3, 0)
-        both(2, 1, 1)
-        second_layer(1, (0,))
+        both_passes(2, 1, W3)
+        second_layer(1, 0)
         hidden(2, 1)
-        copy_out(1, (0,))
+        copy_y(1, 0)
         put_back(1, 0)
-        both(3, 1, 0)
+        both_passes(3, 1, W1)
         silu(3, 1)
-        both(3, 1, 1)
+        both_passes(3, 1, W3)
         hidden(3, 1)
-        turn(2, (1,))
-        turn(3, (0,))
-        second_layer(1, (1,))
-        unturn(2, (1,))
-        turn(3, (1,))
-        unturn(3, (0,))
-        requant(2, 1)
-        requant(3, 0)
-        copy_out(1, (1,))
+
+        turn(2, 1)
+        turn(3, 0)
+        second_layer(1, 1)
+        leave_psum(2, 1)
+        turn(3, 1)
+        leave_psum(3, 0)
+        quantise_h(2, 1)
+        quantise_h(3, 0)
+        copy_y(1, 1)
         put_back(1, 1)
-        unturn(3, (1,))
-        second_layer(2, (0,))
-        second_layer(2, (1,))
-        requant(3, 1)
-        copy_out(2, (0,))
-        copy_out(2, (1,))
-        second_layer(3, (0,))
-        second_layer(3, (1,))
-        copy_out(3, (0,))
-        copy_out(3, (1,))
-        put_back(2, 0)
-        put_back(2, 1)
-        put_back(3, 0)
-        put_back(3, 1)
-        finish(0)
-        finish(1)
+        leave_psum(3, 1)
+        for n in range(NT):
+            second_layer(2, n)
+        quantise_h(3, 1)
+        for n in range(NT):
+            copy_y(2, n)
+        for n in range(NT):
+            second_layer(3, n)
+        for n in range(NT):
+            copy_y(3, n)
+        for j in (2, 3):
+            for n in range(NT):
+                put_back(j, n)
+        for n in range(NT):
+            finish(n)

@@ -27,7 +27,7 @@ W1, W3 = 0, 1
 
 VECTOR_TOKENS_FIRST = 2 * T // 3
 VECTOR_TOKENS = T // 2
-SPARE_PRODUCTS = 13
+SPARE_PRODUCTS = 12
 CUTS = ((0, 192, 448, T), (0, T // 2, T))
 LINE_SLOTS = 50
 
@@ -80,18 +80,17 @@ def tile_moe_res_glu_silu_kernel(
             for r in rows:
                 nc.sync.dma_start(plane[r:P:32].bitcast(I32), by_row[r].bitcast(I32))
 
-        def load_pass(e, m, s):
-            piece = keep.tile([P, 2 * H], U8, name=f"wp{e}{m}{s}", align_bytes=64)
-            nc.sync.dma_start(piece[:].bitcast(I32), words[m][e, s].bitcast(I32))
-            for g in range(G):
-                wt[e, m, s, g] = piece[:, 2 * KP * g : 2 * KP * (g + 1)]
-
-        def load_half(e, m, g):
-            piece = keep.tile([P, PASSES, 2 * KP], U8, name=f"wh{e}{m}{g}", align_bytes=64)
-            source = words[m][e].rearrange("s p b -> p s b")[:, :, 2 * KP * g : 2 * KP * (g + 1)]
-            nc.sync.dma_start(piece[:].bitcast(I32), source.bitcast(I32))
-            for s in range(PASSES):
-                wt[e, m, s, g] = piece[:, s, :]
+        def load_words(e, m, passes, halves):
+            width = 2 * KP * len(halves)
+            piece = keep.tile([P, len(passes), width], U8, name=f"w{e}{m}{passes[0]}{halves[0]}", align_bytes=64)
+            source = words[m][e].rearrange("s p b -> p s b")
+            first = 2 * KP * halves[0]
+            nc.sync.dma_start(
+                piece[:].bitcast(I32), source[:, passes[0] : passes[-1] + 1, first : first + width].bitcast(I32)
+            )
+            for s in passes:
+                for g in halves:
+                    wt[e, m, s, g] = piece[:, s - passes[0], 2 * KP * g - first : 2 * KP * (g + 1) - first]
 
         def load_w2(e):
             w2t[e] = keep.tile([P, PASSES, 2 * N], U8, name=f"w2t{e}", align_bytes=64)
@@ -103,9 +102,11 @@ def tile_moe_res_glu_silu_kernel(
             for c in range(C // P):
                 gates[e * C // P + c] = piece[:, c * P : (c + 1) * P]
 
-        def load_residual(n):
-            residual[n] = keep.tile([P, T], F32, name=f"residual{n}")
-            nc.sync.dma_start(residual[n][:], xr[n * P : (n + 1) * P, :])
+        def load_residual():
+            tiles = keep.tile([P, NT, T], F32, name="residual")
+            nc.sync.dma_start(tiles[:], xr.rearrange("(n p) t -> p n t", p=P))
+            for n in range(NT):
+                residual[n] = tiles[:, n, :]
 
         tables, quads, xq, xs = {}, {}, {}, {}
 
@@ -249,21 +250,22 @@ def tile_moe_res_glu_silu_kernel(
         load_rows(w2sc[0], w2_scales[0], range(4))
         load_x(1, 1)
         load_rows(wsc[0, W1], w1_scales[0], range(4))
-        for s in range(PASSES):
-            load_pass(0, W1, s)
+        for g in range(G):
+            load_words(0, W1, (0,), (g,))
+        load_words(0, W1, (1,), (0, 1))
         load_rows(wsc[0, W3], w3_scales[0], range(4))
         for g in range(G):
-            load_half(0, W3, g)
+            load_words(0, W3, (0, 1), (g,))
         load_rows(wsc[1, W1], w1_scales[1], range(0, 3))
-        load_half(1, W1, 0)
+        load_words(1, W1, (0, 1), (0,))
         load_rows(wsc[1, W1], w1_scales[1], range(3, 4))
         load_rows(wsc[1, W3], w3_scales[1], range(0, 1))
-        load_half(1, W3, 0)
+        load_words(1, W3, (0, 1), (0,))
         load_rows(wsc[1, W3], w3_scales[1], range(1, 4))
         load_w2(0)
         load_gate(0)
         for m in (W1, W3):
-            load_half(1, m, 1)
+            load_words(1, m, (0, 1), (1,))
 
         planes0 = keep.tile([P, 2, SLOTS], U32, name="planes0", align_bytes=64)
         round_pairs(0, 0, VECTOR_TOKENS_FIRST)
@@ -273,8 +275,7 @@ def tile_moe_res_glu_silu_kernel(
         load_w2(1)
         load_rows(w2sc[1], w2_scales[1], range(4))
         load_gate(1)
-        for n in range(NT):
-            load_residual(n)
+        load_residual()
         gather(planes0, 0, 1, 0, SLOTS)
         round_pairs(1, 0, VECTOR_TOKENS)
         weave(0, 0, planes0[:, :, 0:C], nc.scalar.copy)
@@ -293,10 +294,12 @@ def tile_moe_res_glu_silu_kernel(
         quantise(0, C, SLOTS)
         weave(1, C, planes1[:], nc.vector.tensor_copy)
 
-        for s in range(PASSES):
+        for g in range(G):
             for j in range(2):
-                for g in range(G):
-                    product(j, g, W1, s)
+                product(j, g, W1, 0)
+        for j in range(2):
+            for g in range(G):
+                product(j, g, W1, 1)
         for j in range(2):
             for g in range(G):
                 silu(j, g)

@@ -256,12 +256,9 @@ def tile_moe_res_glu_silu_kernel(
         load_rows(wsc[0, W3], w3_scales[0], range(4))
         for g in range(G):
             load_words(0, W3, (0, 1), (g,))
-        load_rows(wsc[1, W1], w1_scales[1], range(0, 3))
-        load_words(1, W1, (0, 1), (0,))
-        load_rows(wsc[1, W1], w1_scales[1], range(3, 4))
-        load_rows(wsc[1, W3], w3_scales[1], range(0, 1))
-        load_words(1, W3, (0, 1), (0,))
-        load_rows(wsc[1, W3], w3_scales[1], range(1, 4))
+        for m in (W1, W3):
+            load_words(1, m, (0, 1), (0,))
+            load_rows(wsc[1, m], scales[m][1], range(4))
         load_w2(0)
         load_gate(0)
         for m in (W1, W3):

@@ -28,7 +28,7 @@ W1, W3 = 0, 1
 VECTOR_TOKENS_FIRST = 2 * T // 3
 VECTOR_TOKENS = T // 2
 SPARE_PRODUCTS = 12
-CUTS = ((0, 192, 448, T), (0, T // 2, T))
+CUTS = ((0, T // 4, T // 2, T), (0, T // 2, T))
 LINE_SLOTS = 50
 
 

@@ -253,13 +253,15 @@ def tile_moe_res_glu_silu_kernel(
         for g in range(G):
             load_words(0, W1, (0,), (g,))
         load_words(0, W1, (1,), (0, 1))
-        load_rows(wsc[0, W3], w3_scales[0], range(4))
         for g in range(G):
+            load_rows(wsc[0, W3], w3_scales[0], range(2 * g, 2 * g + 2))
             load_words(0, W3, (0, 1), (g,))
         for m in (W1, W3):
+            load_rows(wsc[1, W1], w1_scales[1], range(2 * m, 2 * m + 2))
             load_words(1, m, (0, 1), (0,))
-            load_rows(wsc[1, m], scales[m][1], range(4))
+        load_rows(wsc[1, W3], w3_scales[1], range(2))
         load_w2(0)
+        load_rows(wsc[1, W3], w3_scales[1], range(2, 4))
         load_gate(0)
         for m in (W1, W3):
             load_words(1, m, (0, 1), (1,))

@@ -29,6 +29,8 @@ VECTOR_TOKENS_FIRST = 2 * T // 3
 VECTOR_TOKENS = T // 2
 SPARE_PRODUCTS = 12
 CUTS = ((0, T // 4, T // 2, T), (0, T // 2, T))
+VECTOR_TOKENS_THIRD = 5 * T // 12
+VECTOR_TOKENS_LAST = 7 * T // 12
 LINE_SLOTS = 50
 
 
@@ -257,11 +259,10 @@ def tile_moe_res_glu_silu_kernel(
             load_rows(wsc[0, W3], w3_scales[0], range(2 * g, 2 * g + 2))
             load_words(0, W3, (0, 1), (g,))
         for m in (W1, W3):
-            load_rows(wsc[1, W1], w1_scales[1], range(2 * m, 2 * m + 2))
+            load_rows(wsc[1, m], scales[m][1], range(2))
             load_words(1, m, (0, 1), (0,))
-        load_rows(wsc[1, W3], w3_scales[1], range(2))
+            load_rows(wsc[1, m], scales[m][1], range(2, 4))
         load_w2(0)
-        load_rows(wsc[1, W3], w3_scales[1], range(2, 4))
         load_gate(0)
         for m in (W1, W3):
             load_words(1, m, (0, 1), (1,))
@@ -276,15 +277,15 @@ def tile_moe_res_glu_silu_kernel(
         load_gate(1)
         load_residual()
         gather(planes0, 0, 1, 0, SLOTS)
-        round_pairs(1, 0, VECTOR_TOKENS)
-        weave(0, 0, planes0[:, :, 0:C], nc.scalar.copy)
+        round_pairs(1, 0, VECTOR_TOKENS_THIRD)
+        weave(0, 0, planes0[:, :, 0:C], nc.vector.tensor_copy)
+        weave(0, C, planes0[:, :, C:SLOTS], nc.scalar.copy)
         gather_at_a_step(1, 0, 0)
         quantise(0, 0, C)
-        round_pairs(1, 1, VECTOR_TOKENS)
+        round_pairs(1, 1, VECTOR_TOKENS_LAST)
         gather_at_a_step(1, 0, 1)
         for j in range(2):
             gather_at_a_step(1, 1, j)
-        weave(0, C, planes0[:, :, C:SLOTS], nc.scalar.copy)
         for j in range(2):
             quantise(1, j * P, (j + 1) * P)
         planes1 = in_line([P, 2, C], U32, "planes1")

@@ -31,6 +31,7 @@ SPARE_PRODUCTS = 12
 CUTS = ((0, T // 4, T // 2, T), (0, T // 2, T))
 VECTOR_TOKENS_THIRD = 5 * T // 12
 VECTOR_TOKENS_LAST = 7 * T // 12
+DMA_ALIGN = 256
 LINE_SLOTS = 50
 
 
@@ -58,11 +59,11 @@ def tile_moe_res_glu_silu_kernel(
         wsc, w2sc, back = {}, {}, {}
         for e in range(E):
             for m in (W1, W3):
-                wsc[e, m] = keep.tile([P, PASSES, H], U8, name=f"wsc{e}{m}", align_bytes=64)
+                wsc[e, m] = keep.tile([P, PASSES, H], U8, name=f"wsc{e}{m}", align_bytes=DMA_ALIGN)
                 engine = nc.gpsimd if m == W1 else nc.vector
                 engine.memset(wsc[e, m][:].rearrange("p s i -> p (s i)").bitcast(I32), 0)
         for e in range(E):
-            w2sc[e] = keep.tile([P, PASSES, N], U8, name=f"w2sc{e}", align_bytes=64)
+            w2sc[e] = keep.tile([P, PASSES, N], U8, name=f"w2sc{e}", align_bytes=DMA_ALIGN)
             nc.gpsimd.memset(w2sc[e][:].rearrange("p s n -> p (s n)").bitcast(I32), 0)
         for n in range(NT):
             back[n] = keep.tile([P, T], F32, name=f"back{n}", align_bytes=64)
@@ -74,7 +75,7 @@ def tile_moe_res_glu_silu_kernel(
         pieces = xT.rearrange("(s p u d) w -> s u p d w", s=PASSES, p=P, u=2)
 
         def load_x(s, u):
-            raw[s, u] = keep.tile([P, 2, T], F32, name=f"raw{s}{u}", align_bytes=64)
+            raw[s, u] = keep.tile([P, 2, T], F32, name=f"raw{s}{u}", align_bytes=DMA_ALIGN)
             nc.sync.dma_start(raw[s, u][:], pieces[s, u])
 
         def load_rows(plane, source, rows):
@@ -84,7 +85,7 @@ def tile_moe_res_glu_silu_kernel(
 
         def load_words(e, m, passes, halves):
             width = 2 * KP * len(halves)
-            piece = keep.tile([P, len(passes), width], U8, name=f"w{e}{m}{passes[0]}{halves[0]}", align_bytes=64)
+            piece = keep.tile([P, len(passes), width], U8, name=f"w{e}{m}{passes[0]}{halves[0]}", align_bytes=DMA_ALIGN)
             source = words[m][e].rearrange("s p b -> p s b")
             first = 2 * KP * halves[0]
             nc.sync.dma_start(
@@ -95,17 +96,17 @@ def tile_moe_res_glu_silu_kernel(
                     wt[e, m, s, g] = piece[:, s - passes[0], 2 * KP * g - first : 2 * KP * (g + 1) - first]
 
         def load_w2(e):
-            w2t[e] = keep.tile([P, PASSES, 2 * N], U8, name=f"w2t{e}", align_bytes=64)
+            w2t[e] = keep.tile([P, PASSES, 2 * N], U8, name=f"w2t{e}", align_bytes=DMA_ALIGN)
             nc.sync.dma_start(w2t[e][:].bitcast(I32), w2_words[e].rearrange("s p b -> p s b").bitcast(I32))
 
         def load_gate(e):
-            piece = keep.tile([P, C], F32, name=f"gate{e}")
+            piece = keep.tile([P, C], F32, name=f"gate{e}", align_bytes=DMA_ALIGN)
             nc.sync.dma_start(piece[:], gate[0:P, e * C : (e + 1) * C])
             for c in range(C // P):
                 gates[e * C // P + c] = piece[:, c * P : (c + 1) * P]
 
         def load_residual():
-            tiles = keep.tile([P, NT, T], F32, name="residual")
+            tiles = keep.tile([P, NT, T], F32, name="residual", align_bytes=DMA_ALIGN)
             nc.sync.dma_start(tiles[:], xr.rearrange("(n p) t -> p n t", p=P))
             for n in range(NT):
                 residual[n] = tiles[:, n, :]
@@ -239,7 +240,7 @@ def tile_moe_res_glu_silu_kernel(
             nc.vector.tensor_tensor(back[n][:].indirect(listed(j * P, (j + 1) * P)), y_sb[j, n][:], gates[j], MULT)
 
         def finish(n):
-            done = keep.tile([P, T], F32, name=f"done{n}")
+            done = keep.tile([P, T], F32, name=f"done{n}", align_bytes=DMA_ALIGN)
             for first, last in zip(CUTS[n], CUTS[n][1:]):
                 cols = slice(first, last)
                 nc.vector.tensor_tensor(done[:, cols], back[n][:, cols], residual[n][:, cols], ADD)

@@ -28,7 +28,7 @@ W1, W3 = 0, 1
 VECTOR_TOKENS_FIRST = 2 * T // 3
 VECTOR_TOKENS = T // 2
 SPARE_PRODUCTS = 12
-CUTS = ((0, T // 4, T // 2, T), (0, T // 2, T))
+CUTS = ((0, P, 2 * P, T), (0, 4 * P, T))
 VECTOR_TOKENS_THIRD = 5 * T // 12
 VECTOR_TOKENS_LAST = 7 * T // 12
 DMA_ALIGN = 256

@@ -107,9 +107,9 @@ def tile_moe_res_glu_silu_kernel(
 
         def load_residual():
             tiles = keep.tile([P, NT, T], F32, name="residual", align_bytes=DMA_ALIGN)
-            nc.sync.dma_start(tiles[:], xr.rearrange("(n p) t -> p n t", p=P))
             for n in range(NT):
                 residual[n] = tiles[:, n, :]
+                nc.sync.dma_start(residual[n], xr[n * P : (n + 1) * P, :])
 
         tables, quads, xq, xs = {}, {}, {}, {}
 
@@ -250,20 +250,18 @@ def tile_moe_res_glu_silu_kernel(
         nc.sync.dma_start(offsets[:], offs)
         load_x(0, 1)
         load_x(1, 0)
-        load_rows(w2sc[0], w2_scales[0], range(4))
         load_x(1, 1)
         load_rows(wsc[0, W1], w1_scales[0], range(4))
-        for g in range(G):
-            load_words(0, W1, (0,), (g,))
-        load_words(0, W1, (1,), (0, 1))
-        for g in range(G):
-            load_rows(wsc[0, W3], w3_scales[0], range(2 * g, 2 * g + 2))
-            load_words(0, W3, (0, 1), (g,))
+        for s in range(PASSES):
+            load_words(0, W1, (s,), (0, 1))
+        load_words(0, W3, (0, 1), (0,))
+        load_rows(wsc[0, W3], w3_scales[0], range(4))
+        load_words(0, W3, (0, 1), (1,))
         for m in (W1, W3):
-            load_rows(wsc[1, m], scales[m][1], range(2))
             load_words(1, m, (0, 1), (0,))
-            load_rows(wsc[1, m], scales[m][1], range(2, 4))
+            load_rows(wsc[1, m], scales[m][1], range(4))
         load_w2(0)
+        load_rows(w2sc[0], w2_scales[0], range(4))
         load_gate(0)
         for m in (W1, W3):
             load_words(1, m, (0, 1), (1,))

@@ -30,7 +30,7 @@ VECTOR_TOKENS = T // 2
 SPARE_PRODUCTS = 12
 CUTS = ((0, P, 2 * P, T), (0, 4 * P, T))
 VECTOR_TOKENS_THIRD = 5 * T // 12
-VECTOR_TOKENS_LAST = 7 * T // 12
+VECTOR_TOKENS_LAST = 11 * T // 24
 DMA_ALIGN = 256
 LINE_SLOTS = 50
 

@@ -28,7 +28,7 @@ W1, W3 = 0, 1
 VECTOR_TOKENS_FIRST = 2 * T // 3
 VECTOR_TOKENS = T // 2
 SPARE_PRODUCTS = 12
-CUTS = ((0, P, 2 * P, T), (0, 4 * P, T))
+CUTS = ((0, P, 3 * P, T), (0, 3 * P, 5 * P, T))
 VECTOR_TOKENS_THIRD = 5 * T // 12
 VECTOR_TOKENS_LAST = 11 * T // 24
 DMA_ALIGN = 256
@@ -107,9 +107,9 @@ def tile_moe_res_glu_silu_kernel(
 
         def load_residual():
             tiles = keep.tile([P, NT, T], F32, name="residual", align_bytes=DMA_ALIGN)
+            nc.sync.dma_start(tiles[:], xr.rearrange("(n p) t -> p n t", p=P))
             for n in range(NT):
                 residual[n] = tiles[:, n, :]
-                nc.sync.dma_start(residual[n], xr[n * P : (n + 1) * P, :])
 
         tables, quads, xq, xs = {}, {}, {}, {}
 

@@ -83,9 +83,9 @@ def tile_moe_res_glu_silu_kernel(
             for r in rows:
                 nc.sync.dma_start(plane[r:P:32].bitcast(I32), by_row[r].bitcast(I32))
 
-        def load_words(e, m, passes, halves):
+        def load_words(e, m, passes, halves, tag=""):
             width = 2 * KP * len(halves)
-            piece = keep.tile([P, len(passes), width], U8, name=f"w{e}{m}{passes[0]}{halves[0]}", align_bytes=DMA_ALIGN)
+            piece = keep.tile([P, len(passes), width], U8, name=f"w{e}{m}{passes[0]}{halves[0]}", tag=tag or f"w{e}{m}{passes[0]}{halves[0]}", align_bytes=DMA_ALIGN)
             source = words[m][e].rearrange("s p b -> p s b")
             first = 2 * KP * halves[0]
             nc.sync.dma_start(
@@ -106,7 +106,7 @@ def tile_moe_res_glu_silu_kernel(
                 gates[e * C // P + c] = piece[:, c * P : (c + 1) * P]
 
         def load_residual():
-            tiles = keep.tile([P, NT, T], F32, name="residual", align_bytes=DMA_ALIGN)
+            tiles = keep.tile([P, NT, T], F32, name="residual", tag="last", align_bytes=DMA_ALIGN)
             nc.sync.dma_start(tiles[:], xr.rearrange("(n p) t -> p n t", p=P))
             for n in range(NT):
                 residual[n] = tiles[:, n, :]
@@ -263,8 +263,8 @@ def tile_moe_res_glu_silu_kernel(
         load_w2(0)
         load_rows(w2sc[0], w2_scales[0], range(4))
         load_gate(0)
-        for m in (W1, W3):
-            load_words(1, m, (0, 1), (1,))
+        load_words(1, W1, (0, 1), (1,))
+        load_words(1, W3, (0, 1), (1,), tag="last")
 
         planes0 = keep.tile([P, 2, SLOTS], U32, name="planes0", align_bytes=64)
         round_pairs(0, 0, VECTOR_TOKENS_FIRST)
@@ -274,7 +274,6 @@ def tile_moe_res_glu_silu_kernel(
         load_w2(1)
         load_rows(w2sc[1], w2_scales[1], range(4))
         load_gate(1)
-        load_residual()
         gather(planes0, 0, 1, 0, SLOTS)
         round_pairs(1, 0, VECTOR_TOKENS_THIRD)
         weave(0, 0, planes0[:, :, 0:C], nc.vector.tensor_copy)
@@ -354,6 +353,7 @@ def tile_moe_res_glu_silu_kernel(
         both_passes(3, 1, W1)
         silu(3, 1)
         both_passes(3, 1, W3)
+        load_residual()
         hidden(3, 1)
 
         turn(2, 1)

@@ -351,10 +351,10 @@ def tile_moe_res_glu_silu_kernel(
         copy_y(1, 0)
         put_back(1, 0)
         both_passes(3, 1, W1)
-        silu(3, 1)
+        silu(3, 1, in_two)
         both_passes(3, 1, W3)
         load_residual()
-        hidden(3, 1)
+        hidden(3, 1, in_two)
 
         turn(2, 1)
         turn(3, 0)

@@ -26,13 +26,13 @@ NT = N // P
 W1, W3 = 0, 1
 
 VECTOR_TOKENS_FIRST = 2 * T // 3
-VECTOR_TOKENS = T // 2
+VECTOR_TOKENS_SECOND = T // 2
+VECTOR_TOKENS_PASS_1 = 11 * T // 24
 SPARE_PRODUCTS = 12
 CUTS = ((0, P, 3 * P, T), (0, 3 * P, 5 * P, T))
-VECTOR_TOKENS_THIRD = 5 * T // 12
-VECTOR_TOKENS_LAST = 11 * T // 24
-DMA_ALIGN = 256
+MX_ALIGN = 64
 LINE_SLOTS = 50
+ROWS = range(4)
 
 
 def tile_moe_res_glu_silu_kernel(
@@ -45,7 +45,7 @@ def tile_moe_res_glu_silu_kernel(
         psum = ctx.enter_context(tc.psum_pool(name="psum", bufs=8))
 
         def in_line(shape, dtype, name):
-            return ring.tile(shape, dtype, name=name, tag="line", bufs=LINE_SLOTS, align_bytes=64)
+            return ring.tile(shape, dtype, name=name, tag="line", bufs=LINE_SLOTS, align_bytes=MX_ALIGN)
 
         def bank(shape, name):
             return psum.tile(shape, F32, name=name, tag="bank")
@@ -59,14 +59,14 @@ def tile_moe_res_glu_silu_kernel(
         wsc, w2sc, back = {}, {}, {}
         for e in range(E):
             for m in (W1, W3):
-                wsc[e, m] = keep.tile([P, PASSES, H], U8, name=f"wsc{e}{m}", align_bytes=DMA_ALIGN)
+                wsc[e, m] = keep.tile([P, PASSES, H], U8, name=f"wsc{e}{m}", align_bytes=MX_ALIGN)
                 engine = nc.gpsimd if m == W1 else nc.vector
                 engine.memset(wsc[e, m][:].rearrange("p s i -> p (s i)").bitcast(I32), 0)
         for e in range(E):
-            w2sc[e] = keep.tile([P, PASSES, N], U8, name=f"w2sc{e}", align_bytes=DMA_ALIGN)
+            w2sc[e] = keep.tile([P, PASSES, N], U8, name=f"w2sc{e}", align_bytes=MX_ALIGN)
             nc.gpsimd.memset(w2sc[e][:].rearrange("p s n -> p (s n)").bitcast(I32), 0)
         for n in range(NT):
-            back[n] = keep.tile([P, T], F32, name=f"back{n}", align_bytes=64)
+            back[n] = keep.tile([P, T], F32, name=f"back{n}", align_bytes=MX_ALIGN)
             nc.vector.memset(back[n][:], 0.0)
         ident = keep.tile([P, P], F32, name="ident")
         make_identity(nc, ident[:])
@@ -75,7 +75,7 @@ def tile_moe_res_glu_silu_kernel(
         pieces = xT.rearrange("(s p u d) w -> s u p d w", s=PASSES, p=P, u=2)
 
         def load_x(s, u):
-            raw[s, u] = keep.tile([P, 2, T], F32, name=f"raw{s}{u}", align_bytes=DMA_ALIGN)
+            raw[s, u] = keep.tile([P, 2, T], F32, name=f"raw{s}{u}", align_bytes=MX_ALIGN)
             nc.sync.dma_start(raw[s, u][:], pieces[s, u])
 
         def load_rows(plane, source, rows):
@@ -83,9 +83,9 @@ def tile_moe_res_glu_silu_kernel(
             for r in rows:
                 nc.sync.dma_start(plane[r:P:32].bitcast(I32), by_row[r].bitcast(I32))
 
-        def load_words(e, m, passes, halves, tag=""):
+        def load_words(e, m, passes, halves):
             width = 2 * KP * len(halves)
-            piece = keep.tile([P, len(passes), width], U8, name=f"w{e}{m}{passes[0]}{halves[0]}", tag=tag or f"w{e}{m}{passes[0]}{halves[0]}", align_bytes=DMA_ALIGN)
+            piece = keep.tile([P, len(passes), width], U8, name=f"w{e}{m}{passes[0]}{halves[0]}", align_bytes=MX_ALIGN)
             source = words[m][e].rearrange("s p b -> p s b")
             first = 2 * KP * halves[0]
             nc.sync.dma_start(
@@ -96,17 +96,17 @@ def tile_moe_res_glu_silu_kernel(
                     wt[e, m, s, g] = piece[:, s - passes[0], 2 * KP * g - first : 2 * KP * (g + 1) - first]
 
         def load_w2(e):
-            w2t[e] = keep.tile([P, PASSES, 2 * N], U8, name=f"w2t{e}", align_bytes=DMA_ALIGN)
+            w2t[e] = keep.tile([P, PASSES, 2 * N], U8, name=f"w2t{e}", align_bytes=MX_ALIGN)
             nc.sync.dma_start(w2t[e][:].bitcast(I32), w2_words[e].rearrange("s p b -> p s b").bitcast(I32))
 
         def load_gate(e):
-            piece = keep.tile([P, C], F32, name=f"gate{e}", align_bytes=DMA_ALIGN)
+            piece = keep.tile([P, C], F32, name=f"gate{e}")
             nc.sync.dma_start(piece[:], gate[0:P, e * C : (e + 1) * C])
             for c in range(C // P):
                 gates[e * C // P + c] = piece[:, c * P : (c + 1) * P]
 
         def load_residual():
-            tiles = keep.tile([P, NT, T], F32, name="residual", tag="last", align_bytes=DMA_ALIGN)
+            tiles = keep.tile([P, NT, T], F32, name="residual")
             nc.sync.dma_start(tiles[:], xr.rearrange("(n p) t -> p n t", p=P))
             for n in range(NT):
                 residual[n] = tiles[:, n, :]
@@ -135,7 +135,7 @@ def tile_moe_res_glu_silu_kernel(
 
         def quantise(s, first, last):
             codes = in_line([P, last - first], U32, "codes")
-            plane = keep.tile([P, last - first], U8, name=f"xs{s}{first}", align_bytes=64)
+            plane = keep.tile([P, last - first], U8, name=f"xs{s}{first}", align_bytes=MX_ALIGN)
             nc.vector.quantize_mx(
                 out=codes[:].bitcast(FP8X4),
                 scales=plane[:],
@@ -147,7 +147,7 @@ def tile_moe_res_glu_silu_kernel(
 
         def warm_up():
             codes = in_line([P, P], U32, "zero_codes")
-            plane = keep.tile([P, P], U8, name="zero_plane", align_bytes=64)
+            plane = keep.tile([P, P], U8, name="zero_plane", align_bytes=MX_ALIGN)
             nc.vector.quantize_mx(out=codes[:].bitcast(FP8X4), scales=plane[:], in_=back[1][:, 0:N].bitcast(BF16))
             spare = bank([P, N], "spare")
             for _ in range(SPARE_PRODUCTS):
@@ -211,7 +211,7 @@ def tile_moe_res_glu_silu_kernel(
 
         def quantise_h(j, g):
             hq[j, g] = in_line([P, P], U32, "hq")
-            hs[j, g] = keep.tile([P, P], U8, name=f"hs{j}{g}", align_bytes=64)
+            hs[j, g] = keep.tile([P, P], U8, name=f"hs{j}{g}", align_bytes=MX_ALIGN)
             nc.vector.quantize_mx(out=hq[j, g][:].bitcast(FP8X4), scales=hs[j, g][:], in_=h_quads[j, g][:])
 
         def second_product(j, n, g):
@@ -240,7 +240,7 @@ def tile_moe_res_glu_silu_kernel(
             nc.vector.tensor_tensor(back[n][:].indirect(listed(j * P, (j + 1) * P)), y_sb[j, n][:], gates[j], MULT)
 
         def finish(n):
-            done = keep.tile([P, T], F32, name=f"done{n}", align_bytes=DMA_ALIGN)
+            done = keep.tile([P, T], F32, name=f"done{n}")
             for first, last in zip(CUTS[n], CUTS[n][1:]):
                 cols = slice(first, last)
                 nc.vector.tensor_tensor(done[:, cols], back[n][:, cols], residual[n][:, cols], ADD)
@@ -251,36 +251,37 @@ def tile_moe_res_glu_silu_kernel(
         load_x(0, 1)
         load_x(1, 0)
         load_x(1, 1)
-        load_rows(wsc[0, W1], w1_scales[0], range(4))
+        load_rows(wsc[0, W1], w1_scales[0], ROWS)
         for s in range(PASSES):
             load_words(0, W1, (s,), (0, 1))
         load_words(0, W3, (0, 1), (0,))
-        load_rows(wsc[0, W3], w3_scales[0], range(4))
+        load_rows(wsc[0, W3], w3_scales[0], ROWS)
         load_words(0, W3, (0, 1), (1,))
         for m in (W1, W3):
             load_words(1, m, (0, 1), (0,))
-            load_rows(wsc[1, m], scales[m][1], range(4))
+            load_rows(wsc[1, m], scales[m][1], ROWS)
         load_w2(0)
-        load_rows(w2sc[0], w2_scales[0], range(4))
+        load_rows(w2sc[0], w2_scales[0], ROWS)
         load_gate(0)
-        load_words(1, W1, (0, 1), (1,))
-        load_words(1, W3, (0, 1), (1,), tag="last")
+        for m in (W1, W3):
+            load_words(1, m, (0, 1), (1,))
 
-        planes0 = keep.tile([P, 2, SLOTS], U32, name="planes0", align_bytes=64)
+        planes0 = keep.tile([P, 2, SLOTS], U32, name="planes0", align_bytes=MX_ALIGN)
         round_pairs(0, 0, VECTOR_TOKENS_FIRST)
         gather(planes0, 0, 0, 0, SLOTS)
-        round_pairs(0, 1, VECTOR_TOKENS)
+        round_pairs(0, 1, VECTOR_TOKENS_SECOND)
         warm_up()
         load_w2(1)
-        load_rows(w2sc[1], w2_scales[1], range(4))
+        load_rows(w2sc[1], w2_scales[1], ROWS)
         load_gate(1)
+        load_residual()
         gather(planes0, 0, 1, 0, SLOTS)
-        round_pairs(1, 0, VECTOR_TOKENS_THIRD)
+        round_pairs(1, 0, VECTOR_TOKENS_PASS_1)
         weave(0, 0, planes0[:, :, 0:C], nc.vector.tensor_copy)
         weave(0, C, planes0[:, :, C:SLOTS], nc.scalar.copy)
         gather_at_a_step(1, 0, 0)
         quantise(0, 0, C)
-        round_pairs(1, 1, VECTOR_TOKENS_LAST)
+        round_pairs(1, 1, VECTOR_TOKENS_PASS_1)
         gather_at_a_step(1, 0, 1)
         for j in range(2):
             gather_at_a_step(1, 1, j)
@@ -353,7 +354,6 @@ def tile_moe_res_glu_silu_kernel(
         both_passes(3, 1, W1)
         silu(3, 1, in_two)
         both_passes(3, 1, W3)
-        load_residual()
         hidden(3, 1, in_two)
 
         turn(2, 1)

@@ -30,6 +30,7 @@ VECTOR_TOKENS_SECOND = T // 2
 VECTOR_TOKENS_PASS_1 = 11 * T // 24
 SPARE_PRODUCTS = 12
 CUTS = ((0, P, 3 * P, T), (0, 3 * P, 5 * P, T))
+DMA_ALIGN = 256
 MX_ALIGN = 64
 LINE_SLOTS = 50
 ROWS = range(4)
@@ -59,11 +60,11 @@ def tile_moe_res_glu_silu_kernel(
         wsc, w2sc, back = {}, {}, {}
         for e in range(E):
             for m in (W1, W3):
-                wsc[e, m] = keep.tile([P, PASSES, H], U8, name=f"wsc{e}{m}", align_bytes=MX_ALIGN)
+                wsc[e, m] = keep.tile([P, PASSES, H], U8, name=f"wsc{e}{m}", align_bytes=DMA_ALIGN)
                 engine = nc.gpsimd if m == W1 else nc.vector
                 engine.memset(wsc[e, m][:].rearrange("p s i -> p (s i)").bitcast(I32), 0)
         for e in range(E):
-            w2sc[e] = keep.tile([P, PASSES, N], U8, name=f"w2sc{e}", align_bytes=MX_ALIGN)
+            w2sc[e] = keep.tile([P, PASSES, N], U8, name=f"w2sc{e}", align_bytes=DMA_ALIGN)
             nc.gpsimd.memset(w2sc[e][:].rearrange("p s n -> p (s n)").bitcast(I32), 0)
         for n in range(NT):
             back[n] = keep.tile([P, T], F32, name=f"back{n}", align_bytes=MX_ALIGN)
@@ -75,7 +76,7 @@ def tile_moe_res_glu_silu_kernel(
         pieces = xT.rearrange("(s p u d) w -> s u p d w", s=PASSES, p=P, u=2)
 
         def load_x(s, u):
-            raw[s, u] = keep.tile([P, 2, T], F32, name=f"raw{s}{u}", align_bytes=MX_ALIGN)
+            raw[s, u] = keep.tile([P, 2, T], F32, name=f"raw{s}{u}", align_bytes=DMA_ALIGN)
             nc.sync.dma_start(raw[s, u][:], pieces[s, u])
 
         def load_rows(plane, source, rows):
@@ -85,7 +86,7 @@ def tile_moe_res_glu_silu_kernel(
 
         def load_words(e, m, passes, halves):
             width = 2 * KP * len(halves)
-            piece = keep.tile([P, len(passes), width], U8, name=f"w{e}{m}{passes[0]}{halves[0]}", align_bytes=MX_ALIGN)
+            piece = keep.tile([P, len(passes), width], U8, name=f"w{e}{m}{passes[0]}{halves[0]}", align_bytes=DMA_ALIGN)
             source = words[m][e].rearrange("s p b -> p s b")
             first = 2 * KP * halves[0]
             nc.sync.dma_start(
@@ -96,17 +97,17 @@ def tile_moe_res_glu_silu_kernel(
                     wt[e, m, s, g] = piece[:, s - passes[0], 2 * KP * g - first : 2 * KP * (g + 1) - first]
 
         def load_w2(e):
-            w2t[e] = keep.tile([P, PASSES, 2 * N], U8, name=f"w2t{e}", align_bytes=MX_ALIGN)
+            w2t[e] = keep.tile([P, PASSES, 2 * N], U8, name=f"w2t{e}", align_bytes=DMA_ALIGN)
             nc.sync.dma_start(w2t[e][:].bitcast(I32), w2_words[e].rearrange("s p b -> p s b").bitcast(I32))
 
         def load_gate(e):
-            piece = keep.tile([P, C], F32, name=f"gate{e}")
+            piece = keep.tile([P, C], F32, name=f"gate{e}", align_bytes=DMA_ALIGN)
             nc.sync.dma_start(piece[:], gate[0:P, e * C : (e + 1) * C])
             for c in range(C // P):
                 gates[e * C // P + c] = piece[:, c * P : (c + 1) * P]
 
         def load_residual():
-            tiles = keep.tile([P, NT, T], F32, name="residual")
+            tiles = keep.tile([P, NT, T], F32, name="residual", align_bytes=DMA_ALIGN)
             nc.sync.dma_start(tiles[:], xr.rearrange("(n p) t -> p n t", p=P))
             for n in range(NT):
                 residual[n] = tiles[:, n, :]
@@ -240,7 +241,7 @@ def tile_moe_res_glu_silu_kernel(
             nc.vector.tensor_tensor(back[n][:].indirect(listed(j * P, (j + 1) * P)), y_sb[j, n][:], gates[j], MULT)
 
         def finish(n):
-            done = keep.tile([P, T], F32, name=f"done{n}")
+            done = keep.tile([P, T], F32, name=f"done{n}", align_bytes=DMA_ALIGN)
             for first, last in zip(CUTS[n], CUTS[n][1:]):
                 cols = slice(first, last)
                 nc.vector.tensor_tensor(done[:, cols], back[n][:, cols], residual[n][:, cols], ADD)

@@ -353,9 +353,9 @@ def tile_moe_res_glu_silu_kernel(
         copy_y(1, 0)
         put_back(1, 0)
         both_passes(3, 1, W1)
-        silu(3, 1, in_two)
+        silu(3, 1)
         both_passes(3, 1, W3)
-        hidden(3, 1, in_two)
+        hidden(3, 1)
 
         turn(2, 1)
         turn(3, 0)

@@ -28,7 +28,7 @@ W1, W3 = 0, 1
 VECTOR_TOKENS_FIRST = 2 * T // 3
 VECTOR_TOKENS_SECOND = T // 2
 VECTOR_TOKENS_PASS_1 = 11 * T // 24
-SPARE_PRODUCTS = 12
+SPARE_PRODUCTS = 6
 CUTS = ((0, P, 3 * P, T), (0, 3 * P, 5 * P, T))
 DMA_ALIGN = 256
 MX_ALIGN = 64
@@ -59,13 +59,13 @@ def tile_moe_res_glu_silu_kernel(
         words, scales = (w1_words, w3_words), (w1_scales, w3_scales)
         wsc, w2sc, back = {}, {}, {}
         for e in range(E):
+            w2sc[e] = keep.tile([P, PASSES, N], U8, name=f"w2sc{e}", align_bytes=DMA_ALIGN)
+            nc.gpsimd.memset(w2sc[e][:].rearrange("p s n -> p (s n)").bitcast(I32), 0)
+        for e in range(E):
             for m in (W1, W3):
                 wsc[e, m] = keep.tile([P, PASSES, H], U8, name=f"wsc{e}{m}", align_bytes=DMA_ALIGN)
                 engine = nc.gpsimd if m == W1 else nc.vector
                 engine.memset(wsc[e, m][:].rearrange("p s i -> p (s i)").bitcast(I32), 0)
-        for e in range(E):
-            w2sc[e] = keep.tile([P, PASSES, N], U8, name=f"w2sc{e}", align_bytes=DMA_ALIGN)
-            nc.gpsimd.memset(w2sc[e][:].rearrange("p s n -> p (s n)").bitcast(I32), 0)
         for n in range(NT):
             back[n] = keep.tile([P, T], F32, name=f"back{n}", align_bytes=MX_ALIGN)
             nc.vector.memset(back[n][:], 0.0)
@@ -146,18 +146,18 @@ def tile_moe_res_glu_silu_kernel(
                 xq[s, j] = codes[:, j * P - first : (j + 1) * P - first]
                 xs[s, j] = plane[:, j * P - first : (j + 1) * P - first]
 
-        def warm_up():
-            codes = in_line([P, P], U32, "zero_codes")
-            plane = keep.tile([P, P], U8, name="zero_plane", align_bytes=MX_ALIGN)
-            nc.vector.quantize_mx(out=codes[:].bitcast(FP8X4), scales=plane[:], in_=back[1][:, 0:N].bitcast(BF16))
-            spare = bank([P, N], "spare")
+        def warm_up(gathered):
+            codes = in_line([P, C], U32, "spare_codes")
+            plane = keep.tile([P, C], U8, name="spare_plane", align_bytes=MX_ALIGN)
+            nc.vector.quantize_mx(out=codes[:].bitcast(FP8X4), scales=plane[:], in_=gathered.bitcast(BF16))
+            spare = bank([P, KP], "spare")
             for _ in range(SPARE_PRODUCTS):
                 nc.tensor.matmul_mx(
                     out=spare[:],
-                    lhsT=codes[:].bitcast(FP8X4),
-                    lhsT_scale=plane[:],
+                    lhsT=codes[:, 0:P].bitcast(FP8X4),
+                    lhsT_scale=plane[:, 0:P],
                     rhs=codes[:].bitcast(U8).bitcast(FP4X4),
-                    rhs_scale=w2sc[1][:, 0, :],
+                    rhs_scale=w2sc[0][:].rearrange("p s n -> p (s n)"),
                     start=True,
                     stop=True,
                 )
@@ -250,6 +250,7 @@ def tile_moe_res_glu_silu_kernel(
         load_x(0, 0)
         nc.sync.dma_start(offsets[:], offs)
         load_x(0, 1)
+        load_rows(w2sc[0], w2_scales[0], ROWS)
         load_x(1, 0)
         load_x(1, 1)
         load_rows(wsc[0, W1], w1_scales[0], ROWS)
@@ -262,20 +263,19 @@ def tile_moe_res_glu_silu_kernel(
             load_words(1, m, (0, 1), (0,))
             load_rows(wsc[1, m], scales[m][1], ROWS)
         load_w2(0)
-        load_rows(w2sc[0], w2_scales[0], ROWS)
         load_gate(0)
         for m in (W1, W3):
             load_words(1, m, (0, 1), (1,))
+        load_w2(1)
+        load_rows(w2sc[1], w2_scales[1], ROWS)
+        load_gate(1)
+        load_residual()
 
         planes0 = keep.tile([P, 2, SLOTS], U32, name="planes0", align_bytes=MX_ALIGN)
         round_pairs(0, 0, VECTOR_TOKENS_FIRST)
         gather(planes0, 0, 0, 0, SLOTS)
         round_pairs(0, 1, VECTOR_TOKENS_SECOND)
-        warm_up()
-        load_w2(1)
-        load_rows(w2sc[1], w2_scales[1], ROWS)
-        load_gate(1)
-        load_residual()
+        warm_up(planes0[:, 0, :])
         gather(planes0, 0, 1, 0, SLOTS)
         round_pairs(1, 0, VECTOR_TOKENS_PASS_1)
         weave(0, 0, planes0[:, :, 0:C], nc.vector.tensor_copy)

@@ -28,7 +28,7 @@ W1, W3 = 0, 1
 VECTOR_TOKENS_FIRST = 2 * T // 3
 VECTOR_TOKENS_SECOND = T // 2
 VECTOR_TOKENS_PASS_1 = 11 * T // 24
-SPARE_PRODUCTS = 6
+SPARE_PRODUCTS = 5
 CUTS = ((0, P, 3 * P, T), (0, 3 * P, 5 * P, T))
 DMA_ALIGN = 256
 MX_ALIGN = 64

@@ -100,11 +100,11 @@ def tile_moe_res_glu_silu_kernel(
             w2t[e] = keep.tile([P, PASSES, 2 * N], U8, name=f"w2t{e}", align_bytes=DMA_ALIGN)
             nc.sync.dma_start(w2t[e][:].bitcast(I32), w2_words[e].rearrange("s p b -> p s b").bitcast(I32))
 
-        def load_gate(e):
-            piece = keep.tile([P, C], F32, name=f"gate{e}", align_bytes=DMA_ALIGN)
-            nc.sync.dma_start(piece[:], gate[0:P, e * C : (e + 1) * C])
-            for c in range(C // P):
-                gates[e * C // P + c] = piece[:, c * P : (c + 1) * P]
+        def load_gate():
+            piece = keep.tile([P, SLOTS], F32, name="gate", align_bytes=DMA_ALIGN)
+            nc.sync.dma_start(piece[:], gate[0:P, :])
+            for j in range(SLOTS // P):
+                gates[j] = piece[:, j * P : (j + 1) * P]
 
         def load_residual():
             tiles = keep.tile([P, NT, T], F32, name="residual", align_bytes=DMA_ALIGN)
@@ -254,8 +254,9 @@ def tile_moe_res_glu_silu_kernel(
         load_x(1, 0)
         load_x(1, 1)
         load_rows(wsc[0, W1], w1_scales[0], ROWS)
-        for s in range(PASSES):
-            load_words(0, W1, (s,), (0, 1))
+        for g in range(G):
+            load_words(0, W1, (0,), (g,))
+        load_words(0, W1, (1,), (0, 1))
         load_words(0, W3, (0, 1), (0,))
         load_rows(wsc[0, W3], w3_scales[0], ROWS)
         load_words(0, W3, (0, 1), (1,))
@@ -263,12 +264,11 @@ def tile_moe_res_glu_silu_kernel(
             load_words(1, m, (0, 1), (0,))
             load_rows(wsc[1, m], scales[m][1], ROWS)
         load_w2(0)
-        load_gate(0)
+        load_gate()
         for m in (W1, W3):
             load_words(1, m, (0, 1), (1,))
         load_w2(1)
         load_rows(w2sc[1], w2_scales[1], ROWS)
-        load_gate(1)
         load_residual()
 
         planes0 = keep.tile([P, 2, SLOTS], U32, name="planes0", align_bytes=MX_ALIGN)

@@ -24,11 +24,12 @@ PASSES = K // KP
 G = H // KP
 NT = N // P
 W1, W3 = 0, 1
+LAST = SLOTS - P
 
 VECTOR_TOKENS_FIRST = 2 * T // 3
-VECTOR_TOKENS_SECOND = T // 2
-VECTOR_TOKENS_PASS_1 = 11 * T // 24
-SPARE_PRODUCTS = 5
+VECTOR_TOKENS_SECOND = 2 * T // 3
+VECTOR_TOKENS_PASS_1 = T // 2
+SPARE_PRODUCTS = 4
 CUTS = ((0, P, 3 * P, T), (0, 3 * P, 5 * P, T))
 DMA_ALIGN = 256
 MX_ALIGN = 64
@@ -114,13 +115,15 @@ def tile_moe_res_glu_silu_kernel(
 
         tables, quads, xq, xs = {}, {}, {}, {}
 
-        def round_pairs(s, u, vector_tokens):
+        def round_pairs(s, u, vector_tokens, parts=1):
             pairs = in_line([P, T, 2], BF16, "pairs")
             tables[s, u] = pairs[:].rearrange("p w d -> p (w d)").bitcast(U32)
             rows = raw[s, u][:].rearrange("p d w -> p w d")
             cut = T - vector_tokens
             nc.scalar.copy(pairs[:, 0:cut, :], rows[:, 0:cut, :])
-            nc.vector.tensor_copy(pairs[:, cut:T, :], rows[:, cut:T, :])
+            for first in range(cut, T, vector_tokens // parts):
+                last = first + vector_tokens // parts
+                nc.vector.tensor_copy(pairs[:, first:last, :], rows[:, first:last, :])
 
         def gather(planes, s, u, first, last):
             nc.vector.tensor_copy(planes[:, u, :], tables[s, u].indirect(listed(first, last)))
@@ -149,7 +152,8 @@ def tile_moe_res_glu_silu_kernel(
         def warm_up(gathered):
             codes = in_line([P, C], U32, "spare_codes")
             plane = keep.tile([P, C], U8, name="spare_plane", align_bytes=MX_ALIGN)
-            nc.vector.quantize_mx(out=codes[:].bitcast(FP8X4), scales=plane[:], in_=gathered.bitcast(BF16))
+            for half in (slice(0, P), slice(P, C)):
+                nc.vector.quantize_mx(out=codes[:, half].bitcast(FP8X4), scales=plane[:, half], in_=gathered.bitcast(BF16))
             spare = bank([P, KP], "spare")
             for _ in range(SPARE_PRODUCTS):
                 nc.tensor.matmul_mx(
@@ -250,8 +254,8 @@ def tile_moe_res_glu_silu_kernel(
         load_x(0, 0)
         nc.sync.dma_start(offsets[:], offs)
         load_x(0, 1)
-        load_rows(w2sc[0], w2_scales[0], ROWS)
         load_x(1, 0)
+        load_rows(w2sc[0], w2_scales[0], ROWS)
         load_x(1, 1)
         load_rows(wsc[0, W1], w1_scales[0], ROWS)
         for g in range(G):
@@ -271,15 +275,22 @@ def tile_moe_res_glu_silu_kernel(
         load_rows(w2sc[1], w2_scales[1], ROWS)
         load_residual()
 
-        planes0 = keep.tile([P, 2, SLOTS], U32, name="planes0", align_bytes=MX_ALIGN)
-        round_pairs(0, 0, VECTOR_TOKENS_FIRST)
-        gather(planes0, 0, 0, 0, SLOTS)
+        planes0 = keep.tile([P, 2, LAST], U32, name="planes0", align_bytes=MX_ALIGN)
+        round_pairs(0, 0, VECTOR_TOKENS_FIRST, parts=2)
+        warm_up(tables[0, 0][:, C : 2 * C])
+        gather(planes0, 0, 0, 0, LAST)
         round_pairs(0, 1, VECTOR_TOKENS_SECOND)
-        warm_up(planes0[:, 0, :])
-        gather(planes0, 0, 1, 0, SLOTS)
+        planes3 = in_line([P, 2, P], U32, "planes3")
+        gather(planes3, 0, 0, LAST, SLOTS)
+        gather(planes0, 0, 1, 0, LAST)
+        gather(planes3, 0, 1, LAST, SLOTS)
         round_pairs(1, 0, VECTOR_TOKENS_PASS_1)
         weave(0, 0, planes0[:, :, 0:C], nc.vector.tensor_copy)
-        weave(0, C, planes0[:, :, C:SLOTS], nc.scalar.copy)
+        quads[0, C] = in_line([P, C, 2], U32, "quads")
+        for first, planes in ((0, planes0[:, :, C:LAST]), (P, planes3[:])):
+            nc.scalar.copy(
+                quads[0, C][:, first : first + P, :].bitcast(F32), planes.bitcast(F32).rearrange("p u r -> p r u")
+            )
         gather_at_a_step(1, 0, 0)
         quantise(0, 0, C)
         round_pairs(1, 1, VECTOR_TOKENS_PASS_1)

@@ -29,7 +29,7 @@ LAST = SLOTS - P
 VECTOR_TOKENS_FIRST = 2 * T // 3
 VECTOR_TOKENS_SECOND = 2 * T // 3
 VECTOR_TOKENS_PASS_1 = T // 2
-SPARE_PRODUCTS = 4
+SPARE_PRODUCTS = 6
 CUTS = ((0, P, 3 * P, T), (0, 3 * P, 5 * P, T))
 DMA_ALIGN = 256
 MX_ALIGN = 64
@@ -254,8 +254,8 @@ def tile_moe_res_glu_silu_kernel(
         load_x(0, 0)
         nc.sync.dma_start(offsets[:], offs)
         load_x(0, 1)
-        load_x(1, 0)
         load_rows(w2sc[0], w2_scales[0], ROWS)
+        load_x(1, 0)
         load_x(1, 1)
         load_rows(wsc[0, W1], w1_scales[0], ROWS)
         for g in range(G):

@@ -57,7 +57,7 @@ def tile_moe_res_glu_silu_kernel(
         def listed(first, last):
             return offsets[:, first // 16 : last // 16]
 
-        words, scales = (w1_words, w3_words), (w1_scales, w3_scales)
+        words = (w1_words, w3_words)
         wsc, w2sc, back = {}, {}, {}
         for e in range(E):
             w2sc[e] = keep.tile([P, PASSES, N], U8, name=f"w2sc{e}", align_bytes=DMA_ALIGN)
@@ -264,10 +264,11 @@ def tile_moe_res_glu_silu_kernel(
         load_words(0, W3, (0, 1), (0,))
         load_rows(wsc[0, W3], w3_scales[0], ROWS)
         load_words(0, W3, (0, 1), (1,))
-        for m in (W1, W3):
-            load_words(1, m, (0, 1), (0,))
-            load_rows(wsc[1, m], scales[m][1], ROWS)
+        load_words(1, W1, (0, 1), (0,))
+        load_rows(wsc[1, W1], w1_scales[1], ROWS)
         load_w2(0)
+        load_words(1, W3, (0, 1), (0,))
+        load_rows(wsc[1, W3], w3_scales[1], ROWS)
         load_gate()
         for m in (W1, W3):
             load_words(1, m, (0, 1), (1,))

@@ -29,6 +29,7 @@ LAST = SLOTS - P
 VECTOR_TOKENS_FIRST = 2 * T // 3
 VECTOR_TOKENS_SECOND = 2 * T // 3
 VECTOR_TOKENS_PASS_1 = T // 2
+VECTOR_TOKENS_LAST = 448
 SPARE_PRODUCTS = 6
 CUTS = ((0, P, 3 * P, T), (0, 3 * P, 5 * P, T))
 DMA_ALIGN = 256
@@ -113,7 +114,7 @@ def tile_moe_res_glu_silu_kernel(
             for n in range(NT):
                 residual[n] = tiles[:, n, :]
 
-        tables, quads, xq, xs = {}, {}, {}, {}
+        tables, first_pairs, quads, xq, xs = {}, {}, {}, {}, {}
 
         def round_pairs(s, u, vector_tokens, parts=1):
             pairs = in_line([P, T, 2], BF16, "pairs")
@@ -128,10 +129,16 @@ def tile_moe_res_glu_silu_kernel(
         def gather(planes, s, u, first, last):
             nc.vector.tensor_copy(planes[:, u, :], tables[s, u].indirect(listed(first, last)))
 
-        def gather_at_a_step(s, u, j):
-            if u == 0:
-                quads[s, j * P] = in_line([P, P, 2], U32, "quads")
-            nc.vector.tensor_copy(quads[s, j * P][:, :, u], tables[s, u].indirect(listed(j * P, (j + 1) * P)))
+        def gather_first_pairs(s, j):
+            first_pairs[j] = in_line([P, P], U32, "first_pairs")
+            nc.vector.tensor_copy(first_pairs[j][:], tables[s, 0].indirect(listed(j * P, (j + 1) * P)))
+
+        def place_first_pairs(s, j):
+            quads[s, j * P] = in_line([P, P, 2], U32, "quads")
+            nc.scalar.copy(quads[s, j * P][:, :, 0], first_pairs[j][:])
+
+        def gather_second_pairs(s, j):
+            nc.vector.tensor_copy(quads[s, j * P][:, :, 1], tables[s, 1].indirect(listed(j * P, (j + 1) * P)))
 
         def weave(s, first, planes, copy):
             quads[s, first] = in_line([P, C, 2], U32, "quads")
@@ -292,12 +299,14 @@ def tile_moe_res_glu_silu_kernel(
             nc.scalar.copy(
                 quads[0, C][:, first : first + P, :].bitcast(F32), planes.bitcast(F32).rearrange("p u r -> p r u")
             )
-        gather_at_a_step(1, 0, 0)
+        gather_first_pairs(1, 0)
         quantise(0, 0, C)
-        round_pairs(1, 1, VECTOR_TOKENS_PASS_1)
-        gather_at_a_step(1, 0, 1)
+        round_pairs(1, 1, VECTOR_TOKENS_LAST)
+        gather_first_pairs(1, 1)
         for j in range(2):
-            gather_at_a_step(1, 1, j)
+            place_first_pairs(1, j)
+        for j in range(2):
+            gather_second_pairs(1, j)
         for j in range(2):
             quantise(1, j * P, (j + 1) * P)
         planes1 = in_line([P, 2, C], U32, "planes1")

@@ -58,6 +58,11 @@ def tile_moe_res_glu_silu_kernel(
         def listed(first, last):
             return offsets[:, first // 16 : last // 16]
 
+        zeros = ring.tile([P, 2], F32, name="zeros", bufs=1)
+        nc.vector.memset(zeros[:], 0.0)
+        preload = ring.tile([P, 2], F32, name="preload", bufs=1)
+        nc.scalar.activation(preload[:], zeros[:], SILU)
+
         words = (w1_words, w3_words)
         wsc, w2sc, back = {}, {}, {}
         for e in range(E):

@@ -278,9 +278,9 @@ def tile_moe_res_glu_silu_kernel(
         load_words(0, W3, (0, 1), (1,))
         load_words(1, W1, (0, 1), (0,))
         load_rows(wsc[1, W1], w1_scales[1], ROWS)
-        load_w2(0)
         load_words(1, W3, (0, 1), (0,))
         load_rows(wsc[1, W3], w3_scales[1], ROWS)
+        load_w2(0)
         load_gate()
         for m in (W1, W3):
             load_words(1, m, (0, 1), (1,))

@@ -17,6 +17,7 @@ FP8X4 = mybir.dt.float8_e4m3fn_x4
 FP4X4 = mybir.dt.float4_e2m1fn_x4
 MULT, ADD = mybir.AluOpType.mult, mybir.AluOpType.add
 SILU = mybir.ActivationFunctionType.Silu
+COPY = mybir.ActivationFunctionType.Copy
 
 P = 128
 KP = 512
@@ -256,6 +257,24 @@ def tile_moe_res_glu_silu_kernel(
         def put_back(j, n):
             nc.vector.tensor_tensor(back[n][:].indirect(listed(j * P, (j + 1) * P)), y_sb[j, n][:], gates[j], MULT)
 
+        def weigh_y(j, n):
+            y_sb[j, n] = in_line([P, P], F32, "y_sb")
+            nc.vector.tensor_tensor(y_sb[j, n][:], y[j, n][:], gates[j], MULT)
+
+        def put_back_weighed(j, n):
+            nc.scalar.activation(back[n][:].indirect(listed(j * P, (j + 1) * P)), y_sb[j, n][:], COPY)
+
+        def put_back_weighed_vector(j, n):
+            nc.vector.tensor_copy(back[n][:].indirect(listed(j * P, (j + 1) * P)), y_sb[j, n][:])
+
+        def y_out(j):
+            copy_y(j, 0)
+            weigh_y(j, 1)
+
+        def scatters(j):
+            put_back(j, 0)
+            put_back_weighed(j, 1)
+
         def finish(n):
             done = keep.tile([P, T], F32, name=f"done{n}", align_bytes=DMA_ALIGN)
             for first, last in zip(CUTS[n], CUTS[n][1:]):
@@ -397,14 +416,13 @@ def tile_moe_res_glu_silu_kernel(
         for n in range(NT):
             second_layer(2, n)
         quantise_h(3, 1)
-        for n in range(NT):
-            copy_y(2, n)
+        y_out(2)
         for n in range(NT):
             second_layer(3, n)
+        scatters(2)
         for n in range(NT):
-            copy_y(3, n)
-        for j in (2, 3):
-            for n in range(NT):
-                put_back(j, n)
+            weigh_y(3, n)
+        put_back_weighed_vector(3, 0)
+        put_back_weighed(3, 1)
         for n in range(NT):
             finish(n)

@@ -25,17 +25,12 @@ PASSES = K // KP
 G = H // KP
 NT = N // P
 W1, W3 = 0, 1
-LAST = SLOTS - P
 
-VECTOR_TOKENS_FIRST = 2 * T // 3
-VECTOR_TOKENS_SECOND = 2 * T // 3
-VECTOR_TOKENS_PASS_1 = T // 2
-VECTOR_TOKENS_LAST = 448
-SPARE_PRODUCTS = 6
+SPARE_PRODUCTS = 7
 CUTS = ((0, P, 3 * P, T), (0, 3 * P, 5 * P, T))
 DMA_ALIGN = 256
 MX_ALIGN = 64
-LINE_SLOTS = 50
+LINE_SLOTS = 38
 ROWS = range(4)
 
 
@@ -120,61 +115,44 @@ def tile_moe_res_glu_silu_kernel(
             for n in range(NT):
                 residual[n] = tiles[:, n, :]
 
-        tables, first_pairs, quads, xq, xs = {}, {}, {}, {}, {}
+        rows, quads, codes, planes, xq, xs = {}, {}, {}, {}, {}, {}
 
-        def round_pairs(s, u, vector_tokens, parts=1):
-            pairs = in_line([P, T, 2], BF16, "pairs")
-            tables[s, u] = pairs[:].rearrange("p w d -> p (w d)").bitcast(U32)
-            rows = raw[s, u][:].rearrange("p d w -> p w d")
-            cut = T - vector_tokens
-            nc.scalar.copy(pairs[:, 0:cut, :], rows[:, 0:cut, :])
-            for first in range(cut, T, vector_tokens // parts):
-                last = first + vector_tokens // parts
-                nc.vector.tensor_copy(pairs[:, first:last, :], rows[:, first:last, :])
+        def window(s, d, first, last):
+            if (s, first) not in rows:
+                rows[s, first] = in_line([P, 4, last - first], F32, "rows")
+            return rows[s, first][:, d, :], raw[s, d // 2][:, d % 2, :].indirect(listed(first, last))
 
-        def gather(planes, s, u, first, last):
-            nc.vector.tensor_copy(planes[:, u, :], tables[s, u].indirect(listed(first, last)))
+        def gather_vector(s, d, first, last):
+            nc.vector.tensor_copy(*window(s, d, first, last))
 
-        def gather_first_pairs(s, j):
-            first_pairs[j] = in_line([P, P], U32, "first_pairs")
-            nc.vector.tensor_copy(first_pairs[j][:], tables[s, 0].indirect(listed(j * P, (j + 1) * P)))
+        def gather_scalar(s, d, first, last):
+            nc.scalar.activation(*window(s, d, first, last), COPY)
 
-        def place_first_pairs(s, j):
-            quads[s, j * P] = in_line([P, P, 2], U32, "quads")
-            nc.scalar.copy(quads[s, j * P][:, :, 0], first_pairs[j][:])
-
-        def gather_second_pairs(s, j):
-            nc.vector.tensor_copy(quads[s, j * P][:, :, 1], tables[s, 1].indirect(listed(j * P, (j + 1) * P)))
-
-        def weave(s, first, planes, copy):
-            quads[s, first] = in_line([P, C, 2], U32, "quads")
-            copy(quads[s, first][:].bitcast(F32), planes.bitcast(F32).rearrange("p u r -> p r u"))
+        def weave(s, first, last):
+            quads[s, first] = in_line([P, last - first, 4], BF16, "quads")
+            nc.vector.tensor_copy(quads[s, first][:], rows[s, first][:].rearrange("p d r -> p r d"))
 
         def quantise(s, first, last):
-            codes = in_line([P, last - first], U32, "codes")
-            plane = keep.tile([P, last - first], U8, name=f"xs{s}{first}", align_bytes=MX_ALIGN)
+            codes[s, first] = in_line([P, last - first], U32, "codes")
+            planes[s, first] = keep.tile([P, last - first], U8, name=f"xs{s}{first}", align_bytes=MX_ALIGN)
             nc.vector.quantize_mx(
-                out=codes[:].bitcast(FP8X4),
-                scales=plane[:],
-                in_=quads[s, first][:].rearrange("p r u -> p (r u)").bitcast(BF16),
+                out=codes[s, first][:].bitcast(FP8X4),
+                scales=planes[s, first][:],
+                in_=quads[s, first][:].rearrange("p r d -> p (r d)"),
             )
             for j in range(first // P, last // P):
-                xq[s, j] = codes[:, j * P - first : (j + 1) * P - first]
-                xs[s, j] = plane[:, j * P - first : (j + 1) * P - first]
+                xq[s, j] = codes[s, first][:, j * P - first : (j + 1) * P - first]
+                xs[s, j] = planes[s, first][:, j * P - first : (j + 1) * P - first]
 
-        def warm_up(gathered):
-            codes = in_line([P, C], U32, "spare_codes")
-            plane = keep.tile([P, C], U8, name="spare_plane", align_bytes=MX_ALIGN)
-            for half in (slice(0, P), slice(P, C)):
-                nc.vector.quantize_mx(out=codes[:, half].bitcast(FP8X4), scales=plane[:, half], in_=gathered.bitcast(BF16))
-            spare = bank([P, KP], "spare")
+        def warm_up():
+            spare = bank([P, C], "spare")
             for _ in range(SPARE_PRODUCTS):
                 nc.tensor.matmul_mx(
                     out=spare[:],
-                    lhsT=codes[:, 0:P].bitcast(FP8X4),
-                    lhsT_scale=plane[:, 0:P],
-                    rhs=codes[:].bitcast(U8).bitcast(FP4X4),
-                    rhs_scale=w2sc[0][:].rearrange("p s n -> p (s n)"),
+                    lhsT=xq[0, 0].bitcast(FP8X4),
+                    lhsT_scale=xs[0, 0],
+                    rhs=xq[0, 0].bitcast(U8).bitcast(FP4X4),
+                    rhs_scale=w2sc[0][:, 0, :],
                     start=True,
                     stop=True,
                 )
@@ -257,8 +235,11 @@ def tile_moe_res_glu_silu_kernel(
         def put_back(j, n):
             nc.vector.tensor_tensor(back[n][:].indirect(listed(j * P, (j + 1) * P)), y_sb[j, n][:], gates[j], MULT)
 
-        def weigh_y(j, n):
-            y_sb[j, n] = in_line([P, P], F32, "y_sb")
+        def weigh_y(j, n, shared=False):
+            if shared:
+                y_sb[j, n] = ring.tile([P, P], F32, name="y_shared", bufs=1, align_bytes=MX_ALIGN)
+            else:
+                y_sb[j, n] = in_line([P, P], F32, "y_sb")
             nc.vector.tensor_tensor(y_sb[j, n][:], y[j, n][:], gates[j], MULT)
 
         def put_back_weighed(j, n):
@@ -307,37 +288,26 @@ def tile_moe_res_glu_silu_kernel(
         load_rows(w2sc[1], w2_scales[1], ROWS)
         load_residual()
 
-        planes0 = keep.tile([P, 2, LAST], U32, name="planes0", align_bytes=MX_ALIGN)
-        round_pairs(0, 0, VECTOR_TOKENS_FIRST, parts=2)
-        warm_up(tables[0, 0][:, C : 2 * C])
-        gather(planes0, 0, 0, 0, LAST)
-        round_pairs(0, 1, VECTOR_TOKENS_SECOND)
-        planes3 = in_line([P, 2, P], U32, "planes3")
-        gather(planes3, 0, 0, LAST, SLOTS)
-        gather(planes0, 0, 1, 0, LAST)
-        gather(planes3, 0, 1, LAST, SLOTS)
-        round_pairs(1, 0, VECTOR_TOKENS_PASS_1)
-        weave(0, 0, planes0[:, :, 0:C], nc.vector.tensor_copy)
-        quads[0, C] = in_line([P, C, 2], U32, "quads")
-        for first, planes in ((0, planes0[:, :, C:LAST]), (P, planes3[:])):
-            nc.scalar.copy(
-                quads[0, C][:, first : first + P, :].bitcast(F32), planes.bitcast(F32).rearrange("p u r -> p r u")
-            )
-        gather_first_pairs(1, 0)
-        quantise(0, 0, C)
-        round_pairs(1, 1, VECTOR_TOKENS_LAST)
-        gather_first_pairs(1, 1)
-        for j in range(2):
-            place_first_pairs(1, j)
-        for j in range(2):
-            gather_second_pairs(1, j)
-        for j in range(2):
-            quantise(1, j * P, (j + 1) * P)
-        planes1 = in_line([P, 2, C], U32, "planes1")
-        for u in range(2):
-            gather(planes1, 1, u, C, SLOTS)
-        quantise(0, C, SLOTS)
-        weave(1, C, planes1[:], nc.vector.tensor_copy)
+        units = ((0, P), (P, C))
+        for s in range(PASSES):
+            for first, last in units + ((C, SLOTS),):
+                gather_vector(s, 1, first, last)
+                gather_scalar(s, 0, first, last)
+            for first, last in units:
+                gather_vector(s, 3, first, last)
+                gather_scalar(s, 2, first, last)
+            for d in (2, 3):
+                gather_scalar(s, d, C, SLOTS)
+            for first, last in units:
+                weave(s, first, last)
+            for first, last in units:
+                quantise(s, first, last)
+            if s == 0:
+                warm_up()
+        for s in range(PASSES):
+            weave(s, C, SLOTS)
+        for s in range(PASSES):
+            quantise(s, C, SLOTS)
 
         for g in range(G):
             for j in range(2):
@@ -352,7 +322,6 @@ def tile_moe_res_glu_silu_kernel(
             both_passes(0, g, W3)
         for g in range(G):
             hidden(0, g)
-        quantise(1, C, SLOTS)
         for g in range(G):
             both_passes(1, g, W3)
         hidden(1, 0)

from contextlib import ExitStack

import concourse.mybir as mybir
from concourse.masks import make_identity

K, T, E, C, H, N = 1024, 768, 2, 256, 1024, 256
SLOTS = E * C
FLOPS = 2 * SLOTS * (2 * K * H + H * N)

F32 = mybir.dt.float32
BF16 = mybir.dt.bfloat16
U32 = mybir.dt.uint32
I32 = mybir.dt.int32
U16 = mybir.dt.uint16
U8 = mybir.dt.uint8
FP8X4 = mybir.dt.float8_e4m3fn_x4
FP4X4 = mybir.dt.float4_e2m1fn_x4
MULT, ADD = mybir.AluOpType.mult, mybir.AluOpType.add
SILU = mybir.ActivationFunctionType.Silu
COPY = mybir.ActivationFunctionType.Copy

P = 128
KP = 512
PASSES = K // KP
G = H // KP
NT = N // P
W1, W3 = 0, 1

SPARE_PRODUCTS = 7
CUTS = ((0, P, 3 * P, T), (0, 3 * P, 5 * P, T))
DMA_ALIGN = 256
MX_ALIGN = 64
LINE_SLOTS = 38
ROWS = range(4)


def tile_moe_res_glu_silu_kernel(
    tc, xT, xr, w1_words, w1_scales, w3_words, w3_scales, w2_words, w2_scales, gate, offs, out
):
    nc = tc.nc
    with ExitStack() as ctx:
        keep = ctx.enter_context(tc.tile_pool(name="keep", bufs=1))
        ring = ctx.enter_context(tc.tile_pool(name="ring", bufs=2))
        psum = ctx.enter_context(tc.psum_pool(name="psum", bufs=8))

        def in_line(shape, dtype, name):
            return ring.tile(shape, dtype, name=name, tag="line", bufs=LINE_SLOTS, align_bytes=MX_ALIGN)

        def bank(shape, name):
            return psum.tile(shape, F32, name=name, tag="bank")

        offsets = keep.tile([P, SLOTS // 16], U16, name="offsets")

        def listed(first, last):
            return offsets[:, first // 16 : last // 16]

        zeros = ring.tile([P, 2], F32, name="zeros", bufs=1)
        nc.vector.memset(zeros[:], 0.0)
        preload = ring.tile([P, 2], F32, name="preload", bufs=1)
        nc.scalar.activation(preload[:], zeros[:], SILU)

        words = (w1_words, w3_words)
        wsc, w2sc, back = {}, {}, {}
        for e in range(E):
            w2sc[e] = keep.tile([P, PASSES, N], U8, name=f"w2sc{e}", align_bytes=DMA_ALIGN)
            nc.gpsimd.memset(w2sc[e][:].rearrange("p s n -> p (s n)").bitcast(I32), 0)
        for e in range(E):
            for m in (W1, W3):
                wsc[e, m] = keep.tile([P, PASSES, H], U8, name=f"wsc{e}{m}", align_bytes=DMA_ALIGN)
                engine = nc.gpsimd if m == W1 else nc.vector
                engine.memset(wsc[e, m][:].rearrange("p s i -> p (s i)").bitcast(I32), 0)
        for n in range(NT):
            back[n] = keep.tile([P, T], F32, name=f"back{n}", align_bytes=MX_ALIGN)
            nc.vector.memset(back[n][:], 0.0)
        ident = keep.tile([P, P], F32, name="ident")
        make_identity(nc, ident[:])

        raw, wt, w2t, gates, residual = {}, {}, {}, {}, {}
        pieces = xT.rearrange("(s p u d) w -> s u p d w", s=PASSES, p=P, u=2)

        def load_x(s, u):
            raw[s, u] = keep.tile([P, 2, T], F32, name=f"raw{s}{u}", align_bytes=DMA_ALIGN)
            nc.sync.dma_start(raw[s, u][:], pieces[s, u])

        def load_rows(plane, source, rows):
            by_row = source.rearrange("s (q r) i -> r q s i", r=4)
            for r in rows:
                nc.sync.dma_start(plane[r:P:32].bitcast(I32), by_row[r].bitcast(I32))

        def load_words(e, m, passes, halves):
            width = 2 * KP * len(halves)
            piece = keep.tile([P, len(passes), width], U8, name=f"w{e}{m}{passes[0]}{halves[0]}", align_bytes=DMA_ALIGN)
            source = words[m][e].rearrange("s p b -> p s b")
            first = 2 * KP * halves[0]
            nc.sync.dma_start(
                piece[:].bitcast(I32), source[:, passes[0] : passes[-1] + 1, first : first + width].bitcast(I32)
            )
            for s in passes:
                for g in halves:
                    wt[e, m, s, g] = piece[:, s - passes[0], 2 * KP * g - first : 2 * KP * (g + 1) - first]

        def load_w2(e):
            w2t[e] = keep.tile([P, PASSES, 2 * N], U8, name=f"w2t{e}", align_bytes=DMA_ALIGN)
            nc.sync.dma_start(w2t[e][:].bitcast(I32), w2_words[e].rearrange("s p b -> p s b").bitcast(I32))

        def load_gate():
            piece = keep.tile([P, SLOTS], F32, name="gate", align_bytes=DMA_ALIGN)
            nc.sync.dma_start(piece[:], gate[0:P, :])
            for j in range(SLOTS // P):
                gates[j] = piece[:, j * P : (j + 1) * P]

        def load_residual():
            tiles = keep.tile([P, NT, T], F32, name="residual", align_bytes=DMA_ALIGN)
            nc.sync.dma_start(tiles[:], xr.rearrange("(n p) t -> p n t", p=P))
            for n in range(NT):
                residual[n] = tiles[:, n, :]

        rows, quads, codes, planes, xq, xs = {}, {}, {}, {}, {}, {}

        def window(s, d, first, last):
            if (s, first) not in rows:
                rows[s, first] = in_line([P, 4, last - first], F32, "rows")
            return rows[s, first][:, d, :], raw[s, d // 2][:, d % 2, :].indirect(listed(first, last))

        def gather_vector(s, d, first, last):
            nc.vector.tensor_copy(*window(s, d, first, last))

        def gather_scalar(s, d, first, last):
            nc.scalar.activation(*window(s, d, first, last), COPY)

        def weave(s, first, last):
            quads[s, first] = in_line([P, last - first, 4], BF16, "quads")
            nc.vector.tensor_copy(quads[s, first][:], rows[s, first][:].rearrange("p d r -> p r d"))

        def quantise(s, first, last):
            codes[s, first] = in_line([P, last - first], U32, "codes")
            planes[s, first] = keep.tile([P, last - first], U8, name=f"xs{s}{first}", align_bytes=MX_ALIGN)
            nc.vector.quantize_mx(
                out=codes[s, first][:].bitcast(FP8X4),
                scales=planes[s, first][:],
                in_=quads[s, first][:].rearrange("p r d -> p (r d)"),
            )
            for j in range(first // P, last // P):
                xq[s, j] = codes[s, first][:, j * P - first : (j + 1) * P - first]
                xs[s, j] = planes[s, first][:, j * P - first : (j + 1) * P - first]

        def warm_up():
            spare = bank([P, C], "spare")
            for _ in range(SPARE_PRODUCTS):
                nc.tensor.matmul_mx(
                    out=spare[:],
                    lhsT=xq[0, 0].bitcast(FP8X4),
                    lhsT_scale=xs[0, 0],
                    rhs=xq[0, 0].bitcast(U8).bitcast(FP4X4),
                    rhs_scale=w2sc[0][:, 0, :],
                    start=True,
                    stop=True,
                )

        acc, act, h = {}, {}, {}

        def product(j, g, m, s):
            e = j * P // C
            if s == 0:
                acc[j, g, m] = bank([P, KP], "acc")
            nc.tensor.matmul_mx(
                out=acc[j, g, m][:],
                lhsT=xq[s, j].bitcast(FP8X4),
                lhsT_scale=xs[s, j],
                rhs=wt[e, m, s, g].bitcast(FP4X4),
                rhs_scale=wsc[e, m][:, s, g * KP : (g + 1) * KP],
                start=(s == 0),
                stop=(s == PASSES - 1),
            )

        def both_passes(j, g, m):
            for s in range(PASSES):
                product(j, g, m, s)

        def by_pairs(j, g, m):
            return acc[j, g, m][:].rearrange("r (p u e) -> r u p e", u=2, e=2)

        def silu(j, g, parts=(slice(0, 2),)):
            for part in parts:
                act[j, g, part.start] = in_line([P, part.stop - part.start, P, 2], F32, "act")
                nc.scalar.activation(act[j, g, part.start][:], by_pairs(j, g, W1)[:, part], SILU)

        def hidden(j, g, parts=(slice(0, 2),)):
            h[j, g] = in_line([P, 2, P, 2], BF16, "h")
            for part in parts:
                nc.vector.tensor_tensor(h[j, g][:, part], act[j, g, part.start][:], by_pairs(j, g, W3)[:, part], MULT)

        turned, h_quads, hq, hs, y, y_sb = {}, {}, {}, {}, {}, {}

        def turn(j, g):
            turned[j, g] = bank([P, 2, P], "turned")
            pairs = h[j, g][:].rearrange("r u p e -> r (u p e)").bitcast(F32)
            for u in range(2):
                nc.tensor.transpose(turned[j, g][:, u, :], pairs[:, u * P : (u + 1) * P], ident[:])

        def leave_psum(j, g, copy=nc.scalar.copy):
            h_quads[j, g] = in_line([P, 4 * P], BF16, "h_quads")
            copy(
                h_quads[j, g][:].bitcast(F32).rearrange("p (r u) -> p r u", u=2),
                turned[j, g][:].rearrange("p u r -> p r u"),
            )

        def quantise_h(j, g):
            hq[j, g] = in_line([P, P], U32, "hq")
            hs[j, g] = keep.tile([P, P], U8, name=f"hs{j}{g}", align_bytes=MX_ALIGN)
            nc.vector.quantize_mx(out=hq[j, g][:].bitcast(FP8X4), scales=hs[j, g][:], in_=h_quads[j, g][:])

        def second_product(j, n, g):
            e = j * P // C
            if g == 0:
                y[j, n] = bank([P, P], "y")
            nc.tensor.matmul_mx(
                out=y[j, n][:],
                lhsT=w2t[e][:, g, 2 * P * n : 2 * P * (n + 1)].bitcast(FP4X4),
                lhsT_scale=w2sc[e][:, g, P * n : P * (n + 1)],
                rhs=hq[j, g][:].bitcast(FP8X4),
                rhs_scale=hs[j, g][:],
                start=(g == 0),
                stop=(g == G - 1),
            )

        def second_layer(j, n):
            for g in range(G):
                second_product(j, n, g)

        def copy_y(j, n):
            y_sb[j, n] = in_line([P, P], F32, "y_sb")
            nc.scalar.copy(y_sb[j, n][:], y[j, n][:])

        def put_back(j, n):
            nc.vector.tensor_tensor(back[n][:].indirect(listed(j * P, (j + 1) * P)), y_sb[j, n][:], gates[j], MULT)

        def weigh_y(j, n, shared=False):
            if shared:
                y_sb[j, n] = ring.tile([P, P], F32, name="y_shared", bufs=1, align_bytes=MX_ALIGN)
            else:
                y_sb[j, n] = in_line([P, P], F32, "y_sb")
            nc.vector.tensor_tensor(y_sb[j, n][:], y[j, n][:], gates[j], MULT)

        def put_back_weighed(j, n):
            nc.scalar.activation(back[n][:].indirect(listed(j * P, (j + 1) * P)), y_sb[j, n][:], COPY)

        def put_back_weighed_vector(j, n):
            nc.vector.tensor_copy(back[n][:].indirect(listed(j * P, (j + 1) * P)), y_sb[j, n][:])

        def y_out(j):
            copy_y(j, 0)
            weigh_y(j, 1)

        def scatters(j):
            put_back(j, 0)
            put_back_weighed(j, 1)

        def finish(n):
            done = keep.tile([P, T], F32, name=f"done{n}", align_bytes=DMA_ALIGN)
            for first, last in zip(CUTS[n], CUTS[n][1:]):
                cols = slice(first, last)
                nc.vector.tensor_tensor(done[:, cols], back[n][:, cols], residual[n][:, cols], ADD)
                nc.sync.dma_start(out[n * P : (n + 1) * P, cols], done[:, cols])

        load_x(0, 0)
        nc.sync.dma_start(offsets[:], offs)
        load_x(0, 1)
        load_rows(w2sc[0], w2_scales[0], ROWS)
        load_x(1, 0)
        load_x(1, 1)
        load_rows(wsc[0, W1], w1_scales[0], ROWS)
        for g in range(G):
            load_words(0, W1, (0,), (g,))
        load_words(0, W1, (1,), (0, 1))
        load_words(0, W3, (0, 1), (0,))
        load_rows(wsc[0, W3], w3_scales[0], ROWS)
        load_words(0, W3, (0, 1), (1,))
        load_words(1, W1, (0, 1), (0,))
        load_rows(wsc[1, W1], w1_scales[1], ROWS)
        load_words(1, W3, (0, 1), (0,))
        load_rows(wsc[1, W3], w3_scales[1], ROWS)
        load_w2(0)
        load_gate()
        for m in (W1, W3):
            load_words(1, m, (0, 1), (1,))
        load_w2(1)
        load_rows(w2sc[1], w2_scales[1], ROWS)
        load_residual()

        units = ((0, P), (P, C))
        for s in range(PASSES):
            for first, last in units + ((C, SLOTS),):
                gather_vector(s, 1, first, last)
                gather_scalar(s, 0, first, last)
            for first, last in units:
                gather_vector(s, 3, first, last)
                gather_scalar(s, 2, first, last)
            for d in (2, 3):
                gather_scalar(s, d, C, SLOTS)
            for first, last in units:
                weave(s, first, last)
            for first, last in units:
                quantise(s, first, last)
            if s == 0:
                warm_up()
        for s in range(PASSES):
            weave(s, C, SLOTS)
        for s in range(PASSES):
            quantise(s, C, SLOTS)

        for g in range(G):
            for j in range(2):
                product(j, g, W1, 0)
        for j in range(2):
            for g in range(G):
                product(j, g, W1, 1)
        for j in range(2):
            for g in range(G):
                silu(j, g)
        for g in range(G):
            both_passes(0, g, W3)
        for g in range(G):
            hidden(0, g)
        for g in range(G):
            both_passes(1, g, W3)
        hidden(1, 0)

        for g in range(G):
            turn(0, g)
        leave_psum(0, 0)
        leave_psum(0, 1, nc.vector.tensor_copy)
        for g in range(G):
            quantise_h(0, g)
        hidden(1, 1)
        in_two = (slice(0, 1), slice(1, 2))
        both_passes(2, 0, W1)
        silu(2, 0, in_two)
        both_passes(2, 0, W3)
        hidden(2, 0, in_two)
        for g in range(G):
            for n in range(NT):
                second_product(0, n, g)
        copy_y(0, 0)
        put_back(0, 0)
        both_passes(3, 0, W1)
        copy_y(0, 1)
        put_back(0, 1)
        silu(3, 0)

        ready = ((1, 0), (1, 1), (2, 0))
        for j, g in ready:
            turn(j, g)
        for g in range(G):
            leave_psum(1, g)
        for g in range(G):
            quantise_h(1, g)
        both_passes(2, 1, W1)
        leave_psum(2, 0)
        silu(2, 1)
        both_passes(3, 0, W3)
        quantise_h(2, 0)
        hidden(3, 0)
        both_passes(2, 1, W3)
        second_layer(1, 0)
        hidden(2, 1)
        copy_y(1, 0)
        put_back(1, 0)
        both_passes(3, 1, W1)
        silu(3, 1)
        both_passes(3, 1, W3)
        hidden(3, 1)

        turn(2, 1)
        turn(3, 0)
        second_layer(1, 1)
        leave_psum(2, 1)
        turn(3, 1)
        leave_psum(3, 0)
        quantise_h(2, 1)
        quantise_h(3, 0)
        copy_y(1, 1)
        put_back(1, 1)
        leave_psum(3, 1)
        for n in range(NT):
            second_layer(2, n)
        quantise_h(3, 1)
        y_out(2)
        for n in range(NT):
            second_layer(3, n)
        scatters(2)
        for n in range(NT):
            weigh_y(3, n)
        put_back_weighed_vector(3, 0)
        put_back_weighed(3, 1)
        for n in range(NT):
            finish(n)
